import numpy as np, ml_dtypes
CORES = [16,17,18,19,32,33,34,35]
N = 8
BF = ml_dtypes.bfloat16
def gentries(a):
    return np.ascontiguousarray(a.reshape(8, 16, -1).transpose(0, 2, 1)).reshape(8, -1)
def gtable(e):
    e = np.asarray(e); return np.ascontiguousarray(e.reshape(8, -1, 16).transpose(0, 2, 1)).reshape(128, -1).astype(np.int32)
W, V, I, RO = 2048, 2048, 128, 3
P = V // I
def parts(rng):
    return (rng.integers(0, W, (N, 8, 16, W)), rng.integers(0, 256, (N, 8, 16, V)), rng.integers(0, 256, (N, 8, 16, I)),
            rng.integers(0, W, (N, 8, I)), rng.integers(0, 256, (N, 8, 16)))
def pack(S, X, x, s, w):
    return {"stm": np.ascontiguousarray(S.reshape(N, 128, W)).astype(np.int32), "vx": X.reshape(N, 128, V).astype(np.float32).astype(BF),
            "x0": x.reshape(N, 128, I).astype(np.float32).astype(BF), "s0": np.stack([gtable(a) for a in s]), "wt": w.reshape(N, 128, 1).astype(np.int32)}
def two(rng, lo, hi, shape):
    return np.where(rng.random(shape) < 0.5, lo, hi)
def tame(rng, S, w, cl):
    col = np.arange(W); ev = col[((col >> 4) & 1) == 0]
    off = np.where(cl, 0, rng.integers(1, 16, cl.shape))
    S[:, ev] = 32 * np.argsort(rng.random((16, W // 32, 16)), axis=1).reshape(16, W // 2) + 16 + ((ev + off) & 15)
    w[:] = 32 * rng.integers(1, 8, 16)
    return ev
def lay(rng, S, w, cl, no):
    off = rng.integers(1, 15, cl.shape); off = np.where(cl, 0, off + (off >= 16 - no))
    S[:] = 16 * rng.integers(0, W // 16, cl.shape) + ((np.arange(W) + off) & 15)
    w[:] = 32 * rng.integers(1, 8, 16)
def wake(S, X, w, k, c):
    if (S[k, c] & (V - 1)) == (S[k ^ 1, c] & (V - 1)): S[k ^ 1, c] = S[k ^ 1, c] ^ 16
    a = S[k, c] & (V - 1); b = S[k ^ 1, c] & (V - 1)
    X[0, b] = X[0, a] ^ 1
    if int(np.add.reduce(w * np.abs(X[:, a] - X[:, b]))) & (W - 1) == 0: w[0] = w[0] ^ 32
def setup_inputs(rng):
    return pack(*parts(rng))
def setup_inputs_corners(rng):
    S, X, x, s, w = parts(rng); M = W // 2; role = rng.permutation(N)
    for q in range(N):
        kinds = rng.permutation(8); gx = int(rng.integers(0, 8))
        for g in range(8):
            kind = int(kinds[g])
            if role[q] == 0 or role[q] == 2: kind = 0 if g % 2 == 0 else 2
            if role[q] == 1: kind = 1
            if role[q] == 2 and g == gx: kind = 8
            if kind == 6:
                S[q, g] = np.arange(W)[None, :]; s[q, g, 0] = W - 1; s[q, g, I - 1] = 0; continue
            if kind == 7:
                s[q, g] = two(rng, 0, W - 1, I); continue
            cl = np.zeros((16, M), bool); p = rng.permutation(M)
            if kind == 1: cl[:] = True
            if kind == 2: cl[15] = True
            if kind == 3: cl[0] = True; cl[15] = True
            if kind == 4: cl[14:] = rng.random(M) < 0.5
            if kind == 5: cl = np.argsort(rng.random((16, M)), axis=0) < rng.integers(0, 17, M)
            if kind == 8:
                n = int(rng.integers(15, 18)); cl[3, p[:n]] = True; cl[9, p[:n]] = True
            ev = tame(rng, S[q, g], w[q, g], cl)
            s[q, g] = rng.permutation(ev[p[:I]])
    return pack(S, X, x, s, w)
def setup_inputs_late(rng):
    S, X, x, s, w = parts(rng); odd = int(rng.integers(0, 2)); col = np.arange(W)
    for q in range(N):
        if q % 2 == odd:
            al = int(rng.integers(1, 16)); n = 16 * int(rng.integers(I // 16, 5 * I // 16)) + al
            fk = rng.permutation(8 * (I - 1)).reshape(8, I - 1) < n
            for g in range(8):
                m = np.where((col & 1) == 1, rng.integers(0, 2, W), rng.integers(2, 5, W)); m[W - 1] = 0
                lay(rng, S[q, g], w[q, g], np.argsort(rng.random((16, W)), axis=0) < m, al)
                s[q, g] = 2 * rng.integers(0, W // 2, I) + 1; s[q, g, :I - 1] -= fk[g].astype(np.int64); s[q, g, I - 1] = W - 1
            continue
        kinds = rng.permutation(8)
        for g in range(8):
            kind = int(kinds[g]) // 2; Sg, Xg, wg = S[q, g], X[q, g], w[q, g]
            if kind == 3: continue
            no = int(rng.integers(1, 16)); e = 16 * (1 + rng.permutation(W // 16 - 1)[:4])
            if kind == 0:
                lay(rng, Sg, wg, np.zeros((16, W), bool), no)
                k = int(rng.integers(0, 16)); c = int(rng.integers(0, W)); at = np.arange(c & 15, W, 16)
                Sg[k, at] = c; s[q, g] = rng.choice(at, I); wake(Sg, Xg, wg, k, c); continue
            lay(rng, Sg, wg, rng.random((16, W)) < 0.0625, no)
            if kind == 1:
                Sg[Sg == 0] = 16
                Sg[0, e[0]] = 0; Sg[0, e[1]] = 5; Sg[1, e[1]] = 0
                s[q, g, 0] = e[0]; s[q, g, 1] = e[1]; wake(Sg, Xg, wg, 0, 0)
            if kind == 2:
                ka = int(rng.integers(0, 15)); kb = int(rng.integers(ka + 1, 16))
                Sg[:, e] = 16 * rng.integers(0, W // 16, (16, 4)) + rng.integers(1, 16, (16, 4))
                Sg[ka, e] = 16 * rng.integers(1, W // 16, 4); Sg[kb, e] = 0
                z = np.abs(Xg[:, Sg[kb, 0] & (V - 1)] - Xg[:, Sg[kb ^ 1, 0] & (V - 1)])
                s[q, g, 1::2] = rng.choice(e, I // 2); x[q, g, :, 1::2] = z[:, None]
    return pack(S, X, x, s, w)
def setup_inputs_ties(rng):
    S, X, x, s, w = parts(rng)
    pool = np.argsort(rng.random((N, 8, W)), axis=-1)[..., :32]; pool[..., 0] = W - 1; pool[..., 1] = 0
    S = np.take_along_axis(pool[:, :, None, :], rng.integers(0, 32, (N, 8, 16, W)), 3)
    s = np.take_along_axis(pool, rng.integers(0, 32, (N, 8, I)), 2)
    few = np.take_along_axis(X[..., :5], rng.integers(0, 5, (N, 8, 1, V)), 3)
    X[:, ::2] = few[:, ::2]; x[:, 1::2] = x[:, 1::2, :, :1]
    return pack(S, X, x, s, w)
def setup_inputs_ends(rng):
    S, X, x, s, w = parts(rng)
    S = np.where(rng.random(S.shape) < 0.7, two(rng, 0, W - 1, S.shape), S)
    S[..., 0] = two(rng, 0, W - 1, (N, 8, 16)); S[..., W - 1] = two(rng, 0, W - 1, (N, 8, 16))
    S[:, :, [0, 1, 14, 15], 0] = np.array([0, W - 1, 0, W - 1]); S[:, :, [0, 1, 14, 15], W - 1] = np.array([0, W - 1, W - 1, 0])
    S[:, :, 4:6, 0] = 0; S[:, :, 4:6, W - 1] = W - 1
    q = 16 * rng.integers(1, W // 16 - 1, (N, 8)); S[:, :, 2, 0] = q; S[:, :, 2, W - 1] = q + 15
    for a in range(N):
        for g in range(8):
            S[a, g, 2:4, q[a, g]] = W - 1; S[a, g, 2:4, q[a, g] + 15] = 0
    S[:, :, 1, W - 2] = W - 1; S[:, :, 15, W - 2] = W - 1
    X = two(rng, 0, 255, X.shape); X[..., 0] = 0; X[..., V - 1] = 255
    x = two(rng, 0, 255, x.shape); w = two(rng, 0, 255, w.shape)
    w[:, 0] = 255; w[:, 7] = 255; w[:, 1::5] = 0; w[:, 1::5, 15] = 255; w[:, 1::5, 14] = 2
    s = np.where(rng.random(s.shape) < 0.8, two(rng, 0, W - 1, s.shape), s); s[N - 1] = two(rng, 0, W - 1, (8, I))
    s[:, 7, I - 1] = W - 1; s[:, 0, 2] = W - 1; s[:, 7, 1] = 0
    s[:, 1::5, 3] = W - 2; s[:, 1::5, I - 1] = W - 2; s[:, 1::5, I - 2] = W - 1; s[:, 1::5, 4] = W - 1
    return pack(S, X, x, s, w)
def setup_inputs_spread(rng):
    S, X, x, s, w = parts(rng)
    p = rng.choice(np.array([1.0, 1.5, 2.0, 4.0]), (N, 8, 1, 1)); fl = rng.random((N, 8, 1, 1)) < 0.5
    S = np.minimum((W * rng.random(S.shape) ** p).astype(np.int64), W - 1); S = np.where(fl, W - 1 - S, S)
    s = np.minimum((W * rng.random(s.shape) ** p[..., 0]).astype(np.int64), W - 1)
    X = np.minimum((np.exp2(8 * rng.random((N, 8, 1, V))) * rng.random(X.shape)).astype(np.int64), 255)
    x = np.minimum((np.exp2(8 * rng.random((N, 8, 1, I))) * rng.random(x.shape)).astype(np.int64), 255)
    w = np.minimum(np.exp2(8 * rng.random(w.shape)).astype(np.int64), 255)
    return pack(S, X, x, s, w)
def check_inputs(d):
    bad = []
    for k, lo, hi in (("stm", 0, W - 1), ("vx", 0, 255), ("x0", 0, 255), ("s0", 0, W - 1), ("wt", 0, 255)):
        v = np.asarray(d[k]).astype(np.float64)
        if not (np.min(v) >= lo and np.max(v) <= hi): bad.append("range of " + k)
        elif np.any(v != np.floor(v)): bad.append("whole numbers in " + k)
    return bad
def reference(stm, vx, x0, s0, wt):
    S = stm.astype(np.int64).reshape(N, 8, 16, W); X = vx.astype(np.float32).astype(np.int64).reshape(N, 8, 16, V)
    x = x0.astype(np.float32).astype(np.int64).reshape(N, 8, 16, I); w = wt.astype(np.int64).reshape(N, 8, 16, 1, 1)
    s = np.stack([gentries(a) for a in s0]).astype(np.int64)
    A = np.zeros(N, np.int64); mate = np.arange(16) ^ 1
    for t in range(RO):
        c = np.take_along_axis(S, s[:, :, None, :], 3)
        a = np.take_along_axis(S, c, 3) & (V - 1); b = np.take_along_axis(S[:, :, mate], c, 3) & (V - 1)
        z = np.abs(np.take_along_axis(X, a.reshape(N, 8, 1, 16 * I), 3) - np.take_along_axis(X, b.reshape(N, 8, 1, 16 * I), 3)).reshape(N, 8, 16, 16, I)
        u = np.add.reduce(w * z, axis=2) & (W - 1)
        claim = ((((u * u) >> 5) + u + c + A[:, None, None, None]) & 15) == (s & 15)[:, :, None, :]
        n = np.add.accumulate(claim.astype(np.int64), axis=2)
        has = n[:, :, 15] >= 1; fork = n[:, :, 15] >= 2
        k1 = np.argmax(claim & (n == 1), axis=2); k2 = np.argmax(claim & (n == 2), axis=2)
        c1 = np.take_along_axis(c, k1[:, :, None, :], 2)[:, :, 0]; c2 = np.take_along_axis(c, k2[:, :, None, :], 2)[:, :, 0]
        u1 = np.take_along_axis(u, k1[:, :, None, :], 2)[:, :, 0]
        z1 = np.take_along_axis(z, k1[:, :, None, None, :], 3)[:, :, :, 0]; z2 = np.take_along_axis(z, k2[:, :, None, None, :], 3)[:, :, :, 0]
        h = 1 + t % (N - 1)
        came = np.roll(fork, h, axis=0); cc = np.roll(c2, h, axis=0); cx = np.roll(np.abs(x - z2), h, axis=0)
        s = np.where(has, c1, np.where(came, cc, (5 * s + u[:, :, 0]) & (W - 1)))
        x = np.where(has[:, :, None], (x + z1) >> 1, np.where(came[:, :, None], cx, x))
        for r in range(N):
            for g in range(8):
                i = np.flatnonzero(has[r, g])
                X[r, g][:, P * i + (u1[r, g, i] & (P - 1))] = z1[r, g][:, i]
                col, at = np.unique(c1[r, g, i], return_index=True)
                i = i[at]; k = k1[r, g, i]
                S[r, g, k, col] = (S[r, g, k, col] + u1[r, g, i]) & (W - 1)
        A = np.add.reduce(fork.astype(np.int64), axis=(1, 2)) & 15
    return {"yt": np.add.reduce(S.reshape(N, 128, W // 256, 256), axis=2).astype(np.float32), "yv": X.reshape(N, 128, V).astype(np.float32).astype(BF),
            "yx": x.reshape(N, 128, I).astype(np.float32).astype(BF), "ys": np.stack([gtable(e) for e in s]).astype(np.float32)}

@@ -1,0 +1,521 @@
+import math
+from concourse.mybir import AluOpType as OP, ActivationFunctionType as AF
+
+N, RO = 8, 3
+NENG = 8
+PIECES = ((0, 16), (16, 32), (32, 64), (64, 96), (96, 112), (112, 128))
+VB = (4,)
+GS = (1, 2)
+SQ = 3
+
+F32, F16, BF, I4, U2 = "float32", "float16", "bfloat16", "int32", "uint16"
+SCRATCH = {}
+
+
+def _sb(dtype, **bufs):
+    for name in bufs:
+        SCRATCH[name] = ("sbuf", [128, bufs[name]], dtype)
+
+
+_sb(I4, S=2176, si=8, wi=1)
+_sb(BF, ZX=4096, xb=128)
+_sb(U2, su=8)
+_sb(I4, cp=1, cq=4)
+_sb(F32, cI=144, cf=16, tq=128, rc=128, blk=128, mk=128, l256=16, rm=16, gm=8, ex=16, z16=16, THR=128, IL=8, XO=8, il0=8, pf=16)
+_sb(F16, I16=128, P16=128, I32=128, N16=128, L1=144, LK=144, DA=2048, DB=2048, BN=128, SEL=1024, on16=128, TQ=128, RC=128,
+    BO=128, BF1=128, BF2=128, RQ=8, GI=8, CT=16)
+_sb(BF, TB=2048, SL=128, FCB=128, ONB=128, IB=128, NIB=128, WT=144, VJ=16)
+_sb(U2, Cu=128, ABT=256, ou=16, c1u=8, sou=8, xou=8)
+_sb(F16, C16=128, G0=1024, G1=1024, cl=128, FS=256, F1X=384, F2=128, lt=128, c1h=8)
+_sb(BF, XB=2048, DD=2048, EQ=1024, EN=1024, z1=128, z2=128, sg=8)
+_sb(I4, ui=128, w2=128, sq=128, y=128, yy=128, uk=128, Sc=128, Sd=128, Sn=128, x1=8, x2=8, x3=8, n2=8, n3=8, se=8, xv=128,
+    xm=128, xn=128)
+_sb(F32, col=8, cola=8, so=8, n1=8, h1=8, h2=8, sb=8, fc=1, sf=8, yto=256)
+SEMAPHORES = ["qv", "qs", "qp", "qg", "dS0", "dX", "dx0", "dw", "ds0", "oV", "oT", "oX", "oS", "sent"]
+for _t in range(RO):
+    _sb(F32, **{"mN%d" % _t: 8, "rN%d" % _t: 8})
+    _sb(BF, **{"mX%d" % _t: 128, "rX%d" % _t: 128})
+    SEMAPHORES += ["aN%d" % _t, "aX%d" % _t]
+PSUM = ["b%d" % _b for _b in range(8)]
+for _b in PSUM:
+    SCRATCH[_b] = ("psum", [128, 512], F32)
+
+CYC, PECYC, GATH, SCAT, WAKE, LOCAL, FLIGHT = 0.0012, 0.0005, 2.0, 3.8, 0.06, 2.0, 3.0
+ORDER = (
+    "000105270403071t020m0l0k0o080n28061v0b0s242s0q2k0p220g1l0v1b131s0t152p1n191r171j0r2t251c0w181m1o0u1a160y1i5t14121p101u1k2123"
+    "0z1w11261x1f1h1d1g1e0x2v0e382w090h0f0i0j0a312x0c2z0d2y323e3h301q333f353b343i3g3k363c3n3j3l3q3d3o3m3t3r3p3u373s1y3v39293a2046"
+    "3w2a1z3x472h3y484j494k4a3z2b4b412g402f4c42454e444d432d4l4f4h2e4g4i2n4p4m2m2l2i2r2u544v534q4n4y2o4w522c4x554r4o514t2q4z505a5h"
+    "4u4s2j585b56575d605i595c5j5k5f5e5n615u5w5z625o5g5x5v635p645l685y655m695q6a666c5r6b676d5s6e6g6f6h6i9k6z6m6n6t6o6q6p6s75786r6y"
+    "6u6j766w726v797071777b6x737e7a7c747h7k7f7d7i7g6k7j7l6l7m7n7x7o7p7y7q7z8a7r7s807w7v818b827t837u8c858d84868988878p8t8e8g8f8m8r"
+    "8u8h8o8w8v8n8q8i8k8s91988l8x8j8y928z9r93909a94999b9e95969q9n9f9o9z979g9l9c9ma09d9s9p9h9ua19i9j9t9va29w9xa3a79ya4a8a9a5aqada6"
+    "aeakafahagajawazaiaaalaxanatamb0b8b2aob5aub1b3avayb6b4bbb9b7apbcbaabarasbdd9acbebobfbgbpbhbqc1bibjbrc2bsbmbnbtbkbublc3bwc4bv"
+    "c0bzbxcjcickbyc5dgc6cbcgcedhcdcfclccchdicxcqcoctcndkcmcrcyc7czcscpd0dld3cuc8cvdmd4dac9dndcd5djcwdfcadbddd1dsdoded2dpdtd6dqd7"
+    "drd8dwdudxdvdydze0e9e1eae5e2ebe6e3ece7e4e8")
+
+
+def make_plan(g, T):
+    eng = {"v": g.vector, "s": g.scalar, "p": g.tensor, "g": g, "y": g.sync}
+    qsem = {"v": "qv", "s": "qs", "p": "qp", "g": "qg"}
+    nodes = []
+    hist = {}
+
+    def rng(x):
+        return (x, 0, T[x].shape[1]) if isinstance(x, str) else x
+
+    def add(q, rd, wr, fns, dur, sem=None, inc=1, lat=0.0, after=None):
+        i = len(nodes)
+        rd = [rng(x) for x in rd]
+        wr = [rng(x) for x in wr]
+        pred = {}
+        for acc, isw in ((rd, False), (wr, True)):
+            for name, a, b in acc:
+                for (a0, b0, w0, j) in hist.get(name, []):
+                    over = a < b0 and a0 < b and (isw or w0)
+                    if name in PSUM:
+                        if nodes[j]["q"] != q or (over and q != "p"):
+                            pred[j] = True
+                        elif over:
+                            pred.setdefault(j, False)
+                    elif over:
+                        pred[j] = True
+        if after is not None:
+            pred[after] = False
+        nodes.append({"q": q, "fns": fns, "dur": dur, "sem": sem, "inc": inc, "lat": lat, "pred": pred, "i": i})
+        for name, a, b in wr:
+            keep = [h for h in hist.get(name, []) if not (a <= h[0] and h[1] <= b and h[3] in pred)]
+            hist[name] = keep + [(a, b, True, i)]
+        for name, a, b in rd:
+            hist[name] = hist.get(name, []) + [(a, b, False, i)]
+        return i
+
+    def order():
+        n = len(nodes)
+        succ = [[] for _ in nodes]
+        for x in nodes:
+            for j, w in x["pred"].items():
+                succ[j].append((x["i"], w))
+        prio = [0.0] * n
+        for i in range(n - 1, -1, -1):
+            x = nodes[i]
+            best = max([prio[j] + (WAKE if w else 0.0) for j, w in succ[i]] + [0.0])
+            prio[i] = best + x["dur"] + x["lat"]
+        left = [len(x["pred"]) for x in nodes]
+        ready = [0.0] * n
+        free = {}
+        avail = {}
+        for x in nodes:
+            if not left[x["i"]]:
+                avail.setdefault(x["q"], []).append(x["i"])
+        out = []
+        while any(avail.values()):
+            pick = None
+            for q in avail:
+                if not avail[q]:
+                    continue
+                fr = free.get(q, 0.0) if q != "n" else 0.0
+                t0 = min(max(fr, ready[i]) for i in avail[q])
+                c = [i for i in avail[q] if max(fr, ready[i]) <= t0 + 0.02]
+                i = max(c, key=lambda k: prio[k])
+                t1 = max(fr, ready[i])
+                if pick is None or t1 < pick[0]:
+                    pick = (t1, i, q)
+            t1, i, q = pick
+            avail[q].remove(i)
+            x = nodes[i]
+            end = t1 + x["dur"]
+            free[q] = end
+            out.append(i)
+            for j, w in succ[i]:
+                ready[j] = max(ready[j], end + x["lat"] + (WAKE if w else 0.0))
+                left[j] -= 1
+                if not left[j]:
+                    avail.setdefault(nodes[j]["q"], []).append(j)
+        return out
+
+    def emit():
+        count = {}
+        clock = dict((q, {}) for q in eng)
+        event = {}
+        where = {}
+
+        def wait(q, need):
+            for src in sorted(need):
+                if not any(event[(o, need[o])].get(src, 0) >= need[src] for o in need if o != src):
+                    eng[q].wait_ge(T.sem[qsem.get(src, src)], need[src])
+            for src in need:
+                for k, m in event[(src, need[src])].items():
+                    clock[q][k] = max(clock[q].get(k, 0), m)
+
+        seq = [36 * int(ORDER[i], 36) + int(ORDER[i + 1], 36) for i in range(0, len(ORDER), 2)] or order()
+        for i in seq:
+            x = nodes[i]
+            q = x["q"]
+            if q == "n":
+                where[i] = (x["sem"], x["inc"])
+                event[where[i]] = {x["sem"]: x["inc"]}
+                continue
+            need = {}
+            for j, w in x["pred"].items():
+                if w:
+                    src, n = where[j]
+                    if n > clock[q].get(src, 0):
+                        need[src] = max(need.get(src, 0), n)
+            wait(q, need)
+            if x["sem"] is None:
+                for fn in x["fns"]:
+                    fn(eng[q]).then_inc(T.sem[qsem[q]], 1)
+                    count[q] = count.get(q, 0) + 1
+                where[i] = (q, count[q])
+            else:
+                for fn in x["fns"]:
+                    ins = fn(eng[q])
+                    if x["sem"] != "sent":
+                        ins.then_inc(T.sem[x["sem"]], 16)
+                where[i] = (x["sem"], x["inc"])
+            ev = dict(clock[q])
+            ev[where[i][0]] = where[i][1]
+            event[where[i]] = ev
+        for x in nodes:
+            if x["sem"] is not None and x["sem"] != "sent" and x["q"] != "n" and x["inc"] > clock["g"].get(x["sem"], 0):
+                wait("g", {x["sem"]: x["inc"]})
+        g.wait_ge(T.sem.sent, sum(x["inc"] for x in nodes if x["sem"] == "sent"))
+        for q in ("v", "s", "p", "g"):
+            if count[q] > clock["g"].get(q, 0):
+                wait("g", {q: count[q]})
+        return nodes, seq
+    return add, emit
+
+
+def rank_program(g, core, T, topo):
+    rank = T.rank_of(core)
+    if rank is None:
+        return
+    add, emit = make_plan(g, T)
+
+    def cols(x):
+        if isinstance(x, str):
+            n = T[x].shape[1]
+            return T[x][:, 0:n], (x, 0, n)
+        name, a, b = x[:3]
+        if len(x) == 4:
+            return T[name][:, a:b:x[3]], (name, a, b)
+        return T[name][:, a:b], (name, a, b)
+
+    def width(x):
+        r = cols(x)[1]
+        return (r[2] - r[1]) // (x[3] if len(x) == 4 and not isinstance(x, str) else 1)
+
+    def buf(x):
+        return x if isinstance(x, str) else x[0]
+
+    def small(*xs):
+        return all(SCRATCH[buf(x)][2] in (F16, BF, U2) for x in xs)
+
+    def vec(ins, out, fn, cyc):
+        add("v", [cols(x)[1] for x in ins], [cols(out)[1]], [fn], CYC * max(64, cyc))
+
+    def ts(out, in0, s1, op0, s2=None, op1=None):
+        o, i = cols(out)[0], cols(in0)[0]
+        rd = [in0] + [x for x in (s1, s2) if isinstance(x, tuple)]
+        s1 = cols(s1)[0] if isinstance(s1, tuple) else s1
+        s2 = cols(s2)[0] if isinstance(s2, tuple) else s2
+        if op1 is None:
+            fn = lambda e: e.tensor_scalar(o, i, s1, None, op0)
+        else:
+            fn = lambda e: e.tensor_scalar(o, i, s1, s2, op0, op1)
+        vec(rd, out, fn, width(out) * (0.5 if small(out, in0) else 1))
+
+    def tt(out, in0, in1, op):
+        o, a, b = cols(out)[0], cols(in0)[0], cols(in1)[0]
+        ps = buf(in0) in PSUM or buf(in1) in PSUM
+        vec([in0, in1], out, lambda e: e.tensor_tensor(o, a, b, op), width(out) * (1 if ps else 2))
+
+    def cp(out, in0):
+        o, a = cols(out)[0], cols(in0)[0]
+        vec([in0], out, lambda e: e.tensor_copy(o, a), width(out) * (0.5 if small(out, in0) else 1))
+
+    def gat(out, win, off):
+        o, w, f = cols(out)[0], cols(win)[0], cols(off)[0]
+        vec([win, off], out, lambda e: e.tensor_copy(o, w.indirect(f)), 50 + GATH * width(out))
+
+    def gsub(out, win, off, in1):
+        o, w, f, b = cols(out)[0], cols(win)[0], cols(off)[0], cols(in1)[0]
+        vec([win, off, in1], out, lambda e: e.tensor_tensor(o, w.indirect(f), b, OP.subtract), 50 + GATH * width(out))
+
+    def sca(win, off, in0):
+        w, f, a = cols(win)[0], cols(off)[0], cols(in0)[0]
+        vec([off, in0], win, lambda e: e.tensor_copy(w.indirect(f), a), 50 + SCAT * width(in0))
+
+    def fill(out, v):
+        o = cols(out)[0]
+        vec([], out, lambda e: e.memset(o, v), width(out))
+
+    def act(out, in0, func, off=None, **kw):
+        o, a = cols(out)[0], cols(in0)[0]
+        rd, wr, kk = [cols(in0)[1]], [cols(out)[1]], {}
+        for k, v in kw.items():
+            if isinstance(v, tuple):
+                v, r = cols(v)
+                (wr if k == "accum_out" else rd).append(r)
+            kk[k] = v
+        if off is not None:
+            f, rf = cols(off)
+            a = a.indirect(f)
+            rd.append(rf)
+        add("s", rd, wr, [lambda e: e.activation(o, a, func, **kk)], CYC * (65 + width(out) * (GATH if off is not None else 1)))
+
+    def one(x):
+        o, a, b = cols(x[0])[0], cols(x[1])[0], cols(x[2])[0]
+        return lambda e: e.matmul(o, a, b, x[3], x[4])
+
+    def mms(xs):
+        rd = sorted(set(cols(x[1])[1] for x in xs) | set(cols(x[2])[1] for x in xs))
+        wr = sorted(set(cols(x[0])[1] for x in xs))
+        add("p", rd, wr, [one(x) for x in xs], sum(max(64, width(x[0])) * PECYC for x in xs))
+
+    def iota(out, pattern, base, cm, flag=True):
+        o = cols(out)[0]
+        if flag:
+            fn = lambda e: e.iota(o, pattern, base, cm, allow_small_or_imprecise_dtypes=True)
+        else:
+            fn = lambda e: e.iota(o, pattern, base, cm)
+        add("g", [], [cols(out)[1]], [fn], 0.13 + 2 * CYC * width(out))
+
+    def sel(out, op, v):
+        o, ro = cols(out)
+        add("g", [ro], [ro], [lambda e: e.affine_select(o, o, [[1, 128]], op, v, 0, -1)], 0.17 + 2 * CYC * width(out))
+
+    def dma(q, s, rd, wr, out, in_, us):
+        add(q, rd, wr, [lambda e: e.dma_start(out, in_)], 0.1, sem=s, inc=16, lat=us)
+
+    SW, SD, XW, ZW = ("S", 0, 2048), ("S", 0, 2176), ("ZX", 2048, 4096), ("ZX", 0, 4096)
+
+    dma("s", "ds0", [], ["si"], T.si[:], T.s0[:], LOCAL)
+    dma("y", "dS0", [], [SW], T.S[:, 0:2048], T.stm[:], 6.0)
+    dma("s", "dw", [], ["wi"], T.wi[:], T.wt[:], LOCAL)
+    dma("y", "dX", [], [XW], T.ZX[:, 2048:4096], T.vx[:], 9.0)
+    dma("s", "dx0", [], ["xb"], T.xb[:], T.x0[:], LOCAL)
+
+    iota("cp", [[1, 1]], 0, 1, False)
+    iota("pf", [[0, 16]], 0, 1)
+    iota("cI", [[1, 144]], 0, 0)
+    iota("ex", [[1, 16]], 0, 0)
+    iota("blk", [[16, 8], [0, 16]], 0, 0)
+    iota("tq", [[0, 128]], 1, 0)
+    iota("rc", [[0, 128]], 8192, 0)
+    for name, own in (("tq", 32.0), ("rc", -8192.0)):
+        sel(name, OP.is_gt, 0.0)
+        sel(name, OP.not_equal, own)
+    iota("TB", [[0, 128], [-32, 16]], 224, 0)
+    iota("mk", [[0, 8], [1, 16]], 0, 0)
+    iota("il0", [[16, 8]], 0, 0)
+    iota("l256", [[0, 2], [256, 8]], 0, 0)
+    P = ("pf", 0, 1)
+    PX, PM, PG, PG16, KM, K0, WC, CTC, XOC = [("cf", j, j + 1) for j in range(9)]
+    ts(("cq", 0, 1), "cp", 15, OP.bitwise_and)
+    ts(("cq", 1, 2), "cp", 112, OP.bitwise_and)
+    ts(("cq", 2, 3), "cp", 1, OP.bitwise_and)
+    cp(("cf", 1, 3), ("cq", 0, 2))
+    ts(PX, ("cq", 2, 3), -2, OP.mult, 1, OP.add)
+    tt(PX, PX, P, OP.add)
+    ts("I16", ("cI", 0, 128), P, OP.is_equal)
+    ts("P16", ("cI", 0, 128), PX, OP.is_equal)
+    ts("rm", "ex", PM, OP.is_equal)
+    for k in range(16):
+        ts(("DA", 128 * k, 128 * k + 128), "I16", ("rm", k, k + 1), OP.mult)
+        ts(("DB", 128 * k, 128 * k + 128), "P16", ("rm", k ^ 1, (k ^ 1) + 1), OP.mult)
+    cp("su", "si")
+    ts("BN", "blk", PG, OP.is_equal, -32.0, OP.mult)
+    ts("I32", "I16", 32.0, OP.mult)
+    ts("IB", "I16", 1.0, OP.mult)
+    fill("ONB", 32.0)
+    ts("N16", "I16", -16.0, OP.mult)
+    ts(PG16, PG, 16.0, OP.add)
+    cp(WC, "wi")
+    ts("WT", "cI", PG16, OP.is_equal, WC, OP.mult)
+    ts("BO", "BN", -0.03125, OP.mult)
+    tt("TQ", "tq", "BO", OP.mult)
+    tt("RC", "rc", "BO", OP.mult)
+    ts(KM, PM, -2048.0, OP.add)
+    ts(K0, PM, 0.0, OP.is_equal)
+    ts(CTC, PM, 16.0, OP.mult, 2048.0, OP.add)
+    ts(XOC, PM, 16.0, OP.mult)
+    ts("L1", "cI", PG16, OP.is_equal)
+    ts("LK", "cI", PG16, OP.is_equal, KM, OP.mult)
+    fill(("S", 2048, 2176), 0)
+    ts("on16", ("cI", 0, 128), 0.0, OP.mult, 1.0, OP.add)
+    ts("gm", "il0", PG, OP.is_equal)
+    for q in range(8):
+        ts(("SEL", 128 * q, 128 * q + 128), "on16", ("gm", q, q + 1), OP.mult)
+    cp("GI", "gm")
+    ts("CT", "l256", CTC, OP.add)
+    act("z16", "pf", AF.Exp, scale=-math.log(2.0), bias=60.0 * math.log(2.0))
+    ts("THR", "mk", PM, OP.not_equal, 2.0 ** 97, OP.mult)
+    ts("RQ", "gm", 4096.0, OP.mult)
+    ts("IL", "il0", PM, OP.add)
+    ts("XO", ("l256", 0, 8), XOC, OP.add)
+    act("NIB", "IB", AF.Copy, scale=-1.0)
+    ts("BF2", "BN", 32.0, OP.mult)
+    ts("BF1", "BN", 192.0, OP.mult)
+    act("VJ", "pf", AF.Exp, scale=-math.log(2.0), bias=60.0 * math.log(2.0))
+    ts(("z16", 0, 1), ("z16", 0, 1), 2.5, OP.mult)
+    ts("THR", "THR", ("z16", 0, 1), OP.max)
+
+    def slm(m):
+        return 16 - m, 144 - m
+
+    def listing(out, tab, rhs, wid, more=None):
+        xs = [(out, (tab,) + slm(m), (rhs, m, wid, 16), m == 0, more is None and m == 15) for m in range(16)]
+        if more is not None:
+            xs.append((out, more[0], more[1], False, True))
+        mms(xs)
+
+    def send(t, src, dst_buf, sem):
+        to = T.cores[(rank + 1 + t % (N - 1)) % N]
+        rid, pid = topo.addr(to)[:2]
+        mask = sum(1 << e for e in topo.engines(core, to)[:NENG])
+        i = add("g", [src], [], [lambda e: e.remote_dma(T[dst_buf][:], T[src][:], T.sem[sem], T.sem.sent, pid, rid, mask)], 0.3,
+                sem="sent", inc=NENG)
+        add("n", [], [dst_buf], [], 0.0, sem=sem, inc=NENG, lat=FLIGHT, after=i)
+
+    def hf(x, h):
+        if isinstance(x, str):
+            x = (x, 0, 128)
+        return (x[0], x[1] + 64 * h, x[1] + 64 * h + 64)
+
+    def ablist(q, o):
+        st, en = PIECES[q]
+        a = 128 * (st // 64) + 64 * o + st % 64
+        return ("ABT", a, a + en - st)
+
+    def piece(x, q):
+        return (x, 16 * PIECES[q][0], 16 * PIECES[q][1])
+
+    def grp(x, q):
+        return (x, 128 * q, 128 * q + 128)
+
+    def rowbank(q):
+        return ("b%d" % (5 + q // 4), 128 * (q % 4), 128 * (q % 4) + 128)
+
+    E, CP, COL = ("b2", 0, 128), ("b2", 128, 256), ("b2", 264, 272)
+    C2, OO, CNT, SO = ("b0", 256, 264), ("b1", 256, 272), ("b3", 256, 384), ("b3", 384, 392)
+    c1x, u1, u0, X1P = ("b4", 256, 264), ("b4", 264, 272), ("b4", 272, 280), ("b4", 280, 408)
+    XD, XS, X256, XBA = [grp("b7", j) for j in range(4)]
+    FI, SE = grp("FS", 0), grp("FS", 1)
+    F1, X1, U0 = grp("F1X", 0), grp("F1X", 1), grp("F1X", 2)
+
+    for t in range(RO):
+        last = t == RO - 1
+        gat("Cu", SW, "su")
+        for h in range(2):
+            w = 64 // GS[h]
+            for j in range(GS[h]):
+                gat(("G%d" % h, 16 * w * j, 16 * w * (j + 1)), SW, ("Cu", 64 * h + w * j, 64 * h + w * (j + 1)))
+            for tab, bk, o in (("DB", "b%d" % (5 + h), 64), ("DA", "b%d" % h, 0)):
+                mms([((bk, 0, 64), grp(tab, k), ("G%d" % h, k, 1024, 16), k == 0, k == 15) for k in range(16)])
+                cp(("ABT", 128 * h + o, 128 * h + o + 64), (bk, 0, 64))
+        ts("C16", "Cu", 1, OP.add)
+        act("SL", "TB", AF.Copy, off="su")
+        mms([(CP, "I16", "C16", True, True)])
+        xs = [(E, "I32", "C16", True, False), (E, "IB", "SL", False, not t)]
+        if t:
+            xs.append((E, "ONB", "FCB", False, True))
+        mms(xs)
+        for q in range(len(PIECES)):
+            if q in VB:
+                gat(piece("XB", q), XW, ablist(q, 1))
+            else:
+                act(piece("XB", q), XW, AF.Copy, off=ablist(q, 1))
+            gsub(piece("DD", q), XW, ablist(q, 0), piece("XB", q))
+            act(piece("ZX", q), piece("DD", q), AF.Abs)
+        for h in range(2):
+            U, Q, R = ("b%d" % h, 128, 192), ("b%d" % (3 + h), 0, 64), ("b%d" % (3 + h), 64, 128)
+            mms([(U, ("WT",) + slm(k), ("ZX", 1024 * h + k, 1024 * h + 1024, 16), k == 0, k == 15) for k in range(16)])
+            ts(hf("ui", h), U, 16, OP.add)
+            ts(hf("w2", h), hf("ui", h), 255, OP.bitwise_and)
+            tt(hf("sq", h), hf("w2", h), hf("w2", h), OP.mult)
+            tt(hf("y", h), hf("sq", h), hf(E, h), OP.add)
+            ts(hf("yy", h), hf("y", h), 480, OP.bitwise_and)
+            ts(hf("cl", h), hf("yy", h), 0, OP.is_equal)
+            mms([(Q, "TQ", hf("cl", h), True, True)])
+            mms([(R, "RC", hf("cl", h), True, False), (R, "I16", hf("C16", h), False, True)])
+            ts(hf(SE, h), Q, 33.0, OP.is_equal)
+            tt(hf("F2", h), hf(SE, h), hf(CP, h), OP.mult)
+            ts(hf(FI, h), Q, 32.0, OP.is_equal)
+            ts(hf(F1, h), R, 6143.0, OP.add, 0.0, OP.min)
+        ts("uk", "ui", 2047, OP.bitwise_and)
+        ts(U0, "uk", K0, OP.mult)
+        for h in range(2):
+            FP = ("b%d" % (3 + h), 128, 192)
+            mms([(FP, "I16", hf(FI, h), True, True)])
+            tt(hf(X1, h), FP, hf("uk", h), OP.mult)
+        listing(C2, "L1", "F2", 128)
+        ts("mN%d" % t, C2, 4097.0, OP.mult, -1.0, OP.add)
+        send(t, "mN%d" % t, "rN%d" % t, "aN%d" % t)
+        if not last:
+            act("sg", C2, AF.Sign, accum_out=("fc", 0, 1))
+            act("FCB", "IB", AF.Identity, scale=0.0, bias=("fc", 0, 1))
+        mms([(COL, F1, "GI", True, True)])
+        act("cola", COL, AF.Copy, scale=-1.0)
+        act("col", COL, AF.Copy)
+        for q in range(8):
+            mms([(rowbank(q), grp("SEL", q), F1, True, True)])
+        for q in range(8):
+            if q < 8 - SQ:
+                ts(grp("EQ", q), rowbank(q), ("col", q, q + 1), OP.is_equal)
+            else:
+                act(grp("EN", q), rowbank(q), AF.Abs, bias=("cola", q, q + 1))
+        act(("EQ", 1024 - 128 * SQ, 1024), ("EN", 1024 - 128 * SQ, 1024), AF.Relu, scale=-1.0, bias=1.0)
+        for h in range(2):
+            mms([((CNT[0], CNT[1] + 16 * q, CNT[1] + 16 * q + 16), grp("EQ", q), "VJ", True, True) for q in range(4 * h, 4 * h + 4)])
+        listing(("b4", 256, 280), "L1", "F1X", 384)
+        ts("c1u", c1x, 2048.0, OP.add)
+        cp("c1h", c1x)
+        gat("Sc", SD, "c1u")
+        tt("lt", CNT, "THR", OP.is_gt)
+        mms([(SO, "lt", "RQ", True, False), (SO, "I16", "c1h", False, True)])
+        mms([(X1P, "I16", X1, True, False), (X1P, "N16", FI, False, True)])
+        tt("Sd", "Sc", X1P, OP.add)
+        ts("Sn", "Sd", 2047, OP.bitwise_and)
+        tt("so", SO, "IL", OP.min)
+        ts("sou", "so", 2048.0, OP.add)
+        sca(SD, "sou", "Sn")
+        ts("n1", "si", 5, OP.mult, -16, OP.add)
+        ts("h1", c1x, 0.0, OP.is_lt, 16777216.0, OP.mult)
+        tt("h2", "h1", c1x, OP.add)
+        tt("n2", "n1", u0, OP.add)
+        ts("n3", "n2", 2047, OP.bitwise_and)
+        tt("sb", "h2", "n3", OP.max)
+        cp("x1", u1)
+        listing(OO, "LK", "FS", 256, ("I16", "CT"))
+        cp("ou", OO)
+        act("z2", ZW, AF.Copy, off=("ou", 8, 16))
+        act("z1", ZW, AF.Copy, off=("ou", 0, 8))
+        mms([(XD, "BF2", SE, True, False), (XD, "IB", "xb", False, False), (XD, "NIB", "z2", False, True)])
+        act("mX%d" % t, XD, AF.Abs, bias=1024.0)
+        send(t, "mX%d" % t, "rX%d" % t, "aX%d" % t)
+        ts("x2", "x1", 15, OP.bitwise_and)
+        tt("x3", "x2", "XO", OP.add)
+        cp("xou", "x3")
+        sca(XW, "xou", "z1")
+        mms([(XS, "BF1", FI, True, False), (XS, "IB", "xb", False, False), (XS, "IB", "z1", False, True)])
+        act(X256, "xb", AF.Identity, bias=256.0)
+        ts("xv", XS, 0.5, OP.mult, 2047.75, OP.add)
+        tt(XBA, "xv", X256, OP.min)
+        if last:
+            dma("y", "oV", [XW], [], T.yv[:], T.ZX[:, 2048:4096], 2 * LOCAL)
+            acc = ("b5", 0, 256)
+            tt(acc, ("S", 0, 256), ("S", 256, 512), OP.add)
+            for q in range(2, 8):
+                tt(acc if q < 7 else "yto", acc, ("S", 256 * q, 256 * q + 256), OP.add)
+            dma("y", "oT", ["yto"], [], T.yt[:], T.yto[:], LOCAL)
+        tt("se", "sb", "rN%d" % t, OP.max)
+        ts("si", "se", 2047, OP.bitwise_and)
+        cp("sf" if last else "su", "si")
+        if last:
+            dma("s", "oS", ["sf"], [], T.ys[:], T.sf[:], LOCAL)
+        tt("xm", XBA, "rX%d" % t, OP.min)
+        ts("xn", "xm", 255, OP.bitwise_and)
+        cp("xb", "xn")
+    dma("y", "oX", ["xb"], [], T.yx[:], T.xb[:], LOCAL)
+    return emit()

@@ -3,10 +3,14 @@ from concourse.mybir import AluOpType as OP, ActivationFunctionType as AF
 
 N, RO = 8, 3
 NENG = 8
-PIECES = ((0, 16), (16, 32), (32, 64), (64, 96), (96, 112), (112, 128))
-VB = (4,)
-GS = (1, 2)
-SQ = 3
+CFG = {
+    "g": ((("v", 0, 32), ("s", 32, 64)), (("v", 0, 32), ("s", 32, 64))),
+    "x": ((("s", 0, 16), ("s", 16, 40), ("s", 40, 64)), (("s", 0, 32), ("s", 32, 48), ("s", 48, 64))),
+    "after": {},
+    "size": "vs",
+    "cu": "vv", "ab": "svsv", "c16": "vv", "sl": "ss", "qe": "ss", "q": "vv", "sq": "vv", "v16": "vv", "join": "yy", "u0": "ss", "fi": "ss", "f1": "vv", "x1n": "vv", "mn": "vv", "c1u": "vv",
+    "sc": "ss", "su": "vv", "n1": "ss", "x1": "ss", "ou": "s", "db": "v", "yts": 4,
+}
 
 F32, F16, BF, I4, U2 = "float32", "float16", "bfloat16", "int32", "uint16"
 SCRATCH = {}
@@ -17,40 +21,31 @@ def _sb(dtype, **bufs):
         SCRATCH[name] = ("sbuf", [128, bufs[name]], dtype)
 
 
-_sb(I4, S=2176, si=8, wi=1)
-_sb(BF, ZX=4096, xb=128)
+_sb(I4, S=2304, si=8, wi=1)
+_sb(BF, ZB=6144, Z=2048, XB=2048, xb=128)
 _sb(U2, su=8)
 _sb(I4, cp=1, cq=4)
-_sb(F32, cI=144, cf=16, tq=128, rc=128, blk=128, mk=128, l256=16, rm=16, gm=8, ex=16, z16=16, THR=128, IL=8, XO=8, il0=8, pf=16)
-_sb(F16, I16=128, P16=128, I32=128, N16=128, L1=144, LK=144, DA=2048, DB=2048, BN=128, SEL=1024, on16=128, TQ=128, RC=128,
-    BO=128, BF1=128, BF2=128, RQ=8, GI=8, CT=16)
-_sb(BF, TB=2048, SL=128, FCB=128, ONB=128, IB=128, NIB=128, WT=144, VJ=16)
+_sb(F32, cI=144, cf=24, blk=128, mk=64, l256=16, rm=16, ex=16, THR=128, XO=8, il0=8, pf=16, he=32, pw=2)
+_sb(F16, I16=128, P16=128, NI16=128, NI32=128, I6=128, N512=128, K12=64, L1=144, LK=144, DA=2048, DB=2048, BO=128, LT=128, MK=128,
+    SEL=512, BF1=128, BFH=128, BF2=128, RQ=8, GI=8, CT=16)
+_sb(BF, TB=2048, SL=128, FCB=64, ONB=128, IB=128, NIB=128, WN=144, WP=144, VJ=64, hs=512)
 _sb(U2, Cu=128, ABT=256, ou=16, c1u=8, sou=8, xou=8)
-_sb(F16, C16=128, G0=1024, G1=1024, cl=128, FS=256, F1X=384, F2=128, lt=128, c1h=8)
-_sb(BF, XB=2048, DD=2048, EQ=1024, EN=1024, z1=128, z2=128, sg=8)
-_sb(I4, ui=128, w2=128, sq=128, y=128, yy=128, uk=128, Sc=128, Sd=128, Sn=128, x1=8, x2=8, x3=8, n2=8, n3=8, se=8, xv=128,
-    xm=128, xn=128)
-_sb(F32, col=8, cola=8, so=8, n1=8, h1=8, h2=8, sb=8, fc=1, sf=8, yto=256)
+_sb(F16, C16=128, G0=1024, G1=1024, cl=128, FS=256, GF=512, lt=128, V16=128, qe=128, hv=128, SH=1024)
+_sb(BF, EQ=768, z1=128, z2=128, sg=8)
+_sb(I4, ui=128, uk=128, sq=128, yy=128, Sc=128, Sd=128, Sn=128, x1=8, x2=8, n2=8, n3=8, se=8, xm=128, xn=128)
+_sb(F32, n1=8, h1=8, h2=8, sb=8, fc=1, sf=8, yta=256, yto=256)
 SEMAPHORES = ["qv", "qs", "qp", "qg", "dS0", "dX", "dx0", "dw", "ds0", "oV", "oT", "oX", "oS", "sent"]
 for _t in range(RO):
     _sb(F32, **{"mN%d" % _t: 8, "rN%d" % _t: 8})
     _sb(BF, **{"mX%d" % _t: 128, "rX%d" % _t: 128})
-    SEMAPHORES += ["aN%d" % _t, "aX%d" % _t]
+    SEMAPHORES += ["aN%d0" % _t, "aN%d1" % _t, "aX%d" % _t]
 PSUM = ["b%d" % _b for _b in range(8)]
 for _b in PSUM:
     SCRATCH[_b] = ("psum", [128, 512], F32)
 
-CYC, PECYC, GATH, SCAT, WAKE, LOCAL, FLIGHT = 0.0012, 0.0005, 2.0, 3.8, 0.06, 2.0, 3.0
-ORDER = (
-    "000105270403071t020m0l0k0o080n28061v0b0s242s0q2k0p220g1l0v1b131s0t152p1n191r171j0r2t251c0w181m1o0u1a160y1i5t14121p101u1k2123"
-    "0z1w11261x1f1h1d1g1e0x2v0e382w090h0f0i0j0a312x0c2z0d2y323e3h301q333f353b343i3g3k363c3n3j3l3q3d3o3m3t3r3p3u373s1y3v39293a2046"
-    "3w2a1z3x472h3y484j494k4a3z2b4b412g402f4c42454e444d432d4l4f4h2e4g4i2n4p4m2m2l2i2r2u544v534q4n4y2o4w522c4x554r4o514t2q4z505a5h"
-    "4u4s2j585b56575d605i595c5j5k5f5e5n615u5w5z625o5g5x5v635p645l685y655m695q6a666c5r6b676d5s6e6g6f6h6i9k6z6m6n6t6o6q6p6s75786r6y"
-    "6u6j766w726v797071777b6x737e7a7c747h7k7f7d7i7g6k7j7l6l7m7n7x7o7p7y7q7z8a7r7s807w7v818b827t837u8c858d84868988878p8t8e8g8f8m8r"
-    "8u8h8o8w8v8n8q8i8k8s91988l8x8j8y928z9r93909a94999b9e95969q9n9f9o9z979g9l9c9ma09d9s9p9h9ua19i9j9t9va29w9xa3a79ya4a8a9a5aqada6"
-    "aeakafahagajawazaiaaalaxanatamb0b8b2aob5aub1b3avayb6b4bbb9b7apbcbaabarasbdd9acbebobfbgbpbhbqc1bibjbrc2bsbmbnbtbkbublc3bwc4bv"
-    "c0bzbxcjcickbyc5dgc6cbcgcedhcdcfclccchdicxcqcoctcndkcmcrcyc7czcscpd0dld3cuc8cvdmd4dac9dndcd5djcwdfcadbddd1dsdoded2dpdtd6dqd7"
-    "drd8dwdudxdvdydze0e9e1eae5e2ebe6e3ece7e4e8")
+COST = {"cyc": 0.00086, "pe": 0.00045, "gath": 1.35, "scat": 3.8, "wake": 0.23, "own": 0.23, "local": 2.0, "flight": 2.4, "S": 4.3, "X": 6.0, "act": 50,
+        "look": 0.1, "idle": 3.0, "tries": 40, "jit": 0.3, "chunk": 4, "swaps": 8000, "far": 4, "heat": 0.03}
+PLAN = {}
 
 
 def make_plan(g, T):
@@ -58,6 +53,8 @@ def make_plan(g, T):
     qsem = {"v": "qv", "s": "qs", "p": "qp", "g": "qg"}
     nodes = []
     hist = {}
+    hint = []
+    WAKE = COST["wake"]
 
     def rng(x):
         return (x, 0, T[x].shape[1]) if isinstance(x, str) else x
@@ -74,12 +71,14 @@ def make_plan(g, T):
                     if name in PSUM:
                         if nodes[j]["q"] != q or (over and q != "p"):
                             pred[j] = True
-                        elif over:
+                        elif q == "p":
                             pred.setdefault(j, False)
                     elif over:
                         pred[j] = True
         if after is not None:
             pred[after] = False
+        while hint:
+            pred.setdefault(hint.pop(), False)
         nodes.append({"q": q, "fns": fns, "dur": dur, "sem": sem, "inc": inc, "lat": lat, "pred": pred, "i": i})
         for name, a, b in wr:
             keep = [h for h in hist.get(name, []) if not (a <= h[0] and h[1] <= b and h[3] in pred)]
@@ -90,47 +89,144 @@ def make_plan(g, T):
 
     def order():
         n = len(nodes)
+        qs = [x["q"] for x in nodes]
+        dur = [x["dur"] for x in nodes]
         succ = [[] for _ in nodes]
+        pred = [[] for _ in nodes]
         for x in nodes:
             for j, w in x["pred"].items():
-                succ[j].append((x["i"], w))
+                gap = nodes[j]["lat"] + (COST["own"] if qs[j] == x["q"] else WAKE) if w else 0.0
+                succ[j].append((x["i"], gap))
+                pred[x["i"]].append((j, gap))
+
+        def run(prio, first, then, tail):
+            left = [len(x) for x in first]
+            ready = list(tail)
+            free = dict((q, 0.0) for q in "vspgyn")
+            avail = dict((q, []) for q in "vspgyn")
+            best = {}
+            for i in range(n):
+                if not left[i]:
+                    avail[qs[i]].append(i)
+            out, ends, dirty = [], [0.0] * n, set(avail)
+            while len(out) < n:
+                for q in dirty:
+                    best.pop(q, None)
+                    if avail[q]:
+                        fr = free[q]
+                        t0 = max(fr, min(ready[i] for i in avail[q])) + COST["look"]
+                        i = max((i for i in avail[q] if ready[i] <= t0), key=lambda k: prio[k] - COST["idle"] * max(ready[k] - fr, 0.0))
+                        best[q] = (max(fr, ready[i]), i)
+                t1, i = min(best.values())
+                q = qs[i]
+                avail[q].remove(i)
+                dirty = set([q])
+                ends[i] = t1 + dur[i]
+                if q != "n":
+                    free[q] = ends[i]
+                out.append(i)
+                for j, gap in then[i]:
+                    ready[j] = max(ready[j], ends[i] + gap)
+                    left[j] -= 1
+                    if not left[j]:
+                        avail[qs[j]].append(j)
+                        dirty.add(qs[j])
+            return out, ends
+
+        lat = [x["lat"] for x in nodes]
         prio = [0.0] * n
         for i in range(n - 1, -1, -1):
-            x = nodes[i]
-            best = max([prio[j] + (WAKE if w else 0.0) for j, w in succ[i]] + [0.0])
-            prio[i] = best + x["dur"] + x["lat"]
-        left = [len(x["pred"]) for x in nodes]
-        ready = [0.0] * n
-        free = {}
-        avail = {}
-        for x in nodes:
-            if not left[x["i"]]:
-                avail.setdefault(x["q"], []).append(x["i"])
-        out = []
-        while any(avail.values()):
-            pick = None
-            for q in avail:
-                if not avail[q]:
-                    continue
-                fr = free.get(q, 0.0) if q != "n" else 0.0
-                t0 = min(max(fr, ready[i]) for i in avail[q])
-                c = [i for i in avail[q] if max(fr, ready[i]) <= t0 + 0.02]
-                i = max(c, key=lambda k: prio[k])
-                t1 = max(fr, ready[i])
-                if pick is None or t1 < pick[0]:
-                    pick = (t1, i, q)
-            t1, i, q = pick
-            avail[q].remove(i)
-            x = nodes[i]
-            end = t1 + x["dur"]
-            free[q] = end
-            out.append(i)
-            for j, w in succ[i]:
-                ready[j] = max(ready[j], end + x["lat"] + (WAKE if w else 0.0))
-                left[j] -= 1
-                if not left[j]:
-                    avail.setdefault(nodes[j]["q"], []).append(j)
-        return out
+            prio[i] = max([prio[j] + gap for j, gap in succ[i]] + [lat[i]]) + dur[i]
+        best, seed, base = None, 12345, prio
+        for it in range(COST["tries"]):
+            out, ends = run(prio, pred, succ, [0.0] * n)
+            span = max(ends[i] + lat[i] for i in range(n))
+            if best is None or span < best[0]:
+                best, base = (span, out), ends
+            jit = []
+            for i in range(n):
+                seed = (seed * 1103515245 + 12345) % 2147483648
+                jit.append(base[i] + lat[i] + COST["jit"] * (seed / 2147483648.0 - 0.5))
+            prio = run(jit, succ, pred, lat)[1]
+        seq = list(best[1])
+        pos, before, behind, last = [0] * n, [-1] * n, [-1] * n, {}
+        for k, i in enumerate(seq):
+            pos[i] = k
+            if qs[i] != "n":
+                if qs[i] in last:
+                    before[i], behind[last[qs[i]]] = last[qs[i]], i
+                last[qs[i]] = i
+        sinks = [i for i in range(n) if not succ[i]]
+
+        def times(ends, k0):
+            for i in seq[k0:]:
+                t1 = ends[before[i]] if before[i] >= 0 else 0.0
+                for j, gap in pred[i]:
+                    if ends[j] + gap > t1:
+                        t1 = ends[j] + gap
+                ends[i] = t1 + dur[i]
+            return max([ends[i] + lat[i] for i in sinks])
+
+        def swap(u, v):
+            a, b = pos[u], pos[v]
+            old, late = seq[a:b + 1], set([u])
+            for i in old[1:]:
+                if (before[i] in late and i != v) or any(j in late for j, gap in pred[i]):
+                    if i == v:
+                        return None
+                    late.add(i)
+            seq[a:b + 1] = [i for i in old if i not in late] + [i for i in old if i in late]
+            for k in range(a, b + 1):
+                pos[seq[k]] = k
+            p, s = before[u], behind[v]
+            before[v], behind[v], before[u], behind[u] = p, u, v, s
+            if p >= 0:
+                behind[p] = v
+            if s >= 0:
+                before[s] = u
+            return a
+
+        ends = [0.0] * n
+        span = times(ends, 0)
+        best = (span, list(seq))
+        for it in range(COST["swaps"]):
+            i, arcs = max(sinks, key=lambda k: ends[k] + lat[k]), []
+            while i >= 0:
+                start, j0 = ends[i] - dur[i] - 1e-9, -1
+                for j, gap in pred[i]:
+                    if ends[j] + gap > start:
+                        j0 = j
+                if j0 < 0 and before[i] >= 0 and ends[before[i]] > start:
+                    j0 = before[i]
+                    arcs.append((j0, i))
+                i = j0
+            if not arcs:
+                break
+            seed = (seed * 1103515245 + 12345) % 2147483648
+            v = arcs[(seed >> 8) % len(arcs)][1]
+            seed = (seed * 1103515245 + 12345) % 2147483648
+            moved, a = [], n
+            for step in range(1 + (seed >> 8) % COST["far"]):
+                u = before[v]
+                k = swap(u, v) if u >= 0 else None
+                if k is None:
+                    break
+                moved.append(u)
+                a = min(a, k)
+            if not moved:
+                continue
+            trial = list(ends)
+            new = times(trial, a)
+            seed = (seed * 1103515245 + 12345) % 2147483648
+            if new <= span - COST["heat"] * (1 - it / COST["swaps"]) * math.log((seed + 1) / 2147483648.0):
+                span, ends = new, trial
+                if span < best[0]:
+                    best = (span, list(seq))
+            else:
+                for u in reversed(moved):
+                    swap(v, u)
+        PLAN["span"] = best[0]
+        return best[1]
 
     def emit():
         count = {}
@@ -146,8 +242,9 @@ def make_plan(g, T):
                 for k, m in event[(src, need[src])].items():
                     clock[q][k] = max(clock[q].get(k, 0), m)
 
-        seq = [36 * int(ORDER[i], 36) + int(ORDER[i + 1], 36) for i in range(0, len(ORDER), 2)] or order()
-        for i in seq:
+        if "seq" not in PLAN:
+            PLAN["seq"] = order()
+        for i in PLAN["seq"]:
             x = nodes[i]
             q = x["q"]
             if q == "n":
@@ -182,31 +279,38 @@ def make_plan(g, T):
         for q in ("v", "s", "p", "g"):
             if count[q] > clock["g"].get(q, 0):
                 wait("g", {q: count[q]})
-        return nodes, seq
-    return add, emit
+        return nodes
+    return add, emit, hint, lambda: len(nodes) - 1
 
 
 def rank_program(g, core, T, topo):
     rank = T.rank_of(core)
     if rank is None:
         return
-    add, emit = make_plan(g, T)
+    add, emit, hint, count = make_plan(g, T)
+    C = CFG
+    CYC, GATH = COST["cyc"], COST["gath"]
 
     def cols(x):
         if isinstance(x, str):
-            n = T[x].shape[1]
-            return T[x][:, 0:n], (x, 0, n)
+            x = (x, 0, T[x].shape[1])
         name, a, b = x[:3]
+        if len(x) == 6:
+            return (T[name][x[4]:x[5], a:b:x[3]] if x[3] > 1 else T[name][x[4]:x[5], a:b]), (name, a, b)
         if len(x) == 4:
             return T[name][:, a:b:x[3]], (name, a, b)
         return T[name][:, a:b], (name, a, b)
 
     def width(x):
         r = cols(x)[1]
-        return (r[2] - r[1]) // (x[3] if len(x) == 4 and not isinstance(x, str) else 1)
+        st = x[3] if len(x) >= 4 and not isinstance(x, str) else 1
+        return (r[2] - r[1] + st - 1) // st
 
     def buf(x):
         return x if isinstance(x, str) else x[0]
+
+    def part(x, p0, p1):
+        return (x[0], x[1], x[2], x[3] if len(x) > 3 else 1, p0, p1)
 
     def small(*xs):
         return all(SCRATCH[buf(x)][2] in (F16, BF, U2) for x in xs)
@@ -234,21 +338,17 @@ def rank_program(g, core, T, topo):
         o, a = cols(out)[0], cols(in0)[0]
         vec([in0], out, lambda e: e.tensor_copy(o, a), width(out) * (0.5 if small(out, in0) else 1))
 
-    def gat(out, win, off):
-        o, w, f = cols(out)[0], cols(win)[0], cols(off)[0]
-        vec([win, off], out, lambda e: e.tensor_copy(o, w.indirect(f)), 50 + GATH * width(out))
-
     def gsub(out, win, off, in1):
         o, w, f, b = cols(out)[0], cols(win)[0], cols(off)[0], cols(in1)[0]
         vec([win, off, in1], out, lambda e: e.tensor_tensor(o, w.indirect(f), b, OP.subtract), 50 + GATH * width(out))
 
     def sca(win, off, in0):
         w, f, a = cols(win)[0], cols(off)[0], cols(in0)[0]
-        vec([off, in0], win, lambda e: e.tensor_copy(w.indirect(f), a), 50 + SCAT * width(in0))
+        vec([off, in0], win, lambda e: e.tensor_copy(w.indirect(f), a), 50 + COST["scat"] * width(in0))
 
     def fill(out, v):
         o = cols(out)[0]
-        vec([], out, lambda e: e.memset(o, v), width(out))
+        vec([], out, lambda e: e.memset(o, v), width(out) * (0.5 if small(out) else 1))
 
     def act(out, in0, func, off=None, **kw):
         o, a = cols(out)[0], cols(in0)[0]
@@ -262,16 +362,45 @@ def rank_program(g, core, T, topo):
             f, rf = cols(off)
             a = a.indirect(f)
             rd.append(rf)
-        add("s", rd, wr, [lambda e: e.activation(o, a, func, **kk)], CYC * (65 + width(out) * (GATH if off is not None else 1)))
+        add("s", rd, wr, [lambda e: e.activation(o, a, func, **kk)], CYC * (COST["act"] + width(out) * (GATH if off is not None else 1)))
+
+    def gat(q, out, win, off):
+        if q == "s":
+            act(out, win, AF.Copy, off=off)
+        else:
+            o, w, f = cols(out)[0], cols(win)[0], cols(off)[0]
+            vec([win, off], out, lambda e: e.tensor_copy(o, w.indirect(f)), 50 + GATH * width(out))
+
+    def lin(q, out, in0, mul=1.0, plus=0.0):
+        if q == "s":
+            if isinstance(plus, tuple) or plus:
+                act(out, in0, AF.Identity, scale=mul, bias=plus)
+            else:
+                act(out, in0, AF.Copy, scale=mul)
+        elif mul == 1.0 and plus == 0.0:
+            cp(out, in0)
+        else:
+            ts(out, in0, mul, OP.mult, plus, OP.add)
+
+    def pos(q, out, in0, plus):
+        if q == "s":
+            act(out, in0, AF.Relu, bias=plus)
+        else:
+            ts(out, in0, plus, OP.add, 0.0, OP.max)
 
     def one(x):
         o, a, b = cols(x[0])[0], cols(x[1])[0], cols(x[2])[0]
         return lambda e: e.matmul(o, a, b, x[3], x[4])
 
-    def mms(xs):
-        rd = sorted(set(cols(x[1])[1] for x in xs) | set(cols(x[2])[1] for x in xs))
-        wr = sorted(set(cols(x[0])[1] for x in xs))
-        add("p", rd, wr, [one(x) for x in xs], sum(max(64, width(x[0])) * PECYC for x in xs))
+    def mms(all_):
+        for j in range(0, len(all_), COST["chunk"]):
+            xs = all_[j:j + COST["chunk"]]
+            rd = sorted(set(cols(x[1])[1] for x in xs) | set(cols(x[2])[1] for x in xs))
+            wr = sorted(set(cols(x[0])[1] for x in xs))
+            add("p", rd, wr, [one(x) for x in xs], sum(max(64, width(x[0])) * COST["pe"] for x in xs))
+
+    def msum(out, *pairs):
+        mms([(out, a, b, j == 0, j == len(pairs) - 1) for j, (a, b) in enumerate(pairs)])
 
     def iota(out, pattern, base, cm, flag=True):
         o = cols(out)[0]
@@ -279,243 +408,270 @@ def rank_program(g, core, T, topo):
             fn = lambda e: e.iota(o, pattern, base, cm, allow_small_or_imprecise_dtypes=True)
         else:
             fn = lambda e: e.iota(o, pattern, base, cm)
-        add("g", [], [cols(out)[1]], [fn], 0.13 + 2 * CYC * width(out))
+        prev["g"] = add("g", [], [cols(out)[1]], [fn], 0.13 + 2 * CYC * width(out), after=prev.get("g"))
 
-    def sel(out, op, v):
-        o, ro = cols(out)
-        add("g", [ro], [ro], [lambda e: e.affine_select(o, o, [[1, 128]], op, v, 0, -1)], 0.17 + 2 * CYC * width(out))
+    def dma(q, s, rd, wr, out, in_, us, turn=False):
+        prev[q] = add(q, rd, wr, [lambda e: e.dma_start(out, in_)], 0.1, sem=s, inc=16, lat=us, after=prev.get(q) if turn else None)
 
-    def dma(q, s, rd, wr, out, in_, us):
-        add(q, rd, wr, [lambda e: e.dma_start(out, in_)], 0.1, sem=s, inc=16, lat=us)
+    prev = {}
 
-    SW, SD, XW, ZW = ("S", 0, 2048), ("S", 0, 2176), ("ZX", 2048, 4096), ("ZX", 0, 4096)
+    SW, SD = ("S", 0, 2048), ("S", 0, 2304)
+    DW, WX, XW, xw = ("ZB", 0, 4096), ("ZB", 2048, 6144), ("ZB", 4096, 6144), ("ZB", 2048, 4096, 16)
+    LOCAL = COST["local"]
 
     dma("s", "ds0", [], ["si"], T.si[:], T.s0[:], LOCAL)
-    dma("y", "dS0", [], [SW], T.S[:, 0:2048], T.stm[:], 6.0)
-    dma("s", "dw", [], ["wi"], T.wi[:], T.wt[:], LOCAL)
-    dma("y", "dX", [], [XW], T.ZX[:, 2048:4096], T.vx[:], 9.0)
-    dma("s", "dx0", [], ["xb"], T.xb[:], T.x0[:], LOCAL)
+    dma("y", "dS0", [], [SW], T.S[:, 0:2048], T.stm[:], COST["S"])
+    dma("s", "dw", [], ["wi"], T.wi[:], T.wt[:], COST["S"] + 0.5, True)
+    dma("y", "dX", [], [XW], T.ZB[:, 4096:6144], T.vx[:], COST["X"], True)
+    dma("y", "dx0", [], ["xb"], T.xb[:], T.x0[:], COST["X"] + 0.5, True)
 
     iota("cp", [[1, 1]], 0, 1, False)
     iota("pf", [[0, 16]], 0, 1)
     iota("cI", [[1, 144]], 0, 0)
     iota("ex", [[1, 16]], 0, 0)
     iota("blk", [[16, 8], [0, 16]], 0, 0)
-    iota("tq", [[0, 128]], 1, 0)
-    iota("rc", [[0, 128]], 8192, 0)
-    for name, own in (("tq", 32.0), ("rc", -8192.0)):
-        sel(name, OP.is_gt, 0.0)
-        sel(name, OP.not_equal, own)
-    iota("TB", [[0, 128], [-32, 16]], 224, 0)
-    iota("mk", [[0, 8], [1, 16]], 0, 0)
+    iota("mk", [[0, 4], [1, 16]], 0, 0)
     iota("il0", [[16, 8]], 0, 0)
     iota("l256", [[0, 2], [256, 8]], 0, 0)
+    iota("he", [[64, 2], [0, 16]], 0, 0)
+    iota("hs", [[32, 4], [16, 2], [0, 64]], 0, 0)
+    iota("TB", [[0, 128], [32, 16]], 256, 0)
+    iota(("ZB", 2048, 4096), [[0, 2048]], 1024, 0)
     P = ("pf", 0, 1)
-    PX, PM, PG, PG16, KM, K0, WC, CTC, XOC = [("cf", j, j + 1) for j in range(9)]
+    PX, PM, PG, P64, PH, PG16, KM, K0, WC, WM, CTC, XOC, PG64, SP0, SP1 = [("cf", j, j + 1) for j in range(15)]
     ts(("cq", 0, 1), "cp", 15, OP.bitwise_and)
     ts(("cq", 1, 2), "cp", 112, OP.bitwise_and)
-    ts(("cq", 2, 3), "cp", 1, OP.bitwise_and)
-    cp(("cf", 1, 3), ("cq", 0, 2))
-    ts(PX, ("cq", 2, 3), -2, OP.mult, 1, OP.add)
+    ts(("cq", 2, 3), "cp", 63, OP.bitwise_and)
+    ts(("cq", 3, 4), "cp", 1, OP.bitwise_and)
+    cp(("cf", 1, 4), ("cq", 0, 3))
+    ts(PX, ("cq", 3, 4), -2, OP.mult, 1, OP.add)
     tt(PX, PX, P, OP.add)
     ts("I16", ("cI", 0, 128), P, OP.is_equal)
     ts("P16", ("cI", 0, 128), PX, OP.is_equal)
     ts("rm", "ex", PM, OP.is_equal)
     for k in range(16):
         ts(("DA", 128 * k, 128 * k + 128), "I16", ("rm", k, k + 1), OP.mult)
-        ts(("DB", 128 * k, 128 * k + 128), "P16", ("rm", k ^ 1, (k ^ 1) + 1), OP.mult)
-    cp("su", "si")
-    ts("BN", "blk", PG, OP.is_equal, -32.0, OP.mult)
-    ts("I32", "I16", 32.0, OP.mult)
-    ts("IB", "I16", 1.0, OP.mult)
-    fill("ONB", 32.0)
-    ts("N16", "I16", -16.0, OP.mult)
+        lin(C["db"], ("DB", 128 * k, 128 * k + 128), "P16", ("rm", k ^ 1, (k ^ 1) + 1))
+    for h in range(2):
+        cp(("su", 4 * h, 4 * h + 4), ("si", 4 * h, 4 * h + 4))
+    ts("BO", "blk", PG, OP.is_equal)
+    for name, v in (("NI16", -1.0), ("NI32", -32.0), ("I6", 16.0), ("N512", -512.0), ("IB", 1.0), ("NIB", -1.0), ("MK", 4096.0)):
+        lin("s", name, "I16", v)
+    for name, v in (("BF1", -3072.0), ("BFH", -0.5), ("BF2", -1024.0)):
+        lin("s", name, "BO", v)
+    fill("ONB", -16.0)
+    fill("K12", -1280.0)
     ts(PG16, PG, 16.0, OP.add)
     cp(WC, "wi")
-    ts("WT", "cI", PG16, OP.is_equal, WC, OP.mult)
-    ts("BO", "BN", -0.03125, OP.mult)
-    tt("TQ", "tq", "BO", OP.mult)
-    tt("RC", "rc", "BO", OP.mult)
+    ts(WM, "wi", -1.0, OP.mult)
+    ts("WN", "cI", PG16, OP.is_equal, WM, OP.mult)
+    ts("WP", "cI", PG16, OP.is_equal, WC, OP.mult)
+    ts("LT", ("cI", 0, 128), P, OP.is_gt, -2048.0, OP.mult)
+    tt("LT", "LT", "BO", OP.mult)
+    tt("MK", "MK", "LT", OP.add)
     ts(KM, PM, -2048.0, OP.add)
     ts(K0, PM, 0.0, OP.is_equal)
     ts(CTC, PM, 16.0, OP.mult, 2048.0, OP.add)
     ts(XOC, PM, 16.0, OP.mult)
     ts("L1", "cI", PG16, OP.is_equal)
     ts("LK", "cI", PG16, OP.is_equal, KM, OP.mult)
-    fill(("S", 2048, 2176), 0)
-    ts("on16", ("cI", 0, 128), 0.0, OP.mult, 1.0, OP.add)
-    ts("gm", "il0", PG, OP.is_equal)
-    for q in range(8):
-        ts(("SEL", 128 * q, 128 * q + 128), "on16", ("gm", q, q + 1), OP.mult)
-    cp("GI", "gm")
+    fill(("S", 2048, 2304), 0)
+    ts("SEL", "hs", PG, OP.is_equal)
+    ts("GI", "il0", PG, OP.is_equal)
     ts("CT", "l256", CTC, OP.add)
-    act("z16", "pf", AF.Exp, scale=-math.log(2.0), bias=60.0 * math.log(2.0))
-    ts("THR", "mk", PM, OP.not_equal, 2.0 ** 97, OP.mult)
-    ts("RQ", "gm", 4096.0, OP.mult)
-    ts("IL", "il0", PM, OP.add)
     ts("XO", ("l256", 0, 8), XOC, OP.add)
-    act("NIB", "IB", AF.Copy, scale=-1.0)
-    ts("BF2", "BN", 32.0, OP.mult)
-    ts("BF1", "BN", 192.0, OP.mult)
-    act("VJ", "pf", AF.Exp, scale=-math.log(2.0), bias=60.0 * math.log(2.0))
-    ts(("z16", 0, 1), ("z16", 0, 1), 2.5, OP.mult)
-    ts("THR", "THR", ("z16", 0, 1), OP.max)
+    act(("pw", 0, 1), P64, AF.Exp, scale=-math.log(2.0), bias=60.0 * math.log(2.0))
+    act(("pw", 1, 2), P64, AF.Exp, scale=-math.log(2.0), bias=-4.0 * math.log(2.0))
+    tt(PH, P, P64, OP.subtract)
+    tt(PG64, P64, PM, OP.subtract)
+    for h in range(2):
+        ts(("VJ", 32 * h, 32 * h + 32), "he", PH, OP.is_equal, ("pw", h, h + 1), OP.mult)
+        ts(("THR", 64 * h, 64 * h + 64), ("mk", 0, 64), PM, OP.not_equal, 2.0 ** 97, OP.mult)
+        ts(("pw", h, h + 1), ("pw", h, h + 1), 2.5, OP.mult)
+        ts(("THR", 64 * h, 64 * h + 64), ("THR", 64 * h, 64 * h + 64), ("pw", h, h + 1), OP.max)
+        ts((SP0, SP1)[h], P64, 2.0, OP.mult, 2048.0 + 128 * h, OP.add)
+        ts(("RQ", 4 * h, 4 * h + 4), ("il0", 0, 4), PG64, OP.is_equal, (SP0, SP1)[h], OP.mult)
+    lin("s", xw, "xb")
 
     def slm(m):
         return 16 - m, 144 - m
 
-    def listing(out, tab, rhs, wid, more=None):
-        xs = [(out, (tab,) + slm(m), (rhs, m, wid, 16), m == 0, more is None and m == 15) for m in range(16)]
-        if more is not None:
-            xs.append((out, more[0], more[1], False, True))
-        mms(xs)
+    def listing(out, tab, rhs, *more):
+        msum(out, *([((tab,) + slm(m), (rhs[0], rhs[1] + m, rhs[2], 16)) for m in range(16)] + list(more)))
 
-    def send(t, src, dst_buf, sem):
+    def send(t, src, dst, sem):
         to = T.cores[(rank + 1 + t % (N - 1)) % N]
         rid, pid = topo.addr(to)[:2]
         mask = sum(1 << e for e in topo.engines(core, to)[:NENG])
-        i = add("g", [src], [], [lambda e: e.remote_dma(T[dst_buf][:], T[src][:], T.sem[sem], T.sem.sent, pid, rid, mask)], 0.3,
-                sem="sent", inc=NENG)
-        add("n", [], [dst_buf], [], 0.0, sem=sem, inc=NENG, lat=FLIGHT, after=i)
+        (a, ra), (b, rb) = cols(src), cols(dst)
+        i = add("g", [ra], [], [lambda e: e.remote_dma(b, a, T.sem[sem], T.sem.sent, pid, rid, mask)], 0.3, sem="sent", inc=NENG)
+        add("n", [], [rb], [], 0.0, sem=sem, inc=NENG, lat=COST["flight"], after=i)
+
+    def sub(x, n, h):
+        if isinstance(x, str):
+            x = (x, 0)
+        return (x[0], x[1] + n * h, x[1] + n * h + n)
 
     def hf(x, h):
-        if isinstance(x, str):
-            x = (x, 0, 128)
-        return (x[0], x[1] + 64 * h, x[1] + 64 * h + 64)
+        return sub(x, 64, h)
 
-    def ablist(q, o):
-        st, en = PIECES[q]
+    def hl(x, h):
+        return sub(x, 4, h)
+
+    def ablist(st, en, o):
         a = 128 * (st // 64) + 64 * o + st % 64
         return ("ABT", a, a + en - st)
 
-    def piece(x, q):
-        return (x, 16 * PIECES[q][0], 16 * PIECES[q][1])
-
-    def grp(x, q):
-        return (x, 128 * q, 128 * q + 128)
-
-    def rowbank(q):
-        return ("b%d" % (5 + q // 4), 128 * (q % 4), 128 * (q % 4) + 128)
-
-    E, CP, COL = ("b2", 0, 128), ("b2", 128, 256), ("b2", 264, 272)
-    C2, OO, CNT, SO = ("b0", 256, 264), ("b1", 256, 272), ("b3", 256, 384), ("b3", 384, 392)
-    c1x, u1, u0, X1P = ("b4", 256, 264), ("b4", 264, 272), ("b4", 272, 280), ("b4", 280, 408)
-    XD, XS, X256, XBA = [grp("b7", j) for j in range(4)]
-    FI, SE = grp("FS", 0), grp("FS", 1)
-    F1, X1, U0 = grp("F1X", 0), grp("F1X", 1), grp("F1X", 2)
+    LG = ("b2", 256, 288)
+    c1n, OO = ("b2", 268, 276), ("b7", 384, 400)
+    XD, XS, RP = [sub("b7", 128, j) for j in range(3)]
+    FI, SE = sub("FS", 128, 0), sub("FS", 128, 1)
+    U0, G12, X1N, F1N = [(sub("GF", 64, j), sub("GF", 64, 7 - j)) for j in range(4)]
+    LU0, LG12, LX1 = [(sub(LG, 4, j), sub(LG, 4, 7 - j)) for j in range(3)]
+    COL = (("b5", 256, 260), ("b6", 256, 260))
 
     for t in range(RO):
         last = t == RO - 1
-        gat("Cu", SW, "su")
+        mN, rN, mX, rX = "mN%d" % t, "rN%d" % t, "mX%d" % t, "rX%d" % t
+        done = {}
+
+        def named(name, fn, *args):
+            if name in C["after"]:
+                hint.append(done[C["after"][name]])
+            fn(*args)
+            done[name] = count()
+
         for h in range(2):
-            w = 64 // GS[h]
-            for j in range(GS[h]):
-                gat(("G%d" % h, 16 * w * j, 16 * w * (j + 1)), SW, ("Cu", 64 * h + w * j, 64 * h + w * (j + 1)))
-            for tab, bk, o in (("DB", "b%d" % (5 + h), 64), ("DA", "b%d" % h, 0)):
-                mms([((bk, 0, 64), grp(tab, k), ("G%d" % h, k, 1024, 16), k == 0, k == 15) for k in range(16)])
-                cp(("ABT", 128 * h + o, 128 * h + o + 64), (bk, 0, 64))
-        ts("C16", "Cu", 1, OP.add)
-        act("SL", "TB", AF.Copy, off="su")
-        mms([(CP, "I16", "C16", True, True)])
-        xs = [(E, "I32", "C16", True, False), (E, "IB", "SL", False, not t)]
-        if t:
-            xs.append((E, "ONB", "FCB", False, True))
-        mms(xs)
-        for q in range(len(PIECES)):
-            if q in VB:
-                gat(piece("XB", q), XW, ablist(q, 1))
+            gat(C["cu"][h], hf("Cu", h), SW, hl("su", h))
+            for j, (q, a, b) in enumerate(C["g"][h]):
+                named("g%d%d" % (h, j), gat, q, ("G%d" % h, 16 * a, 16 * b), SW, ("Cu", 64 * h + a, 64 * h + b))
+            if h:
+                sca(SD, hl("sou", 0), hf("Sn", 0))
+            for o, tab, bk in ((1, "DB", "b%d" % (5 + h)), (0, "DA", "b%d" % h)):
+                msum((bk, 0, 64), *[(sub(tab, 128, k), ("G%d" % h, k, 1024, 16)) for k in range(16)])
+                lin(C["ab"][2 * h + 1 - o], ablist(64 * h, 64 * h + 64, o), (bk, 0, 64))
+            EN, EM = ("b%d" % (3 + h), 384, 448), ("b%d" % (3 + h), 448, 512)
+            lin(C["c16"][h], hf("C16", h), hf("Cu", h))
+            gat(C["sl"][h], hf("SL", h), "TB", hl("su", h))
+            en = [("NI32", hf("C16", h)), ("IB", hf("SL", h))] + ([("ONB", "FCB")] if t else [])
+            msum(EN, *en)
+            lin(C["qe"][h], hf("qe", h), EN, 1.0 / 512, 1280.0 - 15.0 / 32)
+            msum(EM, *(en + [("N512", "K12"), ("N512", hf("qe", h))]))
+            lin(C["n1"][h], hl("n1", h), hl("si", h), 5.0, -16.0)
+            for j, (q, st, end) in enumerate(C["x"][h]):
+                st, end = st + 64 * h, end + 64 * h
+                xb_, d_, z_ = [(x, 16 * st, 16 * end) for x in ("XB", "ZB", "Z")]
+                named("b%d%d" % (h, j), gat, q, xb_, XW, ablist(st, end, 1))
+                named("d%d%d" % (h, j), gsub, d_, XW, ablist(st, end, 0), xb_)
+                if C["size"][h] == "s":
+                    named("z%d%d" % (h, j), act, z_, d_, AF.Abs)
+                else:
+                    named("z%d%d" % (h, j), ts, z_, d_, 0.0, OP.max, 2.0, OP.mult)
+            A, V = "b%d" % h, "b%d" % (3 + h)
+            U = (A, 128, 192)
+            XP, CNT, SO = (V, 192, 256), (V, 256, 320), (V, 320, 324)
+            cl = hf("cl", h)
+            tabs = [("WN", "ZB"), ("WP", "Z")] if C["size"][h] == "v" else [("WP", "Z")]
+            msum(U, *[((w,) + slm(k), (z, 1024 * h + k, 1024 * h + 1024, 16)) for w, z in tabs for k in range(16)])
+            lin(C["q"][h], hf("ui", h), U, 1.0, 16.0)
+            ts(hf("uk", h), hf("ui", h), 2047, OP.bitwise_and)
+            if C["sq"][h] == "s":
+                act(hf("sq", h), hf("uk", h), AF.Square)
             else:
-                act(piece("XB", q), XW, AF.Copy, off=ablist(q, 1))
-            gsub(piece("DD", q), XW, ablist(q, 0), piece("XB", q))
-            act(piece("ZX", q), piece("DD", q), AF.Abs)
-        for h in range(2):
-            U, Q, R = ("b%d" % h, 128, 192), ("b%d" % (3 + h), 0, 64), ("b%d" % (3 + h), 64, 128)
-            mms([(U, ("WT",) + slm(k), ("ZX", 1024 * h + k, 1024 * h + 1024, 16), k == 0, k == 15) for k in range(16)])
-            ts(hf("ui", h), U, 16, OP.add)
-            ts(hf("w2", h), hf("ui", h), 255, OP.bitwise_and)
-            tt(hf("sq", h), hf("w2", h), hf("w2", h), OP.mult)
-            tt(hf("y", h), hf("sq", h), hf(E, h), OP.add)
-            ts(hf("yy", h), hf("y", h), 480, OP.bitwise_and)
-            ts(hf("cl", h), hf("yy", h), 0, OP.is_equal)
-            mms([(Q, "TQ", hf("cl", h), True, True)])
-            mms([(R, "RC", hf("cl", h), True, False), (R, "I16", hf("C16", h), False, True)])
-            ts(hf(SE, h), Q, 33.0, OP.is_equal)
-            tt(hf("F2", h), hf(SE, h), hf(CP, h), OP.mult)
-            ts(hf(FI, h), Q, 32.0, OP.is_equal)
-            ts(hf(F1, h), R, 6143.0, OP.add, 0.0, OP.min)
-        ts("uk", "ui", 2047, OP.bitwise_and)
-        ts(U0, "uk", K0, OP.mult)
-        for h in range(2):
-            FP = ("b%d" % (3 + h), 128, 192)
-            mms([(FP, "I16", hf(FI, h), True, True)])
-            tt(hf(X1, h), FP, hf("uk", h), OP.mult)
-        listing(C2, "L1", "F2", 128)
-        ts("mN%d" % t, C2, 4097.0, OP.mult, -1.0, OP.add)
-        send(t, "mN%d" % t, "rN%d" % t, "aN%d" % t)
+                tt(hf("sq", h), hf("uk", h), hf("uk", h), OP.mult)
+            lin(C["v16"][h], hf("V16", h), hf("uk", h))
+            lin(C["u0"][h], U0[h], hf("uk", h), K0)
+            ts(hf("yy", h), hf("sq", h), 480, OP.bitwise_and)
+            named("cl%d" % h, tt, cl, hf("yy", h), (V, 448, 512), OP.is_equal)
+            made = {}
+
+            def tab(name, q):
+                if (name, q) not in made:
+                    j = {"Q": 0, "R": 2 - h, "RU": 1 + h}[name]
+                    made[(name, q)] = (A, 192 + 64 * j, 256 + 64 * j) if q == "s" else (V, 64 * j, 64 * j + 64)
+                    less = {"Q": [], "R": [("NI16", hf("C16", h))], "RU": [("NI16", hf("V16", h))]}[name]
+                    msum(made[(name, q)], *(less + [("MK", cl)]))
+                return made[(name, q)]
+
+            qf, qx, qi = C["f1"][h], C["x1n"][h], C["fi"][h]
+            for name, q in (("R", qf), ("R", "v"), ("RU", qx), ("Q", "v"), ("Q", qi)):
+                tab(name, q)
+            if qf == qx and C["join"][h] == "y":
+                a, o = min(tab("R", qf), tab("RU", qf)), min(F1N[h], X1N[h])
+                pos(qf, (o[0], o[1], o[1] + 128), (a[0], a[1], a[1] + 128), -2048.0)
+            else:
+                pos(qf, F1N[h], tab("R", qf), -2048.0)
+                pos(qx, X1N[h], tab("RU", qx), -2048.0)
+            named("f%d" % h, ts, G12[h], tab("R", "v"), 0.0, OP.max, 2048.0, OP.min)
+            ts(hf(SE, h), tab("Q", "v"), 2048.0, OP.is_equal)
+            pos(qi, hf(FI, h), tab("Q", qi), -4095.0)
+            rows = "b%d" % (5 + h)
+            mms([(part(COL[h], 64 * e, 64 * e + 64), F1N[h], ("GI", e, 8, 2), True, True) for e in range(2)])
+            mms([(sub(rows, 64, j), sub("SEL", 128, j), F1N[h], True, True) for j in range(4)])
+            listing(sub(LG, 16, h), "L1", sub("GF", 256, h))
+            lin(C["mn"][h], hl(mN, h), LG12[h], 4095.0, -2048.0 * 4095)
+            send(t, hl(mN, h), hl(rN, h), "aN%d%d" % (t, h))
+            lin(C["c1u"][h], hl("c1u", h), hl(c1n, h), -1.0, 2048.0)
+            tt(hl("n2", h), hl("n1", h), LU0[h], OP.add)
+            lin(C["x1"][h], hl("x1", h), LX1[h], -1.0)
+            if h:
+                ts("h1", c1n, 0.0, OP.is_gt, 2.0 ** 23 + 2048, OP.mult)
+                tt("h2", "h1", c1n, OP.subtract)
+                ts("n3", "n2", 2047, OP.bitwise_and)
+                tt("sb", "h2", "n3", OP.max)
+            for lo in range(h + 1):
+                for j in range(4):
+                    named("e%d" % h, ts, sub("EQ", 64, 4 * (h + lo) + j), sub(rows, 64, j), sub(COL[lo], 1, j), OP.is_equal)
+            msum(XP, ("I16", X1N[h]), ("I6", hf(FI, h)))
+            for j in range(4):
+                out = part(sub(CNT, 32, j % 2), 64 * (j // 2), 64 * (j // 2) + 64)
+                msum(out, *[(sub("EQ", 64, 4 * (h + lo) + j), sub("VJ", 32, lo)) for lo in range(h + 1)])
+            gat(C["sc"][h], hf("Sc", h), SD, hl("c1u", h))
+            named("l%d" % h, tt, hf("lt", h), CNT, hf("THR", h), OP.is_gt)
+            tt(hf("Sd", h), hf("Sc", h), XP, OP.subtract)
+            mms([(part(SO, 64 * e, 64 * e + 64), part(hf("lt", h), 64 * e, 64 * e + 64), part(hl("RQ", h), 64 * e, 64 * e + 64), True, True)
+                 for e in range(2)])
+            ts(hf("Sn", h), hf("Sd", h), 2047, OP.bitwise_and)
+            named("s%d" % h, tt, hl("sou", h), SO, hl("c1u", h), OP.max)
+        sca(SD, hl("sou", 1), hf("Sn", 1))
         if not last:
-            act("sg", C2, AF.Sign, accum_out=("fc", 0, 1))
-            act("FCB", "IB", AF.Identity, scale=0.0, bias=("fc", 0, 1))
-        mms([(COL, F1, "GI", True, True)])
-        act("cola", COL, AF.Copy, scale=-1.0)
-        act("col", COL, AF.Copy)
-        for q in range(8):
-            mms([(rowbank(q), grp("SEL", q), F1, True, True)])
-        for q in range(8):
-            if q < 8 - SQ:
-                ts(grp("EQ", q), rowbank(q), ("col", q, q + 1), OP.is_equal)
-            else:
-                act(grp("EN", q), rowbank(q), AF.Abs, bias=("cola", q, q + 1))
-        act(("EQ", 1024 - 128 * SQ, 1024), ("EN", 1024 - 128 * SQ, 1024), AF.Relu, scale=-1.0, bias=1.0)
+            act("sg", mN, AF.Sign, bias=-0.5, accum_out=("fc", 0, 1))
+            act("FCB", ("IB", 0, 64), AF.Identity, scale=0.0, bias=("fc", 0, 1))
         for h in range(2):
-            mms([((CNT[0], CNT[1] + 16 * q, CNT[1] + 16 * q + 16), grp("EQ", q), "VJ", True, True) for q in range(4 * h, 4 * h + 4)])
-        listing(("b4", 256, 280), "L1", "F1X", 384)
-        ts("c1u", c1x, 2048.0, OP.add)
-        cp("c1h", c1x)
-        gat("Sc", SD, "c1u")
-        tt("lt", CNT, "THR", OP.is_gt)
-        mms([(SO, "lt", "RQ", True, False), (SO, "I16", "c1h", False, True)])
-        mms([(X1P, "I16", X1, True, False), (X1P, "N16", FI, False, True)])
-        tt("Sd", "Sc", X1P, OP.add)
-        ts("Sn", "Sd", 2047, OP.bitwise_and)
-        tt("so", SO, "IL", OP.min)
-        ts("sou", "so", 2048.0, OP.add)
-        sca(SD, "sou", "Sn")
-        ts("n1", "si", 5, OP.mult, -16, OP.add)
-        ts("h1", c1x, 0.0, OP.is_lt, 16777216.0, OP.mult)
-        tt("h2", "h1", c1x, OP.add)
-        tt("n2", "n1", u0, OP.add)
-        ts("n3", "n2", 2047, OP.bitwise_and)
-        tt("sb", "h2", "n3", OP.max)
-        cp("x1", u1)
-        listing(OO, "LK", "FS", 256, ("I16", "CT"))
-        cp("ou", OO)
-        act("z2", ZW, AF.Copy, off=("ou", 8, 16))
-        act("z1", ZW, AF.Copy, off=("ou", 0, 8))
-        mms([(XD, "BF2", SE, True, False), (XD, "IB", "xb", False, False), (XD, "NIB", "z2", False, True)])
-        act("mX%d" % t, XD, AF.Abs, bias=1024.0)
-        send(t, "mX%d" % t, "rX%d" % t, "aX%d" % t)
-        ts("x2", "x1", 15, OP.bitwise_and)
-        tt("x3", "x2", "XO", OP.add)
-        cp("xou", "x3")
-        sca(XW, "xou", "z1")
-        mms([(XS, "BF1", FI, True, False), (XS, "IB", "xb", False, False), (XS, "IB", "z1", False, True)])
-        act(X256, "xb", AF.Identity, bias=256.0)
-        ts("xv", XS, 0.5, OP.mult, 2047.75, OP.add)
-        tt(XBA, "xv", X256, OP.min)
+            tt(hl("se", h), hl("sb", h), hl(rN, h), OP.max)
+            ts(hl("si", h), hl("se", h), 2047, OP.bitwise_and)
+            if not last:
+                lin(C["su"][h], hl("su", h), hl("si", h))
         if last:
-            dma("y", "oV", [XW], [], T.yv[:], T.ZX[:, 2048:4096], 2 * LOCAL)
-            acc = ("b5", 0, 256)
-            tt(acc, ("S", 0, 256), ("S", 256, 512), OP.add)
-            for q in range(2, 8):
-                tt(acc if q < 7 else "yto", acc, ("S", 256 * q, 256 * q + 256), OP.add)
-            dma("y", "oT", ["yto"], [], T.yt[:], T.yto[:], LOCAL)
-        tt("se", "sb", "rN%d" % t, OP.max)
-        ts("si", "se", 2047, OP.bitwise_and)
-        cp("sf" if last else "su", "si")
-        if last:
+            cp("sf", "si")
             dma("s", "oS", ["sf"], [], T.ys[:], T.sf[:], LOCAL)
-        tt("xm", XBA, "rX%d" % t, OP.min)
+        listing(OO, "LK", ("FS", 0, 256), ("I16", "CT"))
+        lin(C["ou"], "ou", OO)
+        act("z2", DW, AF.Abs, off=("ou", 8, 16))
+        act("z1", DW, AF.Abs, off=("ou", 0, 8))
+        msum(XD, ("BF2", SE), ("IB", xw), ("NIB", "z2"))
+        act(mX, XD, AF.Abs, bias=1024.0)
+        send(t, mX, rX, "aX%d" % t)
+        msum(XS, ("BF1", FI), ("BFH", FI), ("IB", xw), ("IB", "z1"))
+        lin("s", "hv", XS, 0.5, 256.0)
+        ts("x2", "x1", 2048 + 15, OP.bitwise_and)
+        tt("xou", "x2", "XO", OP.add)
+        sca(WX, "xou", "z1")
+        if last:
+            dma("y", "oV", [XW], [], T.yv[:], T.ZB[:, 4096:6144], 2 * LOCAL)
+            n = C["yts"]
+            acc, rest = ("b5", 0, 256), ("b6", 0, 256)
+            for q in range(n):
+                lin("s", sub("SH", 256, q), sub("S", 256, 8 - n + q))
+            msum(rest, *[("I16", sub("SH", 256, q)) for q in range(n)])
+            tt(acc, ("S", 0, 256), ("S", 256, 512), OP.add)
+            for q in range(2, 8 - n):
+                tt(acc if q < 7 - n else "yta", acc, sub("S", 256, q), OP.add)
+            tt("yto", "yta", rest, OP.add)
+            dma("y", "oT", ["yto"], [], T.yt[:], T.yto[:], LOCAL)
+        msum(RP, ("IB", rX))
+        tt("xm", "hv", RP, OP.min)
         ts("xn", "xm", 255, OP.bitwise_and)
-        cp("xb", "xn")
+        lin("s", "xb" if last else xw, "xn")
     dma("y", "oX", ["xb"], [], T.yx[:], T.xb[:], LOCAL)
     return emit()

@@ -4,12 +4,13 @@ from concourse.mybir import AluOpType as OP, ActivationFunctionType as AF
 N, RO = 8, 3
 NENG = 8
 CFG = {
-    "g": ((("v", 0, 32), ("s", 32, 64)), (("v", 0, 32), ("s", 32, 64))),
-    "x": ((("s", 0, 16), ("s", 16, 40), ("s", 40, 64)), (("s", 0, 32), ("s", 32, 48), ("s", 48, 64))),
-    "after": {},
-    "size": "vs",
-    "cu": "vv", "ab": "svsv", "c16": "vv", "sl": "ss", "qe": "ss", "q": "vv", "sq": "vv", "v16": "vv", "join": "yy", "u0": "ss", "fi": "ss", "f1": "vv", "x1n": "vv", "mn": "vv", "c1u": "vv",
-    "sc": "ss", "su": "vv", "n1": "ss", "x1": "ss", "ou": "s", "db": "v", "yts": 4,
+    "g": ((("v", 0, 16), ("v", 16, 32), ("s", 32, 64)), (("v", 0, 32), ("s", 32, 64))),
+    "x": ((("s", 0, 16), ("v", 16, 32), ("s", 32, 48), ("s", 48, 64)), (("s", 0, 16), ("s", 16, 32), ("s", 32, 48), ("s", 48, 64))),
+    "after": {}, "push": (0.0, 0.0, 0.0, 0.0),
+    "xb": "vv", "size": ("svvv", "ssss"),
+    "cu": "vs", "pick": (((0, 64, "sv"),), ((0, 64, "sv"),)), "c16": "vv", "sl": "ss", "qe": "ss", "q": "ss", "v16": "vv", "join": "yy", "u0": "ss", "fi": "vv", "f1": "vv", "x1n": "vv", "c1u": "vv",
+    "su": "ss", "n1": "ss", "x1": "vv", "ou": "s", "db": 8, "c1h": "vv", "merge": 2,
+    "yt": (("s", 0, 2), ("v", 5, 7), ("s", 2, 4), ("v", 7, 8), ("s", 4, 5)), "yo": "s",
 }
 
 F32, F16, BF, I4, U2 = "float32", "float16", "bfloat16", "int32", "uint16"
@@ -22,30 +23,51 @@ def _sb(dtype, **bufs):
 
 
 _sb(I4, S=2304, si=8, wi=1)
-_sb(BF, ZB=6144, Z=2048, XB=2048, xb=128)
+_sb(BF, ZB=6144, Z=4096, XB=2048, xb=128)
 _sb(U2, su=8)
 _sb(I4, cp=1, cq=4)
-_sb(F32, cI=144, cf=24, blk=128, mk=64, l256=16, rm=16, ex=16, THR=128, XO=8, il0=8, pf=16, he=32, pw=2)
-_sb(F16, I16=128, P16=128, NI16=128, NI32=128, I6=128, N512=128, K12=64, L1=144, LK=144, DA=2048, DB=2048, BO=128, LT=128, MK=128,
-    SEL=512, BF1=128, BFH=128, BF2=128, RQ=8, GI=8, CT=16)
-_sb(BF, TB=2048, SL=128, FCB=64, ONB=128, IB=128, NIB=128, WN=144, WP=144, VJ=64, hs=512)
+_sb(F32, cI=144, cf=16, blk=128, l256=16, rm=16, ex=16, XO=8, SP=8, il0=8, pf=16)
+_sb(F16, I16=128, P16=128, NI16=128, NI32=128, N512=128, K12=68, L1=144, LK=144, L7=144, DA=2048, DB=2048, BO=128, LT=128, MK=128,
+    SEL=1024, TRI=512, BF1=128, BFH=128, BF2=128, GI=8, CT=16)
+_sb(BF, TB=2048, SL=128, FCB=64, ONB=128, IB=128, NIB=128, WN=144, WP=144, K4=2, ZO=128, hs=1024, c64=512)
 _sb(U2, Cu=128, ABT=256, ou=16, c1u=8, sou=8, xou=8)
-_sb(F16, C16=128, G0=1024, G1=1024, cl=128, FS=256, GF=512, lt=128, V16=128, qe=128, hv=128, SH=1024)
-_sb(BF, EQ=768, z1=128, z2=128, sg=8)
+_sb(F16, C16=128, G0=1024, G1=1024, cl=128, FS=256, GF=384, c1h=8, V16=128, qe=128, hv=128, SH=2048)
+_sb(BF, z1=128, z2=128, sg=128)
 _sb(I4, ui=128, uk=128, sq=128, yy=128, Sc=128, Sd=128, Sn=128, x1=8, x2=8, n2=8, n3=8, se=8, xm=128, xn=128)
-_sb(F32, n1=8, h1=8, h2=8, sb=8, fc=1, sf=8, yta=256, yto=256)
+_sb(F32, n1=8, h1=8, h2=8, sb=8, fc=1, sf=8, yto=256)
 SEMAPHORES = ["qv", "qs", "qp", "qg", "dS0", "dX", "dx0", "dw", "ds0", "oV", "oT", "oX", "oS", "sent"]
+for _h in range(2):
+    SCRATCH["EQ%d" % _h] = ("sbuf", [128, 4, 128], BF)
 for _t in range(RO):
-    _sb(F32, **{"mN%d" % _t: 8, "rN%d" % _t: 8})
-    _sb(BF, **{"mX%d" % _t: 128, "rX%d" % _t: 128})
-    SEMAPHORES += ["aN%d0" % _t, "aN%d1" % _t, "aX%d" % _t]
+    _sb(F16, mN=128 * RO, rN=128 * RO)
+    _sb(BF, mX=128 * RO, rX=128 * RO)
+    SEMAPHORES += ["aN%d0" % _t, "aN%d1" % _t, "aX%d0" % _t, "aX%d1" % _t]
 PSUM = ["b%d" % _b for _b in range(8)]
 for _b in PSUM:
     SCRATCH[_b] = ("psum", [128, 512], F32)
 
-COST = {"cyc": 0.00086, "pe": 0.00045, "gath": 1.35, "scat": 3.8, "wake": 0.23, "own": 0.23, "local": 2.0, "flight": 2.4, "S": 4.3, "X": 6.0, "act": 50,
-        "look": 0.1, "idle": 3.0, "tries": 40, "jit": 0.3, "chunk": 4, "swaps": 8000, "far": 4, "heat": 0.03}
+COST = {"cyc": 0.00086, "pe": 0.00045, "gath": 1.35, "scat": 3.8, "wake": 0.23, "own": 0.23, "local": 2.0, "flight": 2.1, "S": 3.2, "X": 4.9, "act": 50,
+        "look": 0.05, "idle": 3.0, "tries": 30, "jit": 0.3, "chunk": 4, "long": 0.4, "seed": 12345, "swaps": 20000, "shifts": 0, "shift": 1.5, "warm": 0.1, "far": 4, "drift": 1, "heat": 0.05}
 PLAN = {}
+_E0, _E1 = [" ".join("EQ%d:%d" % (_h, 16 * _j) for _j in range(8)) for _h in range(2)]
+_V = ("Cu:0 G0:0 <se:4 G0:256 <si:4 <ZB:2048 G1:0 ABT:0 "
+      "XB:256 ZB:256 ZB:0 Z:256 ZB:512 ABT:128 ZB:768 Z:512 ZB:1024 Z:768 ZB:1280 ZB:1536 ZB:1792 "
+      "uk:0 V16:0 yy:0 cl:0 uk:64 mN:0 GF:64 FS:64 FS:0 V16:64 <xm:0 yy:64 <xn:0 cl:64 " + _E0 + " h1:0 c1h:0 GF:192 mN:64 ")
+_R = " c1u:4 c1h:4 Sn:0 sou:0 Sd:64 S:0a Sn:64 sou:4 "
+_S0 = "G0:512 <mX:0 SL:0 <su:4 Cu:64 ABT:64 G1:512 "
+_S = ("XB:0 XB:512 XB:768 ABT:192 qe:0 XB:1024 Z:0 XB:1280 XB:1536 XB:1792 qe:64 Z:1024 Z:1280 ui:0 Z:1536 Z:1792 "
+      "sq:0 GF:0 ui:64 sq:64 <xb:0 <ZB:2048 GF:320 ")
+_P = ("b5:0 b0:0 b6:0 b1:0 b5:0t b6:0t b0:144d b0:128 b4:448 b1:128 b3:128 <b7:256 b5:0r b0:384 b5:256r b2:0 b4:64 b3:400 "
+      "b6:0r b1:384 b6:256r ")
+TURN = {
+    "v": _V + "c1u:0 x1:0 h2:0 n2:0 FS:128 FS:192 Sd:0 " + _E1 + _R + "se:0 S:0 si:0",
+    "v2": _V + "FS:128 FS:192 c1u:0 x1:0 h2:0 n2:0 Sd:0 " + _E1 + " z2:64" + _R + "S:0 ZB:2048 SH:1280 SH:1792 se:0 xm:0",
+    "s": _S0 + _S + "z1:0 z1:64 z2:0",
+    "s0": "Cu:64 G0:512 G1:512 ABT:64 " + _S + "z1:0 z1:64 z2:0",
+    "s2": _S0 + _S + "ou:0 z2:0 z1:0 ou:8 mX:0 z1:64 mX:64 hv:0 SH:0",
+    "p": _P + "b2:16 b0:400 b0:403 b1:400 b1:403 b3:300 b7:400",
+    "p2": _P + "b7:408 b3:136 b2:16 b0:400 b0:403 b1:400 b1:403 b7:0 b7:64 b3:300 b4:300",
+}
 
 
 def make_plan(g, T):
@@ -54,6 +76,7 @@ def make_plan(g, T):
     nodes = []
     hist = {}
     hint = []
+    push = [0.0, -1, "", None]
     WAKE = COST["wake"]
 
     def rng(x):
@@ -79,7 +102,7 @@ def make_plan(g, T):
             pred[after] = False
         while hint:
             pred.setdefault(hint.pop(), False)
-        nodes.append({"q": q, "fns": fns, "dur": dur, "sem": sem, "inc": inc, "lat": lat, "pred": pred, "i": i})
+        nodes.append({"q": q, "wr": wr, "push": push[0], "step": push[1], "tag": push[2], "name": push[3], "fns": fns, "dur": dur, "sem": sem, "inc": inc, "lat": lat, "pred": pred, "i": i})
         for name, a, b in wr:
             keep = [h for h in hist.get(name, []) if not (a <= h[0] and h[1] <= b and h[3] in pred)]
             hist[name] = keep + [(a, b, True, i)]
@@ -89,6 +112,17 @@ def make_plan(g, T):
 
     def order():
         n = len(nodes)
+        by = {}
+        for x in nodes:
+            if x["wr"]:
+                by.setdefault((x["step"], x["q"], x["name"] or "%s:%d" % x["wr"][0][:2] + x["tag"]), []).append(x["i"])
+        for q in "vsp":
+            for t in range(RO):
+                ids = [by.get((t - 1, q, w[1:]) if w[0] == "<" else (t, q, w)) for w in TURN.get(q + str(t), TURN.get(q, "")).split()]
+                ids = [x for x in ids if x]
+                for a, b in zip(ids, ids[1:]):
+                    nodes[b[0]]["pred"].setdefault(a[-1], False)
+        top, left = [], [len(x["pred"]) for x in nodes]
         qs = [x["q"] for x in nodes]
         dur = [x["dur"] for x in nodes]
         succ = [[] for _ in nodes]
@@ -98,6 +132,14 @@ def make_plan(g, T):
                 gap = nodes[j]["lat"] + (COST["own"] if qs[j] == x["q"] else WAKE) if w else 0.0
                 succ[j].append((x["i"], gap))
                 pred[x["i"]].append((j, gap))
+        top = [i for i in range(n) if not left[i]]
+        for i in top:
+            for j, gap in succ[i]:
+                left[j] -= 1
+                if not left[j]:
+                    top.append(j)
+        assert len(top) == n
+        top.reverse()
 
         def run(prio, first, then, tail):
             left = [len(x) for x in first]
@@ -135,19 +177,43 @@ def make_plan(g, T):
 
         lat = [x["lat"] for x in nodes]
         prio = [0.0] * n
-        for i in range(n - 1, -1, -1):
+        for i in top:
             prio[i] = max([prio[j] + gap for j, gap in succ[i]] + [lat[i]]) + dur[i]
-        best, seed, base = None, 12345, prio
+        best, seed, base = None, COST["seed"], prio
+        PLAN["dag"] = (max(prio), prio, succ, nodes)
+        prio = [prio[i] + nodes[i]["push"] for i in range(n)]
         for it in range(COST["tries"]):
             out, ends = run(prio, pred, succ, [0.0] * n)
             span = max(ends[i] + lat[i] for i in range(n))
             if best is None or span < best[0]:
-                best, base = (span, out), ends
+                best, base, good = (span, out), ends, prio
             jit = []
             for i in range(n):
                 seed = (seed * 1103515245 + 12345) % 2147483648
                 jit.append(base[i] + lat[i] + COST["jit"] * (seed / 2147483648.0 - 0.5))
-            prio = run(jit, succ, pred, lat)[1]
+            prio = run([jit[i] - nodes[i]["push"] for i in range(n)], succ, pred, lat)[1]
+            prio = [prio[i] + nodes[i]["push"] for i in range(n)]
+        same = {}
+        for x in nodes:
+            same.setdefault((x["q"], tuple(x["wr"][:1])), []).append(x["i"])
+        same = [x for x in same.values() if len(x) > 1]
+        span, good = 1e9, list(dur)
+        for it in range(COST["shifts"]):
+            more = list(good)
+            for step in range(1 + it % 2):
+                seed = (seed * 1103515245 + 12345) % 2147483648
+                for i in same[(seed >> 12) % len(same)]:
+                    more[i] += COST["shift"] * ((seed >> 4) % 256 / 128.0 - 1.0)
+            for i in top:
+                prio[i] = max([prio[j] + gap for j, gap in succ[i]] + [lat[i]]) + more[i]
+            out, ends = run(prio, pred, succ, [0.0] * n)
+            new = max(ends[i] + lat[i] for i in range(n))
+            seed = (seed * 1103515245 + 12345) % 2147483648
+            if new <= span - COST["warm"] * (1 - it / COST["shifts"]) * math.log((seed + 1) / 2147483648.0):
+                span, good = new, more
+                if span < best[0]:
+                    best = (span, out)
+        PLAN["mid"] = best[0]
         seq = list(best[1])
         pos, before, behind, last = [0] * n, [-1] * n, [-1] * n, {}
         for k, i in enumerate(seq):
@@ -188,7 +254,7 @@ def make_plan(g, T):
 
         ends = [0.0] * n
         span = times(ends, 0)
-        best = (span, list(seq))
+        best = (span, list(seq), ends)
         for it in range(COST["swaps"]):
             i, arcs = max(sinks, key=lambda k: ends[k] + lat[k]), []
             while i >= 0:
@@ -203,15 +269,21 @@ def make_plan(g, T):
             if not arcs:
                 break
             seed = (seed * 1103515245 + 12345) % 2147483648
-            v = arcs[(seed >> 8) % len(arcs)][1]
+            u, v = arcs[(seed >> 8) % len(arcs)]
             seed = (seed * 1103515245 + 12345) % 2147483648
+            kind = (seed >> 16) % 10
+            if kind < COST["drift"]:
+                v = (seed >> 4) % n
             moved, a = [], n
             for step in range(1 + (seed >> 8) % COST["far"]):
-                u = before[v]
-                k = swap(u, v) if u >= 0 else None
+                if kind % 2:
+                    v = behind[u]
+                else:
+                    u = before[v]
+                k = swap(u, v) if u >= 0 and v >= 0 else None
                 if k is None:
                     break
-                moved.append(u)
+                moved.append((u, v))
                 a = min(a, k)
             if not moved:
                 continue
@@ -221,12 +293,12 @@ def make_plan(g, T):
             if new <= span - COST["heat"] * (1 - it / COST["swaps"]) * math.log((seed + 1) / 2147483648.0):
                 span, ends = new, trial
                 if span < best[0]:
-                    best = (span, list(seq))
+                    best = (span, list(seq), ends)
             else:
-                for u in reversed(moved):
+                for u, v in reversed(moved):
                     swap(v, u)
         PLAN["span"] = best[0]
-        return best[1]
+        return best[1:]
 
     def emit():
         count = {}
@@ -243,7 +315,8 @@ def make_plan(g, T):
                     clock[q][k] = max(clock[q].get(k, 0), m)
 
         if "seq" not in PLAN:
-            PLAN["seq"] = order()
+            PLAN["seq"], PLAN["ends"] = order()
+        ends, mine = PLAN["ends"], dict((q, []) for q in eng)
         for i in PLAN["seq"]:
             x = nodes[i]
             q = x["q"]
@@ -257,8 +330,14 @@ def make_plan(g, T):
                     src, n = where[j]
                     if n > clock[q].get(src, 0):
                         need[src] = max(need.get(src, 0), n)
+            if q in need:
+                for j in reversed(mine[q]):
+                    if ends[j] + COST["long"] <= ends[i] - x["dur"] or where[j][1] <= need[q]:
+                        need[q] = max(need[q], where[j][1])
+                        break
             wait(q, need)
             if x["sem"] is None:
+                mine[q].append(i)
                 for fn in x["fns"]:
                     fn(eng[q]).then_inc(T.sem[qsem[q]], 1)
                     count[q] = count.get(q, 0) + 1
@@ -280,14 +359,14 @@ def make_plan(g, T):
             if count[q] > clock["g"].get(q, 0):
                 wait("g", {q: count[q]})
         return nodes
-    return add, emit, hint, lambda: len(nodes) - 1
+    return add, emit, hint, push, lambda: len(nodes) - 1
 
 
 def rank_program(g, core, T, topo):
     rank = T.rank_of(core)
     if rank is None:
         return
-    add, emit, hint, count = make_plan(g, T)
+    add, emit, hint, push, count = make_plan(g, T)
     C = CFG
     CYC, GATH = COST["cyc"], COST["gath"]
 
@@ -295,6 +374,8 @@ def rank_program(g, core, T, topo):
         if isinstance(x, str):
             x = (x, 0, T[x].shape[1])
         name, a, b = x[:3]
+        if len(T[name].shape) == 3:
+            return (T[name][x[4]:x[5], :, a:b] if x[3] == "all" else T[name][x[4]:x[5], x[3], a:b]), (name, a, b)
         if len(x) == 6:
             return (T[name][x[4]:x[5], a:b:x[3]] if x[3] > 1 else T[name][x[4]:x[5], a:b]), (name, a, b)
         if len(x) == 4:
@@ -304,6 +385,8 @@ def rank_program(g, core, T, topo):
     def width(x):
         r = cols(x)[1]
         st = x[3] if len(x) >= 4 and not isinstance(x, str) else 1
+        if st == "all":
+            return 4 * (r[2] - r[1])
         return (r[2] - r[1] + st - 1) // st
 
     def buf(x):
@@ -430,20 +513,17 @@ def rank_program(g, core, T, topo):
     iota("cI", [[1, 144]], 0, 0)
     iota("ex", [[1, 16]], 0, 0)
     iota("blk", [[16, 8], [0, 16]], 0, 0)
-    iota("mk", [[0, 4], [1, 16]], 0, 0)
     iota("il0", [[16, 8]], 0, 0)
-    iota("l256", [[0, 2], [256, 8]], 0, 0)
-    iota("he", [[64, 2], [0, 16]], 0, 0)
-    iota("hs", [[32, 4], [16, 2], [0, 64]], 0, 0)
+    iota("l256", [[1024, 2], [0, 2], [256, 4]], 0, 0)
     iota("TB", [[0, 128], [32, 16]], 256, 0)
-    iota(("ZB", 2048, 4096), [[0, 2048]], 1024, 0)
+    iota("c64", [[0, 8], [1, 64]], 64, 0)
+    iota("hs", [[16, 8], [0, 128]], 0, 0)
     P = ("pf", 0, 1)
-    PX, PM, PG, P64, PH, PG16, KM, K0, WC, WM, CTC, XOC, PG64, SP0, SP1 = [("cf", j, j + 1) for j in range(15)]
+    PX, PM, PG, PG16, KM, K0, WC, WM, CTC, XOC = [("cf", j, j + 1) for j in range(10)]
     ts(("cq", 0, 1), "cp", 15, OP.bitwise_and)
     ts(("cq", 1, 2), "cp", 112, OP.bitwise_and)
-    ts(("cq", 2, 3), "cp", 63, OP.bitwise_and)
     ts(("cq", 3, 4), "cp", 1, OP.bitwise_and)
-    cp(("cf", 1, 4), ("cq", 0, 3))
+    cp(("cf", 1, 3), ("cq", 0, 2))
     ts(PX, ("cq", 3, 4), -2, OP.mult, 1, OP.add)
     tt(PX, PX, P, OP.add)
     ts("I16", ("cI", 0, 128), P, OP.is_equal)
@@ -451,16 +531,17 @@ def rank_program(g, core, T, topo):
     ts("rm", "ex", PM, OP.is_equal)
     for k in range(16):
         ts(("DA", 128 * k, 128 * k + 128), "I16", ("rm", k, k + 1), OP.mult)
-        lin(C["db"], ("DB", 128 * k, 128 * k + 128), "P16", ("rm", k ^ 1, (k ^ 1) + 1))
+        lin("s" if k < C["db"] else "v", ("DB", 128 * k, 128 * k + 128), "P16", ("rm", k ^ 1, (k ^ 1) + 1))
     for h in range(2):
         cp(("su", 4 * h, 4 * h + 4), ("si", 4 * h, 4 * h + 4))
     ts("BO", "blk", PG, OP.is_equal)
-    for name, v in (("NI16", -1.0), ("NI32", -32.0), ("I6", 16.0), ("N512", -512.0), ("IB", 1.0), ("NIB", -1.0), ("MK", 4096.0)):
+    for name, v in (("NI16", -1.0), ("NI32", -32.0), ("N512", -512.0), ("IB", 1.0), ("NIB", -1.0), ("MK", 4096.0)):
         lin("s", name, "I16", v)
     for name, v in (("BF1", -3072.0), ("BFH", -0.5), ("BF2", -1024.0)):
         lin("s", name, "BO", v)
-    fill("ONB", -16.0)
-    fill("K12", -1280.0)
+    fill("ONB", -32.0)
+    fill(("K12", 0, 64), -1280.0)
+    fill(("K12", 64, 68), 8188.0)
     ts(PG16, PG, 16.0, OP.add)
     cp(WC, "wi")
     ts(WM, "wi", -1.0, OP.mult)
@@ -475,29 +556,24 @@ def rank_program(g, core, T, topo):
     ts(XOC, PM, 16.0, OP.mult)
     ts("L1", "cI", PG16, OP.is_equal)
     ts("LK", "cI", PG16, OP.is_equal, KM, OP.mult)
+    lin("s", "L7", "L1", 2047.0)
     fill(("S", 2048, 2304), 0)
     ts("SEL", "hs", PG, OP.is_equal)
     ts("GI", "il0", PG, OP.is_equal)
     ts("CT", "l256", CTC, OP.add)
-    ts("XO", ("l256", 0, 8), XOC, OP.add)
-    act(("pw", 0, 1), P64, AF.Exp, scale=-math.log(2.0), bias=60.0 * math.log(2.0))
-    act(("pw", 1, 2), P64, AF.Exp, scale=-math.log(2.0), bias=-4.0 * math.log(2.0))
-    tt(PH, P, P64, OP.subtract)
-    tt(PG64, P64, PM, OP.subtract)
-    for h in range(2):
-        ts(("VJ", 32 * h, 32 * h + 32), "he", PH, OP.is_equal, ("pw", h, h + 1), OP.mult)
-        ts(("THR", 64 * h, 64 * h + 64), ("mk", 0, 64), PM, OP.not_equal, 2.0 ** 97, OP.mult)
-        ts(("pw", h, h + 1), ("pw", h, h + 1), 2.5, OP.mult)
-        ts(("THR", 64 * h, 64 * h + 64), ("THR", 64 * h, 64 * h + 64), ("pw", h, h + 1), OP.max)
-        ts((SP0, SP1)[h], P64, 2.0, OP.mult, 2048.0 + 128 * h, OP.add)
-        ts(("RQ", 4 * h, 4 * h + 4), ("il0", 0, 4), PG64, OP.is_equal, (SP0, SP1)[h], OP.mult)
+    ts("XO", ("l256", 4, 12), XOC, OP.add)
+    ts("TRI", "c64", P, OP.is_le, 4096.0, OP.mult)
+    lin("s", "SP", "XO", 1.0 / 16, 2048.0)
+    fill("K4", 4096.0)
+    fill("ZO", 0.0)
+    fill(("Z", 3072, 4096, 16), 1024.0)
     lin("s", xw, "xb")
 
     def slm(m):
         return 16 - m, 144 - m
 
     def listing(out, tab, rhs, *more):
-        msum(out, *([((tab,) + slm(m), (rhs[0], rhs[1] + m, rhs[2], 16)) for m in range(16)] + list(more)))
+        msum(out, *(list(more) + [((tab,) + slm(m), (rhs[0], rhs[1] + m, rhs[2], 16)) for m in range(16)]))
 
     def send(t, src, dst, sem):
         to = T.cores[(rank + 1 + t % (N - 1)) % N]
@@ -522,18 +598,17 @@ def rank_program(g, core, T, topo):
         a = 128 * (st // 64) + 64 * o + st % 64
         return ("ABT", a, a + en - st)
 
-    LG = ("b2", 256, 288)
-    c1n, OO = ("b2", 268, 276), ("b7", 384, 400)
-    XD, XS, RP = [sub("b7", 128, j) for j in range(3)]
-    FI, SE = sub("FS", 128, 0), sub("FS", 128, 1)
-    U0, G12, X1N, F1N = [(sub("GF", 64, j), sub("GF", 64, 7 - j)) for j in range(4)]
-    LU0, LG12, LX1 = [(sub(LG, 4, j), sub(LG, 4, 7 - j)) for j in range(3)]
-    COL = (("b5", 256, 260), ("b6", 256, 260))
+    XS, RP = ("b7", 0, 128), ("b7", 256, 384)
+    FI, SE = (("FS", 0, 64), ("FS", 192, 256)), ("FS", 64, 192)
+    U0, X1N, F1N = [(sub("GF", 64, j), sub("GF", 64, 5 - j)) for j in range(3)]
+    LG = (("b2", 0, 12), ("b2", 16, 28))
+    LU0, LX1, c1n = [(sub(LG[0], 4, j), sub(LG[1], 4, 2 - j)) for j in range(3)]
 
     for t in range(RO):
         last = t == RO - 1
-        mN, rN, mX, rX = "mN%d" % t, "rN%d" % t, "mX%d" % t, "rX%d" % t
+        mN, rN, mX, rX = [sub(x, 128, t) for x in ("mN", "rN", "mX", "rX")]
         done = {}
+        push[1] = t
 
         def named(name, fn, *args):
             if name in C["after"]:
@@ -541,44 +616,72 @@ def rank_program(g, core, T, topo):
             fn(*args)
             done[name] = count()
 
+        def columns(a, b):
+            oo = ("b7" if b == 128 else "b3", 400 + a // 8, 400 + b // 8)
+            listing(oo, "LK", ("FS", 2 * a, 2 * b), ("I16", ("CT", a // 8, b // 8)))
+            lin(C["ou"], ("ou", a // 8, b // 8), oo)
+            off = ("ou", 4 + a // 16, 4 + b // 16)
+            if a == 64:
+                gsub(("z2", a, b), "Z", off, ("xb", a, b))
+                push[3] = "mX:%d" % a
+                act((mX[0], mX[1] + a, mX[1] + b), ("z2", a, b), AF.Abs)
+            else:
+                act(("z2", a, b), DW, AF.Abs, off=off)
+                xd = (oo[0], 136 + a, 136 + b) if b == 64 else (oo[0], 128 + a, 128 + b)
+                msum(xd, ("BF2", (SE[0], SE[1] + a, SE[1] + b)), ("IB", ("xb", a, b)), ("NIB", ("z2", a, b)))
+                push[3] = "mX:%d" % a
+                act((mX[0], mX[1] + a, mX[1] + b), xd, AF.Abs, bias=1024.0)
+            push[3] = None
+            send(t, (mX[0], mX[1] + a, mX[1] + b), (rX[0], rX[1] + a, rX[1] + b), "aX%d%d" % (t, a // 64))
+
         for h in range(2):
             gat(C["cu"][h], hf("Cu", h), SW, hl("su", h))
             for j, (q, a, b) in enumerate(C["g"][h]):
                 named("g%d%d" % (h, j), gat, q, ("G%d" % h, 16 * a, 16 * b), SW, ("Cu", 64 * h + a, 64 * h + b))
-            if h:
+            if h and C["merge"] == 0:
+                push[2] = "a"
                 sca(SD, hl("sou", 0), hf("Sn", 0))
-            for o, tab, bk in ((1, "DB", "b%d" % (5 + h)), (0, "DA", "b%d" % h)):
-                msum((bk, 0, 64), *[(sub(tab, 128, k), ("G%d" % h, k, 1024, 16)) for k in range(16)])
-                lin(C["ab"][2 * h + 1 - o], ablist(64 * h, 64 * h + 64, o), (bk, 0, 64))
+                push[2] = ""
+            for a, b, qs in C["pick"][h]:
+                for o, tab, bk in ((1, "DB", "b%d" % (5 + h)), (0, "DA", "b%d" % h)):
+                    msum((bk, a, b), *[(sub(tab, 128, k), ("G%d" % h, 16 * a + k, 16 * b, 16)) for k in range(16)])
+                    lin(qs[1 - o], ablist(64 * h + a, 64 * h + b, o), (bk, a, b))
             EN, EM = ("b%d" % (3 + h), 384, 448), ("b%d" % (3 + h), 448, 512)
             lin(C["c16"][h], hf("C16", h), hf("Cu", h))
             gat(C["sl"][h], hf("SL", h), "TB", hl("su", h))
             en = [("NI32", hf("C16", h)), ("IB", hf("SL", h))] + ([("ONB", "FCB")] if t else [])
             msum(EN, *en)
             lin(C["qe"][h], hf("qe", h), EN, 1.0 / 512, 1280.0 - 15.0 / 32)
-            msum(EM, *(en + [("N512", "K12"), ("N512", hf("qe", h))]))
-            lin(C["n1"][h], hl("n1", h), hl("si", h), 5.0, -16.0)
+            msum(EM, *(en + [("N512", ("K12", 0, 64)), ("N512", hf("qe", h))]))
+            lin(C["n1"][h], hl("n1", h), hl("si", h), 5.0)
+            push[0] = C["push"][2 * h]
             for j, (q, st, end) in enumerate(C["x"][h]):
                 st, end = st + 64 * h, end + 64 * h
                 xb_, d_, z_ = [(x, 16 * st, 16 * end) for x in ("XB", "ZB", "Z")]
                 named("b%d%d" % (h, j), gat, q, xb_, XW, ablist(st, end, 1))
                 named("d%d%d" % (h, j), gsub, d_, XW, ablist(st, end, 0), xb_)
-                if C["size"][h] == "s":
+                if C["size"][h][j] == "s":
                     named("z%d%d" % (h, j), act, z_, d_, AF.Abs)
                 else:
                     named("z%d%d" % (h, j), ts, z_, d_, 0.0, OP.max, 2.0, OP.mult)
             A, V = "b%d" % h, "b%d" % (3 + h)
+            push[0] = C["push"][2 * h + 1]
             U = (A, 128, 192)
-            XP, CNT, SO = (V, 192, 256), (V, 256, 320), (V, 320, 324)
+            COL, SO = (A, 384, 392), (A, 400, 404)
             cl = hf("cl", h)
-            tabs = [("WN", "ZB"), ("WP", "Z")] if C["size"][h] == "v" else [("WP", "Z")]
-            msum(U, *[((w,) + slm(k), (z, 1024 * h + k, 1024 * h + 1024, 16)) for w, z in tabs for k in range(16)])
-            lin(C["q"][h], hf("ui", h), U, 1.0, 16.0)
+            off = [x for j, x in enumerate(C["x"][h]) if C["size"][h][j] == "v"]
+            if off:
+                a, b = off[0][1], off[-1][2]
+                push[2] = "o"
+                mms([(U, "ZO", ("IB", 0, 64), True, False)])
+                push[2] = "d"
+                mms([((A, 128 + a, 128 + b), ("WN",) + slm(k), ("ZB", 1024 * h + 16 * a + k, 1024 * h + 16 * b, 16), False, False)
+                     for k in range(16)])
+                push[2] = ""
+            mms([(U, ("WP",) + slm(k), ("Z", 1024 * h + k, 1024 * h + 1024, 16), k == 0 and not off, k == 15) for k in range(16)])
+            lin(C["q"][h], hf("ui", h), U)
             ts(hf("uk", h), hf("ui", h), 2047, OP.bitwise_and)
-            if C["sq"][h] == "s":
-                act(hf("sq", h), hf("uk", h), AF.Square)
-            else:
-                tt(hf("sq", h), hf("uk", h), hf("uk", h), OP.mult)
+            act(hf("sq", h), hf("uk", h), AF.Square, bias=16.0)
             lin(C["v16"][h], hf("V16", h), hf("uk", h))
             lin(C["u0"][h], U0[h], hf("uk", h), K0)
             ts(hf("yy", h), hf("sq", h), 480, OP.bitwise_and)
@@ -602,76 +705,93 @@ def rank_program(g, core, T, topo):
             else:
                 pos(qf, F1N[h], tab("R", qf), -2048.0)
                 pos(qx, X1N[h], tab("RU", qx), -2048.0)
-            named("f%d" % h, ts, G12[h], tab("R", "v"), 0.0, OP.max, 2048.0, OP.min)
+            push[3] = "mN:%d" % (64 * h)
+            ts(hf(mN, h), tab("R", "v"), 0.0, OP.max, 2048.0, OP.min)
+            push[3] = None
+            send(t, hf(mN, h), hf(rN, h), "aN%d%d" % (t, h))
             ts(hf(SE, h), tab("Q", "v"), 2048.0, OP.is_equal)
-            pos(qi, hf(FI, h), tab("Q", qi), -4095.0)
-            rows = "b%d" % (5 + h)
-            mms([(part(COL[h], 64 * e, 64 * e + 64), F1N[h], ("GI", e, 8, 2), True, True) for e in range(2)])
-            mms([(sub(rows, 64, j), sub("SEL", 128, j), F1N[h], True, True) for j in range(4)])
-            listing(sub(LG, 16, h), "L1", sub("GF", 256, h))
-            lin(C["mn"][h], hl(mN, h), LG12[h], 4095.0, -2048.0 * 4095)
-            send(t, hl(mN, h), hl(rN, h), "aN%d%d" % (t, h))
-            lin(C["c1u"][h], hl("c1u", h), hl(c1n, h), -1.0, 2048.0)
+            pos(qi, FI[h], tab("Q", qi), -4095.0)
+            rows, nj = "b%d" % (5 + h), 64 * (h + 1)
+            low = (lambda x: x) if h else (lambda x: part(x, 0, 64))
+            tri = [("I16", 0, 128), ("TRI", 0, 512)] if h else [("I16", 64, 128, 1, 64, 128), ("TRI", 0, 512, 1, 64, 128)]
+            push[2] = "t"
+            mms([(low((rows, 0, 512)), tri[0], tri[1], True, False)])
+            push[2] = "r"
+            mms([(low(sub(rows, 64, j)), ("SEL", 128 * j, 128 * j + nj), F1N[h], False, j == 7) for j in range(8)])
+            push[2] = ""
+            msum(low(COL), (("GF", 128, 128 + nj), "GI"))
+            listing(LG[h], "L1", sub("GF", 192, h))
+            for j in range(8):
+                ts(("EQ%d" % h, 16 * j, 16 * j + 16, "all", 0, nj), low(sub(rows, 64, j)), low(sub(COL, 1, j)), OP.is_equal)
+            lin(C["c1u"][h], hl("c1u", h), c1n[h], -1.0, 2048.0)
+            lin(C["c1h"][h], hl("c1h", h), c1n[h], -1.0, 2048.0)
             tt(hl("n2", h), hl("n1", h), LU0[h], OP.add)
+            ts(hl("h1", h), c1n[h], 0.0, OP.is_gt, 2.0 ** 23 + 2048, OP.mult)
+            tt(hl("h2", h), hl("h1", h), c1n[h], OP.subtract)
+            ts(hl("n3", h), hl("n2", h), 2047, OP.bitwise_and)
+            tt(hl("sb", h), hl("h2", h), hl("n3", h), OP.max)
             lin(C["x1"][h], hl("x1", h), LX1[h], -1.0)
-            if h:
-                ts("h1", c1n, 0.0, OP.is_gt, 2.0 ** 23 + 2048, OP.mult)
-                tt("h2", "h1", c1n, OP.subtract)
-                ts("n3", "n2", 2047, OP.bitwise_and)
-                tt("sb", "h2", "n3", OP.max)
-            for lo in range(h + 1):
-                for j in range(4):
-                    named("e%d" % h, ts, sub("EQ", 64, 4 * (h + lo) + j), sub(rows, 64, j), sub(COL[lo], 1, j), OP.is_equal)
-            msum(XP, ("I16", X1N[h]), ("I6", hf(FI, h)))
-            for j in range(4):
-                out = part(sub(CNT, 32, j % 2), 64 * (j // 2), 64 * (j // 2) + 64)
-                msum(out, *[(sub("EQ", 64, 4 * (h + lo) + j), sub("VJ", 32, lo)) for lo in range(h + 1)])
-            gat(C["sc"][h], hf("Sc", h), SD, hl("c1u", h))
-            named("l%d" % h, tt, hf("lt", h), CNT, hf("THR", h), OP.is_gt)
-            tt(hf("Sd", h), hf("Sc", h), XP, OP.subtract)
-            mms([(part(SO, 64 * e, 64 * e + 64), part(hf("lt", h), 64 * e, 64 * e + 64), part(hl("RQ", h), 64 * e, 64 * e + 64), True, True)
-                 for e in range(2)])
+            mms([(SO, "I16", hl("c1h", h), True, False)] +
+                [(sub(SO, 1, j), ("EQ%d" % h, 0, 128, j, 0, nj), low(("K4", 0, 1)), False, j == 3) for j in range(4)])
+            gsub(hf("Sd", h), SD, hl("c1u", h), X1N[h])
             ts(hf("Sn", h), hf("Sd", h), 2047, OP.bitwise_and)
-            named("s%d" % h, tt, hl("sou", h), SO, hl("c1u", h), OP.max)
-        sca(SD, hl("sou", 1), hf("Sn", 1))
+            tt(hl("sou", h), SO, hl("SP", h), OP.min)
+            push[0] = 0.0
+        if last:
+            columns(0, 64)
+        if C["merge"] == 1:
+            sca(SD, "sou", "Sn")
+        else:
+            if C["merge"] == 2:
+                push[2] = "a"
+                sca(SD, hl("sou", 0), hf("Sn", 0))
+                push[2] = ""
+            sca(SD, hl("sou", 1), hf("Sn", 1))
         if not last:
-            act("sg", mN, AF.Sign, bias=-0.5, accum_out=("fc", 0, 1))
+            act("sg", SE, AF.Copy, accum_out=("fc", 0, 1))
             act("FCB", ("IB", 0, 64), AF.Identity, scale=0.0, bias=("fc", 0, 1))
         for h in range(2):
-            tt(hl("se", h), hl("sb", h), hl(rN, h), OP.max)
+            RL = ("b%d" % (3 + h), 300, 304)
+            push[2] = "k"
+            mms([(RL, "N512", ("K12", 64, 68), True, False)])
+            push[2] = ""
+            a = hf(rN, h)
+            mms([(RL, ("L7",) + slm(m), (a[0], a[1] + m, a[2], 16), False, m == 15) for m in range(16)])
+            tt(hl("se", h), hl("sb", h), RL, OP.max)
             ts(hl("si", h), hl("se", h), 2047, OP.bitwise_and)
             if not last:
                 lin(C["su"][h], hl("su", h), hl("si", h))
         if last:
             cp("sf", "si")
             dma("s", "oS", ["sf"], [], T.ys[:], T.sf[:], LOCAL)
-        listing(OO, "LK", ("FS", 0, 256), ("I16", "CT"))
-        lin(C["ou"], "ou", OO)
-        act("z2", DW, AF.Abs, off=("ou", 8, 16))
-        act("z1", DW, AF.Abs, off=("ou", 0, 8))
-        msum(XD, ("BF2", SE), ("IB", xw), ("NIB", "z2"))
-        act(mX, XD, AF.Abs, bias=1024.0)
-        send(t, mX, rX, "aX%d" % t)
-        msum(XS, ("BF1", FI), ("BFH", FI), ("IB", xw), ("IB", "z1"))
+        columns(64 if last else 0, 128)
+        for h in range(2):
+            act(hf("z1", h), DW, AF.Abs, off=hl("ou", 3 * h))
+            msum(hf(XS, h), ("BF1", FI[h]), ("BFH", FI[h]), ("IB", hf("xb", h)), ("IB", hf("z1", h)))
         lin("s", "hv", XS, 0.5, 256.0)
         ts("x2", "x1", 2048 + 15, OP.bitwise_and)
         tt("xou", "x2", "XO", OP.add)
         sca(WX, "xou", "z1")
         if last:
             dma("y", "oV", [XW], [], T.yv[:], T.ZB[:, 4096:6144], 2 * LOCAL)
-            n = C["yts"]
-            acc, rest = ("b5", 0, 256), ("b6", 0, 256)
-            for q in range(n):
-                lin("s", sub("SH", 256, q), sub("S", 256, 8 - n + q))
-            msum(rest, *[("I16", sub("SH", 256, q)) for q in range(n)])
-            tt(acc, ("S", 0, 256), ("S", 256, 512), OP.add)
-            for q in range(2, 8 - n):
-                tt(acc if q < 7 - n else "yta", acc, sub("S", 256, q), OP.add)
-            tt("yto", "yta", rest, OP.add)
+            turn = []
+            for q, a, b in C["yt"]:
+                lin(q, ("SH", 256 * a, 256 * b), ("S", 256 * a, 256 * b))
+                turn += range(a, b)
+            for j, q in enumerate(turn):
+                mms([(("b5", 256, 512), "I16", sub("SH", 256, q), j == 0, j == 7)])
+            lin(C["yo"], "yto", ("b5", 256, 512))
             dma("y", "oT", ["yto"], [], T.yt[:], T.yto[:], LOCAL)
-        msum(RP, ("IB", rX))
-        tt("xm", "hv", RP, OP.min)
-        ts("xn", "xm", 255, OP.bitwise_and)
-        lin("s", "xb" if last else xw, "xn")
+        if last:
+            for h in range(2):
+                tt(hf("xm", h), hf("hv", h), hf(rX, h), OP.min)
+                ts(hf("xn", h), hf("xm", h), 255, OP.bitwise_and)
+                lin(C["xb"][h], hf("xb", h), hf("xn", h))
+        else:
+            msum(RP, ("IB", rX))
+            tt("xm", "hv", RP, OP.min)
+            ts("xn", "xm", 255, OP.bitwise_and)
+            lin("s", "xb", "xn")
+            lin("s", xw, "xn")
     dma("y", "oX", ["xb"], [], T.yx[:], T.xb[:], LOCAL)
     return emit()

@@ -4,13 +4,13 @@ from concourse.mybir import AluOpType as OP, ActivationFunctionType as AF
 N, RO = 8, 3
 NENG = 8
 CFG = {
-    "g": ((("v", 0, 16), ("v", 16, 32), ("s", 32, 64)), (("v", 0, 32), ("s", 32, 64))),
-    "x": ((("s", 0, 16), ("v", 16, 32), ("s", 32, 48), ("s", 48, 64)), (("s", 0, 16), ("s", 16, 32), ("s", 32, 48), ("s", 48, 64))),
+    "g": ((("v", 0, 14), ("v", 14, 30), ("s", 30, 64)), (("v", 0, 48), ("s", 48, 64))),
+    "x": ((("s", 0, 16), ("s", 16, 32), ("s", 32, 48), ("s", 48, 64)),) * 2,
     "after": {}, "push": (0.0, 0.0, 0.0, 0.0),
     "xb": "vv", "size": ("svvv", "ssss"),
     "cu": "vs", "pick": (((0, 64, "sv"),), ((0, 64, "sv"),)), "c16": "vv", "sl": "ss", "qe": "ss", "q": "ss", "v16": "vv", "join": "yy", "u0": "ss", "fi": "vv", "f1": "vv", "x1n": "vv", "c1u": "vv",
-    "su": "ss", "n1": "ss", "x1": "vv", "ou": "s", "db": 8, "c1h": "vv", "merge": 2,
-    "yt": (("s", 0, 2), ("v", 5, 7), ("s", 2, 4), ("v", 7, 8), ("s", 4, 5)), "yo": "s",
+    "su": "ss", "n1": "ss", "x1": "vv", "ou": "s", "db": 8, "c1h": "vv", "merge": (0, 0, 1),
+    "yt": tuple(("sv"[j % 2], j, j + 1) for j in range(8)), "yo": "s",
 }
 
 F32, F16, BF, I4, U2 = "float32", "float16", "bfloat16", "int32", "uint16"
@@ -22,20 +22,20 @@ def _sb(dtype, **bufs):
         SCRATCH[name] = ("sbuf", [128, bufs[name]], dtype)
 
 
-_sb(I4, S=2304, si=8, wi=1)
-_sb(BF, ZB=6144, Z=4096, XB=2048, xb=128)
+_sb(I4, S=2176, si=8, wi=1)
+_sb(BF, ZB=8192, Z=4096, XB=2048, xb=128)
 _sb(U2, su=8)
 _sb(I4, cp=1, cq=4)
-_sb(F32, cI=144, cf=16, blk=128, l256=16, rm=16, ex=16, XO=8, SP=8, il0=8, pf=16)
-_sb(F16, I16=128, P16=128, NI16=128, NI32=128, N512=128, K12=68, L1=144, LK=144, L7=144, DA=2048, DB=2048, BO=128, LT=128, MK=128,
-    SEL=1024, TRI=512, BF1=128, BFH=128, BF2=128, GI=8, CT=16)
-_sb(BF, TB=2048, SL=128, FCB=64, ONB=128, IB=128, NIB=128, WN=144, WP=144, K4=2, ZO=128, hs=1024, c64=512)
+_sb(F32, cI=144, cf=16, blk=128, l256=16, rm=16, ex=16, XO=8, SP=8, gm=8, il0=8, pf=16)
+_sb(F16, I16=128, P16=128, NI16=128, NI32=128, N512=128, K12=68, L1=144, LK=144, L7=144, DA=2048, DB=2048, BO=128, MK=128,
+    SEL=1024, BF1=128, BFH=128, BF2=128, GI=8, CT=16)
+_sb(BF, TB=2048, SL=128, FCB=64, ONB=128, IB=128, NIB=128, WN=144, WP=144, K4=2, ZO=128, LT=128, TRI=512)
 _sb(U2, Cu=128, ABT=256, ou=16, c1u=8, sou=8, xou=8)
-_sb(F16, C16=128, G0=1024, G1=1024, cl=128, FS=256, GF=384, c1h=8, V16=128, qe=128, hv=128, SH=2048)
+_sb(F16, C16=128, G0=1024, G1=1024, cl=128, FS=256, GF=512, c1h=8, V16=128, qe=128, hv=128, SH=2048)
 _sb(BF, z1=128, z2=128, sg=128)
-_sb(I4, ui=128, uk=128, sq=128, yy=128, Sc=128, Sd=128, Sn=128, x1=8, x2=8, n2=8, n3=8, se=8, xm=128, xn=128)
-_sb(F32, n1=8, h1=8, h2=8, sb=8, fc=1, sf=8, yto=256)
-SEMAPHORES = ["qv", "qs", "qp", "qg", "dS0", "dX", "dx0", "dw", "ds0", "oV", "oT", "oX", "oS", "sent"]
+_sb(I4, ui=128, uk=128, sq=128, yy=128, Sc=128, Sd=128, Sn=128, x1=8, x2=8, n2=8, n3=8, xm=128, xn=128)
+_sb(F32, n1=8, h1=8, h2=8, se=48, SC=24, fc=1, sf=8, yto=256)
+SEMAPHORES = ["qv", "qs", "qp", "qg", "dS0", "dX", "dx0", "dw", "ds0", "oV0", "oV1", "oT", "oX", "oS", "sent"]
 for _h in range(2):
     SCRATCH["EQ%d" % _h] = ("sbuf", [128, 4, 128], BF)
 for _t in range(RO):
@@ -50,23 +50,29 @@ COST = {"cyc": 0.00086, "pe": 0.00045, "gath": 1.35, "scat": 3.8, "wake": 0.23, 
         "look": 0.05, "idle": 3.0, "tries": 30, "jit": 0.3, "chunk": 4, "long": 0.4, "seed": 12345, "swaps": 20000, "shifts": 0, "shift": 1.5, "warm": 0.1, "far": 4, "drift": 1, "heat": 0.05}
 PLAN = {}
 _E0, _E1 = [" ".join("EQ%d:%d" % (_h, 16 * _j) for _j in range(8)) for _h in range(2)]
-_V = ("Cu:0 G0:0 <se:4 G0:256 <si:4 <ZB:2048 G1:0 ABT:0 "
-      "XB:256 ZB:256 ZB:0 Z:256 ZB:512 ABT:128 ZB:768 Z:512 ZB:1024 Z:768 ZB:1280 ZB:1536 ZB:1792 "
-      "uk:0 V16:0 yy:0 cl:0 uk:64 mN:0 GF:64 FS:64 FS:0 V16:64 <xm:0 yy:64 <xn:0 cl:64 " + _E0 + " h1:0 c1h:0 GF:192 mN:64 ")
-_R = " c1u:4 c1h:4 Sn:0 sou:0 Sd:64 S:0a Sn:64 sou:4 "
-_S0 = "G0:512 <mX:0 SL:0 <su:4 Cu:64 ABT:64 G1:512 "
-_S = ("XB:0 XB:512 XB:768 ABT:192 qe:0 XB:1024 Z:0 XB:1280 XB:1536 XB:1792 qe:64 Z:1024 Z:1280 ui:0 Z:1536 Z:1792 "
+_V0 = "Cu:0 G0:0 <se:24 G0:224 <su:4 <ZB:4096 C16:0 G1:0 ABT:0 C16:64 "
+_V = ("ZB:0 ZB:256 ZB:512 Z:256 ABT:128 ZB:768 Z:512 ZB:1024 Z:768 ZB:1280 ZB:1536 ZB:1792 "
+      "uk:0 MK:0 V16:0 yy:0 cl:0 mN:0 uk:64 GF:128 GF:64 FS:64 FS:0 V16:64 <xm:0 yy:64 <xn:0 cl:64 " + _E0 + " GF:192 mN:64 ")
+_L = "c1h:0 h1:0 c1u:0 GF:256 n2:0 x1:0 h2:0 Sd:0 "
+_V1 = (_L + "n3:0 FS:128 FS:192 " + _E1.replace("EQ1:64", "sou:0 Sn:0 sb:0 EQ1:64") +
+       " c1h:4 c1u:4 S:0a n2:4 h1:4 x1:4 Sd:64 sou:4 n3:4 h2:4 Sn:64 se:0 sb:4 S:0 su:0")
+_V2 = ("GF:384 GF:448 GF:256 c1h:0 c1u:0 x1:0 FS:192 h1:0 n2:0 Sd:0 x2:0 h2:0 xou:0 n3:0 Sn:0 ou:8 c1u:4 c1h:4 x1:4 h1:4 z2:64 " + _E1 +
+       " Sd:64 sou:0 n2:4 h2:4 sb:0 Sn:64 x2:4 sou:4 n3:4 ZB:4096 S:0 xou:4 sb:4 SH:256 ZB:5120 SH:768 SH:1280 SH:1792 "
+       "xm:0 se:0 se:24 xm:64 xn:0 sf:0 sf:4 xn:64 xb:0 xb:64")
+_S0 = "G0:480 <mX:0 SL:0 n1:0 Cu:64 G1:768 ABT:64 "
+_S = ("XB:0 XB:256 XB:512 XB:768 ABT:192 Z:0 XB:1024 qe:0 XB:1280 XB:1536 XB:1792 qe:64 Z:1024 Z:1280 ui:0 Z:1536 Z:1792 "
       "sq:0 GF:0 ui:64 sq:64 <xb:0 <ZB:2048 GF:320 ")
-_P = ("b5:0 b0:0 b6:0 b1:0 b5:0t b6:0t b0:144d b0:128 b4:448 b1:128 b3:128 <b7:256 b5:0r b0:384 b5:256r b2:0 b4:64 b3:400 "
-      "b6:0r b1:384 b6:256r ")
+_P = ("b5:0 b0:0 b6:0 b1:0 b0:144d b0:128 b5:0t b6:0t b4:448 b1:128 b0:192 b3:64 <b7:256 b0:384 b5:0r0 b5:256r0 b2:0 "
+      "b1:192 b4:64 b4:0 b3:400 b5:256t ")
 TURN = {
-    "v": _V + "c1u:0 x1:0 h2:0 n2:0 FS:128 FS:192 Sd:0 " + _E1 + _R + "se:0 S:0 si:0",
-    "v2": _V + "FS:128 FS:192 c1u:0 x1:0 h2:0 n2:0 Sd:0 " + _E1 + " z2:64" + _R + "S:0 ZB:2048 SH:1280 SH:1792 se:0 xm:0",
+    "v0": "Cu:0 G0:0 G0:224 G1:0 C16:0 C16:64 ABT:0 " + _V + _V1,
+    "v": _V0 + _V + _V1,
+    "v2": _V0 + _V + _V2,
+    "s0": "Cu:64 G0:480 G1:768 SL:0 SL:64 ABT:64 " + _S + "z1:0 z1:64 z2:0",
     "s": _S0 + _S + "z1:0 z1:64 z2:0",
-    "s0": "Cu:64 G0:512 G1:512 ABT:64 " + _S + "z1:0 z1:64 z2:0",
-    "s2": _S0 + _S + "ou:0 z2:0 z1:0 ou:8 mX:0 z1:64 mX:64 hv:0 SH:0",
-    "p": _P + "b2:16 b0:400 b0:403 b1:400 b1:403 b3:300 b7:400",
-    "p2": _P + "b7:408 b3:136 b2:16 b0:400 b0:403 b1:400 b1:403 b7:0 b7:64 b3:300 b4:300",
+    "s2": _S0 + _S + "ou:0 z2:0 z1:0 mX:0 mX:64 z1:64 hv:0 SH:0",
+    "p": _P + "b1:384 b6:0r1 b5:256r1 b0:400 b0:403 b2:16 b7:400 b3:301k b1:400 b1:403 b3:301",
+    "p2": _P + "b7:416 b1:384 b6:0r1 b5:256r1 b3:136 b0:400 b0:403 b1:400 b1:403 b7:0 b7:64 b3:301 b4:301 b5:256",
 }
 
 
@@ -99,7 +105,7 @@ def make_plan(g, T):
                     elif over:
                         pred[j] = True
         if after is not None:
-            pred[after] = False
+            pred.setdefault(after, False)
         while hint:
             pred.setdefault(hint.pop(), False)
         nodes.append({"q": q, "wr": wr, "push": push[0], "step": push[1], "tag": push[2], "name": push[3], "fns": fns, "dur": dur, "sem": sem, "inc": inc, "lat": lat, "pred": pred, "i": i})
@@ -115,7 +121,7 @@ def make_plan(g, T):
         by = {}
         for x in nodes:
             if x["wr"]:
-                by.setdefault((x["step"], x["q"], x["name"] or "%s:%d" % x["wr"][0][:2] + x["tag"]), []).append(x["i"])
+                by.setdefault((0 if x["wr"][0][0] == "MK" else x["step"], x["q"], x["name"] or "%s:%d" % x["wr"][0][:2] + x["tag"]), []).append(x["i"])
         for q in "vsp":
             for t in range(RO):
                 ids = [by.get((t - 1, q, w[1:]) if w[0] == "<" else (t, q, w)) for w in TURN.get(q + str(t), TURN.get(q, "")).split()]
@@ -417,6 +423,10 @@ def rank_program(g, core, T, topo):
         ps = buf(in0) in PSUM or buf(in1) in PSUM
         vec([in0, in1], out, lambda e: e.tensor_tensor(o, a, b, op), width(out) * (1 if ps else 2))
 
+    def scan(out, d0, d1):
+        o, a, b = cols(out)[0], cols(d0)[0], cols(d1)[0]
+        vec([d0, d1], out, lambda e: e.tensor_tensor_scan(o, a, b, -4e9, OP.max, OP.add), width(out))
+
     def cp(out, in0):
         o, a = cols(out)[0], cols(in0)[0]
         vec([in0], out, lambda e: e.tensor_copy(o, a), width(out) * (0.5 if small(out, in0) else 1))
@@ -493,13 +503,18 @@ def rank_program(g, core, T, topo):
             fn = lambda e: e.iota(o, pattern, base, cm)
         prev["g"] = add("g", [], [cols(out)[1]], [fn], 0.13 + 2 * CYC * width(out), after=prev.get("g"))
 
+    def pick(out, pattern, op, v, base, cm):
+        o, r = cols(out)
+        prev["g"] = add("g", [r], [r], [lambda e: e.affine_select(o, o, pattern, op, v, base, cm)], 0.17 + 2 * CYC * width(out),
+                        after=prev.get("g"))
+
     def dma(q, s, rd, wr, out, in_, us, turn=False):
         prev[q] = add(q, rd, wr, [lambda e: e.dma_start(out, in_)], 0.1, sem=s, inc=16, lat=us, after=prev.get(q) if turn else None)
 
     prev = {}
 
-    SW, SD = ("S", 0, 2048), ("S", 0, 2304)
-    DW, WX, XW, xw = ("ZB", 0, 4096), ("ZB", 2048, 6144), ("ZB", 4096, 6144), ("ZB", 2048, 4096, 16)
+    SW, SD = ("S", 0, 2048), ("S", 0, 2176)
+    DW, XW, xw = ("ZB", 0, 4096), ("ZB", 4096, 6144), ("ZB", 2048, 4096, 16)
     LOCAL = COST["local"]
 
     dma("s", "ds0", [], ["si"], T.si[:], T.s0[:], LOCAL)
@@ -516,10 +531,14 @@ def rank_program(g, core, T, topo):
     iota("il0", [[16, 8]], 0, 0)
     iota("l256", [[1024, 2], [0, 2], [256, 4]], 0, 0)
     iota("TB", [[0, 128], [32, 16]], 256, 0)
-    iota("c64", [[0, 8], [1, 64]], 64, 0)
-    iota("hs", [[16, 8], [0, 128]], 0, 0)
+    iota("LT", [[0, 128]], -2048, 0)
+    pick("LT", [[1, 128]], OP.is_gt, 0.0, 0, -1)
+    pick("LT", [[1, 128]], OP.not_equal, 4096.0, 0, -1)
+    iota("TRI", [[0, 512]], 4096, 0)
+    pick("TRI", [[0, 8], [-1, 64]], OP.is_ge, 0.0, -64, 1)
     P = ("pf", 0, 1)
-    PX, PM, PG, PG16, KM, K0, WC, WM, CTC, XOC = [("cf", j, j + 1) for j in range(10)]
+    PX, PM, PG, PG16, KM, WC, WM, CTC, XOC = [("cf", j, j + 1) for j in range(9)]
+    K0 = ("rm", 0, 1)
     ts(("cq", 0, 1), "cp", 15, OP.bitwise_and)
     ts(("cq", 1, 2), "cp", 112, OP.bitwise_and)
     ts(("cq", 3, 4), "cp", 1, OP.bitwise_and)
@@ -535,7 +554,7 @@ def rank_program(g, core, T, topo):
     for h in range(2):
         cp(("su", 4 * h, 4 * h + 4), ("si", 4 * h, 4 * h + 4))
     ts("BO", "blk", PG, OP.is_equal)
-    for name, v in (("NI16", -1.0), ("NI32", -32.0), ("N512", -512.0), ("IB", 1.0), ("NIB", -1.0), ("MK", 4096.0)):
+    for name, v in (("NI16", -1.0), ("NI32", -32.0), ("N512", -512.0), ("IB", 1.0), ("NIB", -1.0)):
         lin("s", name, "I16", v)
     for name, v in (("BF1", -3072.0), ("BFH", -0.5), ("BF2", -1024.0)):
         lin("s", name, "BO", v)
@@ -543,29 +562,30 @@ def rank_program(g, core, T, topo):
     fill(("K12", 0, 64), -1280.0)
     fill(("K12", 64, 68), 8188.0)
     ts(PG16, PG, 16.0, OP.add)
-    cp(WC, "wi")
-    ts(WM, "wi", -1.0, OP.mult)
-    ts("WN", "cI", PG16, OP.is_equal, WM, OP.mult)
-    ts("WP", "cI", PG16, OP.is_equal, WC, OP.mult)
-    ts("LT", ("cI", 0, 128), P, OP.is_gt, -2048.0, OP.mult)
-    tt("LT", "LT", "BO", OP.mult)
-    tt("MK", "MK", "LT", OP.add)
-    ts(KM, PM, -2048.0, OP.add)
-    ts(K0, PM, 0.0, OP.is_equal)
-    ts(CTC, PM, 16.0, OP.mult, 2048.0, OP.add)
-    ts(XOC, PM, 16.0, OP.mult)
+    lin("s", WC, "wi")
+    lin("s", WM, "wi", -1.0)
+    tt("MK", "LT", "BO", OP.mult)
+    lin("s", KM, PM, 1.0, -2048.0)
+    lin("s", CTC, PM, 16.0, 2048.0)
+    lin("s", XOC, PM, 16.0)
     ts("L1", "cI", PG16, OP.is_equal)
-    ts("LK", "cI", PG16, OP.is_equal, KM, OP.mult)
-    lin("s", "L7", "L1", 2047.0)
-    fill(("S", 2048, 2304), 0)
-    ts("SEL", "hs", PG, OP.is_equal)
-    ts("GI", "il0", PG, OP.is_equal)
-    ts("CT", "l256", CTC, OP.add)
-    ts("XO", ("l256", 4, 12), XOC, OP.add)
-    ts("TRI", "c64", P, OP.is_le, 4096.0, OP.mult)
+    for name, v in (("WN", WM), ("WP", WC), ("LK", KM), ("L7", 2047.0)):
+        lin("s", name, "L1", v)
+    fill(("S", 2048, 2176), 0)
+    ts("gm", "il0", PG, OP.is_equal)
+    lin("s", "GI", "gm")
+    for j in range(8):
+        act(("SEL", 128 * j, 128 * j + 128), "I16", AF.Identity, scale=0.0, bias=("gm", j, j + 1))
+    lin("s", "CT", "l256", 1.0, CTC)
+    lin("s", "XO", ("l256", 4, 12), 1.0, XOC)
     lin("s", "SP", "XO", 1.0 / 16, 2048.0)
     fill("K4", 4096.0)
     fill("ZO", 0.0)
+    fill("SC", 0.0)
+    for j, v in ((2, -1023.5), (3, 1.5 * 2.0 ** 34), (4, -1.5 * 2.0 ** 34), (5, -4e9)):
+        fill(("SC", j, 24, 6), v)
+    for h in range(2):
+        fill(("b%d" % (3 + h), 300, 324), -1e10)
     fill(("Z", 3072, 4096, 16), 1024.0)
     lin("s", xw, "xb")
 
@@ -618,8 +638,9 @@ def rank_program(g, core, T, topo):
 
         def columns(a, b):
             oo = ("b7" if b == 128 else "b3", 400 + a // 8, 400 + b // 8)
-            listing(oo, "LK", ("FS", 2 * a, 2 * b), ("I16", ("CT", a // 8, b // 8)))
-            lin(C["ou"], ("ou", a // 8, b // 8), oo)
+            if a == 0:
+                listing(oo, "LK", ("FS", 2 * a, 2 * b), ("I16", ("CT", a // 8, b // 8)))
+                lin(C["ou"], ("ou", a // 8, b // 8), oo)
             off = ("ou", 4 + a // 16, 4 + b // 16)
             if a == 64:
                 gsub(("z2", a, b), "Z", off, ("xb", a, b))
@@ -638,7 +659,7 @@ def rank_program(g, core, T, topo):
             gat(C["cu"][h], hf("Cu", h), SW, hl("su", h))
             for j, (q, a, b) in enumerate(C["g"][h]):
                 named("g%d%d" % (h, j), gat, q, ("G%d" % h, 16 * a, 16 * b), SW, ("Cu", 64 * h + a, 64 * h + b))
-            if h and C["merge"] == 0:
+            if h and C["merge"][t] == 0:
                 push[2] = "a"
                 sca(SD, hl("sou", 0), hf("Sn", 0))
                 push[2] = ""
@@ -653,7 +674,7 @@ def rank_program(g, core, T, topo):
             msum(EN, *en)
             lin(C["qe"][h], hf("qe", h), EN, 1.0 / 512, 1280.0 - 15.0 / 32)
             msum(EM, *(en + [("N512", ("K12", 0, 64)), ("N512", hf("qe", h))]))
-            lin(C["n1"][h], hl("n1", h), hl("si", h), 5.0)
+            lin(C["n1"][h], hl("n1", h), hl("su", h), 5.0)
             push[0] = C["push"][2 * h]
             for j, (q, st, end) in enumerate(C["x"][h]):
                 st, end = st + 64 * h, end + 64 * h
@@ -686,51 +707,54 @@ def rank_program(g, core, T, topo):
             lin(C["u0"][h], U0[h], hf("uk", h), K0)
             ts(hf("yy", h), hf("sq", h), 480, OP.bitwise_and)
             named("cl%d" % h, tt, cl, hf("yy", h), (V, 448, 512), OP.is_equal)
-            made = {}
-
-            def tab(name, q):
-                if (name, q) not in made:
-                    j = {"Q": 0, "R": 2 - h, "RU": 1 + h}[name]
-                    made[(name, q)] = (A, 192 + 64 * j, 256 + 64 * j) if q == "s" else (V, 64 * j, 64 * j + 64)
-                    less = {"Q": [], "R": [("NI16", hf("C16", h))], "RU": [("NI16", hf("V16", h))]}[name]
-                    msum(made[(name, q)], *(less + [("MK", cl)]))
-                return made[(name, q)]
-
-            qf, qx, qi = C["f1"][h], C["x1n"][h], C["fi"][h]
-            for name, q in (("R", qf), ("R", "v"), ("RU", qx), ("Q", "v"), ("Q", qi)):
-                tab(name, q)
-            if qf == qx and C["join"][h] == "y":
-                a, o = min(tab("R", qf), tab("RU", qf)), min(F1N[h], X1N[h])
-                pos(qf, (o[0], o[1], o[1] + 128), (a[0], a[1], a[1] + 128), -2048.0)
-            else:
-                pos(qf, F1N[h], tab("R", qf), -2048.0)
-                pos(qx, X1N[h], tab("RU", qx), -2048.0)
+            R, RU, Q = (A, 192, 256), (V, 64, 128), (V, 0, 64)
+            push[2] = "c"
+            mms([(R, "NI16", hf("C16", h), True, False)])
+            push[2] = ""
+            mms([(R, "MK", cl, False, True)])
+            msum(RU, ("NI16", hf("V16", h)), ("MK", cl))
+            msum(Q, ("MK", cl))
+            pos("v", F1N[h], R, -2048.0)
             push[3] = "mN:%d" % (64 * h)
-            ts(hf(mN, h), tab("R", "v"), 0.0, OP.max, 2048.0, OP.min)
+            ts(hf(mN, h), R, 0.0, OP.max, 2048.0, OP.min)
             push[3] = None
             send(t, hf(mN, h), hf(rN, h), "aN%d%d" % (t, h))
-            ts(hf(SE, h), tab("Q", "v"), 2048.0, OP.is_equal)
-            pos(qi, FI[h], tab("Q", qi), -4095.0)
-            rows, nj = "b%d" % (5 + h), 64 * (h + 1)
+            pos(C["x1n"][h], X1N[h], RU, -2048.0)
+            pos(C["fi"][h], FI[h], Q, -4095.0)
+            lanes = last and h
+            if lanes:
+                ts(("GF", 384, 448), Q, 2048.0, OP.is_equal, KM, OP.mult)
+                ts(("GF", 448, 512), Q, 4096.0, OP.is_equal, KM, OP.mult)
+            else:
+                ts(hf(SE, h), Q, 2048.0, OP.is_equal)
+            nj = 64 * (h + 1)
             low = (lambda x: x) if h else (lambda x: part(x, 0, 64))
-            tri = [("I16", 0, 128), ("TRI", 0, 512)] if h else [("I16", 64, 128, 1, 64, 128), ("TRI", 0, 512, 1, 64, 128)]
-            push[2] = "t"
-            mms([(low((rows, 0, 512)), tri[0], tri[1], True, False)])
-            push[2] = "r"
-            mms([(low(sub(rows, 64, j)), ("SEL", 128 * j, 128 * j + nj), F1N[h], False, j == 7) for j in range(8)])
-            push[2] = ""
+            banks = ((("b6", 0, 256), 0, 4), (("b5", 256, 512), 4, 8)) if h else ((("b5", 0, 512), 0, 8),)
             msum(low(COL), (("GF", 128, 128 + nj), "GI"))
-            listing(LG[h], "L1", sub("GF", 192, h))
-            for j in range(8):
-                ts(("EQ%d" % h, 16 * j, 16 * j + 16, "all", 0, nj), low(sub(rows, 64, j)), low(sub(COL, 1, j)), OP.is_equal)
+            for rows, j0, j1 in banks:
+                n = 64 * (j1 - j0)
+                tri = [("IB", 0, 128), ("TRI", 0, n)] if h else [("IB", 64, 128, 1, 64, 128), ("TRI", 0, n, 1, 64, 128)]
+                push[2] = "t"
+                mms([(low(rows), tri[0], tri[1], True, False)])
+                push[2] = "r%d" % h
+                mms([(low(sub(rows, 64, j - j0)), ("SEL", 128 * j, 128 * j + nj), F1N[h], False, j == j1 - 1) for j in range(j0, j1)])
+                push[2] = ""
+            if lanes:
+                listing(("b7", 416, 436), "L1", ("GF", 192, 512))
+                tt(("ou", 8, 16), ("b7", 428, 436), ("CT", 8, 16), OP.add)
+                c1n, LX1, LU0 = [(None, ("b7", 416 + 4 * j, 420 + 4 * j)) for j in range(3)]
+            else:
+                listing(LG[h], "L1", sub("GF", 192, h))
+            for rows, j0, j1 in banks:
+                for j in range(j0, j1):
+                    ts(("EQ%d" % h, 16 * j, 16 * j + 16, "all", 0, nj), low(sub(rows, 64, j - j0)), low(sub(COL, 1, j)), OP.is_equal)
             lin(C["c1u"][h], hl("c1u", h), c1n[h], -1.0, 2048.0)
             lin(C["c1h"][h], hl("c1h", h), c1n[h], -1.0, 2048.0)
             tt(hl("n2", h), hl("n1", h), LU0[h], OP.add)
-            ts(hl("h1", h), c1n[h], 0.0, OP.is_gt, 2.0 ** 23 + 2048, OP.mult)
+            ts(hl("h1", h), c1n[h], 0.0, OP.is_gt, 2.0 ** 22 + 2048, OP.mult)
             tt(hl("h2", h), hl("h1", h), c1n[h], OP.subtract)
             ts(hl("n3", h), hl("n2", h), 2047, OP.bitwise_and)
-            tt(hl("sb", h), hl("h2", h), hl("n3", h), OP.max)
-            lin(C["x1"][h], hl("x1", h), LX1[h], -1.0)
+            lin(C["x1"][h], hl("x1", h), LX1[h], -1.0, 2048.0)
             mms([(SO, "I16", hl("c1h", h), True, False)] +
                 [(sub(SO, 1, j), ("EQ%d" % h, 0, 128, j, 0, nj), low(("K4", 0, 1)), False, j == 3) for j in range(4)])
             gsub(hf("Sd", h), SD, hl("c1u", h), X1N[h])
@@ -739,10 +763,10 @@ def rank_program(g, core, T, topo):
             push[0] = 0.0
         if last:
             columns(0, 64)
-        if C["merge"] == 1:
+        if C["merge"][t] == 1:
             sca(SD, "sou", "Sn")
         else:
-            if C["merge"] == 2:
+            if C["merge"][t] == 2:
                 push[2] = "a"
                 sca(SD, hl("sou", 0), hf("Sn", 0))
                 push[2] = ""
@@ -751,29 +775,37 @@ def rank_program(g, core, T, topo):
             act("sg", SE, AF.Copy, accum_out=("fc", 0, 1))
             act("FCB", ("IB", 0, 64), AF.Identity, scale=0.0, bias=("fc", 0, 1))
         for h in range(2):
-            RL = ("b%d" % (3 + h), 300, 304)
+            V = "b%d" % (3 + h)
+            RL = (V, 301, 324, 6)
+            push[3] = "sb:%d" % (4 * h)
+            tt((V, 300, 324, 6), hl("h2", h), hl("n3", h), OP.max)
+            push[3] = None
             push[2] = "k"
             mms([(RL, "N512", ("K12", 64, 68), True, False)])
             push[2] = ""
             a = hf(rN, h)
             mms([(RL, ("L7",) + slm(m), (a[0], a[1] + m, a[2], 16), False, m == 15) for m in range(16)])
-            tt(hl("se", h), hl("sb", h), RL, OP.max)
-            ts(hl("si", h), hl("se", h), 2047, OP.bitwise_and)
-            if not last:
-                lin(C["su"][h], hl("su", h), hl("si", h))
+            se = sub("se", 24, h)
+            scan(se, (V, 300, 324), "SC")
+            tt(hl("sf" if last else "su", h), (se[0], se[1] + 1, se[2], 6), (se[0], se[1] + 4, se[2], 6), OP.subtract)
         if last:
-            cp("sf", "si")
-            dma("s", "oS", ["sf"], [], T.ys[:], T.sf[:], LOCAL)
+            dma("y", "oS", ["sf"], [], T.ys[:], T.sf[:], LOCAL)
         columns(64 if last else 0, 128)
         for h in range(2):
             act(hf("z1", h), DW, AF.Abs, off=hl("ou", 3 * h))
             msum(hf(XS, h), ("BF1", FI[h]), ("BFH", FI[h]), ("IB", hf("xb", h)), ("IB", hf("z1", h)))
         lin("s", "hv", XS, 0.5, 256.0)
-        ts("x2", "x1", 2048 + 15, OP.bitwise_and)
-        tt("xou", "x2", "XO", OP.add)
-        sca(WX, "xou", "z1")
-        if last:
-            dma("y", "oV", [XW], [], T.yv[:], T.ZB[:, 4096:6144], 2 * LOCAL)
+        if not last:
+            ts("x2", "x1", 2048 + 15, OP.bitwise_and)
+            tt("xou", "x2", "XO", OP.add)
+            sca(("ZB", 4096, 8192), "xou", "z1")
+        else:
+            for h in range(2):
+                ts(hl("x2", h), hl("x1", h), 2048 + 15, OP.bitwise_and)
+                tt(hl("xou", h), hl("x2", h), hl("XO", 0), OP.add)
+                a = 4096 + 1024 * h
+                sca(("ZB", a, 8192), hl("xou", h), hf("z1", h))
+                dma("y", "oV%d" % h, [("ZB", a, a + 1024)], [], T.yv[:, 1024 * h:1024 * h + 1024], T.ZB[:, a:a + 1024], 1.4 * LOCAL)
             turn = []
             for q, a, b in C["yt"]:
                 lin(q, ("SH", 256 * a, 256 * b), ("S", 256 * a, 256 * b))
@@ -781,7 +813,7 @@ def rank_program(g, core, T, topo):
             for j, q in enumerate(turn):
                 mms([(("b5", 256, 512), "I16", sub("SH", 256, q), j == 0, j == 7)])
             lin(C["yo"], "yto", ("b5", 256, 512))
-            dma("y", "oT", ["yto"], [], T.yt[:], T.yto[:], LOCAL)
+            dma("s", "oT", ["yto"], [], T.yt[:], T.yto[:], LOCAL)
         if last:
             for h in range(2):
                 tt(hf("xm", h), hf("hv", h), hf(rX, h), OP.min)

import math
from concourse.mybir import AluOpType as OP, ActivationFunctionType as AF

N, RO = 8, 3
NENG = 8
CFG = {
    "g": ((("v", 0, 14), ("v", 14, 30), ("s", 30, 64)), (("v", 0, 48), ("s", 48, 64))),
    "x": ((("s", 0, 16), ("s", 16, 32), ("s", 32, 48), ("s", 48, 64)),) * 2,
    "after": {}, "push": (0.0, 0.0, 0.0, 0.0),
    "xb": "vv", "size": ("svvv", "ssss"),
    "cu": "vs", "pick": (((0, 64, "sv"),), ((0, 64, "sv"),)), "c16": "vv", "sl": "ss", "qe": "ss", "q": "ss", "v16": "vv", "join": "yy", "u0": "ss", "fi": "vv", "f1": "vv", "x1n": "vv", "c1u": "vv",
    "su": "ss", "n1": "ss", "x1": "vv", "ou": "s", "db": 8, "c1h": "vv", "merge": (0, 0, 1),
    "yt": tuple(("sv"[j % 2], j, j + 1) for j in range(8)), "yo": "s",
}

F32, F16, BF, I4, U2 = "float32", "float16", "bfloat16", "int32", "uint16"
SCRATCH = {}


def _sb(dtype, **bufs):
    for name in bufs:
        SCRATCH[name] = ("sbuf", [128, bufs[name]], dtype)


_sb(I4, S=2176, si=8, wi=1)
_sb(BF, ZB=8192, Z=4096, XB=2048, xb=128)
_sb(U2, su=8)
_sb(I4, cp=1, cq=4)
_sb(F32, cI=144, cf=16, blk=128, l256=16, rm=16, ex=16, XO=8, SP=8, gm=8, il0=8, pf=16)
_sb(F16, I16=128, P16=128, NI16=128, NI32=128, N512=128, K12=68, L1=144, LK=144, L7=144, DA=2048, DB=2048, BO=128, MK=128,
    SEL=1024, BF1=128, BFH=128, BF2=128, GI=8, CT=16)
_sb(BF, TB=2048, SL=128, FCB=64, ONB=128, IB=128, NIB=128, WN=144, WP=144, K4=2, ZO=128, LT=128, TRI=512)
_sb(U2, Cu=128, ABT=256, ou=16, c1u=8, sou=8, xou=8)
_sb(F16, C16=128, G0=1024, G1=1024, cl=128, FS=256, GF=512, c1h=8, V16=128, qe=128, hv=128, SH=2048)
_sb(BF, z1=128, z2=128, sg=128)
_sb(I4, ui=128, uk=128, sq=128, yy=128, Sc=128, Sd=128, Sn=128, x1=8, x2=8, n2=8, n3=8, xm=128, xn=128)
_sb(F32, n1=8, h1=8, h2=8, se=48, SC=24, fc=1, sf=8, yto=256)
SEMAPHORES = ["qv", "qs", "qp", "qg", "dS0", "dX", "dx0", "dw", "ds0", "oV0", "oV1", "oT", "oX", "oS", "sent"]
for _h in range(2):
    SCRATCH["EQ%d" % _h] = ("sbuf", [128, 4, 128], BF)
for _t in range(RO):
    _sb(F16, mN=128 * RO, rN=128 * RO)
    _sb(BF, mX=128 * RO, rX=128 * RO)
    SEMAPHORES += ["aN%d0" % _t, "aN%d1" % _t, "aX%d0" % _t, "aX%d1" % _t]
PSUM = ["b%d" % _b for _b in range(8)]
for _b in PSUM:
    SCRATCH[_b] = ("psum", [128, 512], F32)

COST = {"cyc": 0.00086, "pe": 0.00045, "gath": 1.35, "scat": 3.8, "wake": 0.23, "own": 0.23, "local": 2.0, "flight": 2.1, "S": 3.2, "X": 4.9, "act": 50,
        "look": 0.05, "idle": 3.0, "tries": 30, "jit": 0.3, "chunk": 4, "long": 0.4, "seed": 12345, "swaps": 20000, "shifts": 0, "shift": 1.5, "warm": 0.1, "far": 4, "drift": 1, "heat": 0.05}
PLAN = {}
_E0, _E1 = [" ".join("EQ%d:%d" % (_h, 16 * _j) for _j in range(8)) for _h in range(2)]
_V0 = "Cu:0 G0:0 <se:24 G0:224 <su:4 <ZB:4096 C16:0 G1:0 ABT:0 C16:64 "
_V = ("ZB:0 ZB:256 ZB:512 Z:256 ABT:128 ZB:768 Z:512 ZB:1024 Z:768 ZB:1280 ZB:1536 ZB:1792 "
      "uk:0 MK:0 V16:0 yy:0 cl:0 mN:0 uk:64 GF:128 GF:64 FS:64 FS:0 V16:64 <xm:0 yy:64 <xn:0 cl:64 " + _E0 + " GF:192 mN:64 ")
_L = "c1h:0 h1:0 c1u:0 GF:256 n2:0 x1:0 h2:0 Sd:0 "
_V1 = (_L + "n3:0 FS:128 FS:192 " + _E1.replace("EQ1:64", "sou:0 Sn:0 sb:0 EQ1:64") +
       " c1h:4 c1u:4 S:0a n2:4 h1:4 x1:4 Sd:64 sou:4 n3:4 h2:4 Sn:64 se:0 sb:4 S:0 su:0")
_V2 = ("GF:384 GF:448 GF:256 c1h:0 c1u:0 x1:0 FS:192 h1:0 n2:0 Sd:0 x2:0 h2:0 xou:0 n3:0 Sn:0 ou:8 c1u:4 c1h:4 x1:4 h1:4 z2:64 " + _E1 +
       " Sd:64 sou:0 n2:4 h2:4 sb:0 Sn:64 x2:4 sou:4 n3:4 ZB:4096 S:0 xou:4 sb:4 SH:256 ZB:5120 SH:768 SH:1280 SH:1792 "
       "xm:0 se:0 se:24 xm:64 xn:0 sf:0 sf:4 xn:64 xb:0 xb:64")
_S0 = "G0:480 <mX:0 SL:0 n1:0 Cu:64 G1:768 ABT:64 "
_S = ("XB:0 XB:256 XB:512 XB:768 ABT:192 Z:0 XB:1024 qe:0 XB:1280 XB:1536 XB:1792 qe:64 Z:1024 Z:1280 ui:0 Z:1536 Z:1792 "
      "sq:0 GF:0 ui:64 sq:64 <xb:0 <ZB:2048 GF:320 ")
_P = ("b5:0 b0:0 b6:0 b1:0 b0:144d b0:128 b5:0t b6:0t b4:448 b1:128 b0:192 b3:64 <b7:256 b0:384 b5:0r0 b5:256r0 b2:0 "
      "b1:192 b4:64 b4:0 b3:400 b5:256t ")
TURN = {
    "v0": "Cu:0 G0:0 G0:224 G1:0 C16:0 C16:64 ABT:0 " + _V + _V1,
    "v": _V0 + _V + _V1,
    "v2": _V0 + _V + _V2,
    "s0": "Cu:64 G0:480 G1:768 SL:0 SL:64 ABT:64 " + _S + "z1:0 z1:64 z2:0",
    "s": _S0 + _S + "z1:0 z1:64 z2:0",
    "s2": _S0 + _S + "ou:0 z2:0 z1:0 mX:0 mX:64 z1:64 hv:0 SH:0",
    "p": _P + "b1:384 b6:0r1 b5:256r1 b0:400 b0:403 b2:16 b7:400 b3:301k b1:400 b1:403 b3:301",
    "p2": _P + "b7:416 b1:384 b6:0r1 b5:256r1 b3:136 b0:400 b0:403 b1:400 b1:403 b7:0 b7:64 b3:301 b4:301 b5:256",
}


def make_plan(g, T):
    eng = {"v": g.vector, "s": g.scalar, "p": g.tensor, "g": g, "y": g.sync}
    qsem = {"v": "qv", "s": "qs", "p": "qp", "g": "qg"}
    nodes = []
    hist = {}
    hint = []
    push = [0.0, -1, "", None]
    WAKE = COST["wake"]

    def rng(x):
        return (x, 0, T[x].shape[1]) if isinstance(x, str) else x

    def add(q, rd, wr, fns, dur, sem=None, inc=1, lat=0.0, after=None):
        i = len(nodes)
        rd = [rng(x) for x in rd]
        wr = [rng(x) for x in wr]
        pred = {}
        for acc, isw in ((rd, False), (wr, True)):
            for name, a, b in acc:
                for (a0, b0, w0, j) in hist.get(name, []):
                    over = a < b0 and a0 < b and (isw or w0)
                    if name in PSUM:
                        if nodes[j]["q"] != q or (over and q != "p"):
                            pred[j] = True
                        elif q == "p":
                            pred.setdefault(j, False)
                    elif over:
                        pred[j] = True
        if after is not None:
            pred.setdefault(after, False)
        while hint:
            pred.setdefault(hint.pop(), False)
        nodes.append({"q": q, "wr": wr, "push": push[0], "step": push[1], "tag": push[2], "name": push[3], "fns": fns, "dur": dur, "sem": sem, "inc": inc, "lat": lat, "pred": pred, "i": i})
        for name, a, b in wr:
            keep = [h for h in hist.get(name, []) if not (a <= h[0] and h[1] <= b and h[3] in pred)]
            hist[name] = keep + [(a, b, True, i)]
        for name, a, b in rd:
            hist[name] = hist.get(name, []) + [(a, b, False, i)]
        return i

    def order():
        n = len(nodes)
        by = {}
        for x in nodes:
            if x["wr"]:
                by.setdefault((0 if x["wr"][0][0] == "MK" else x["step"], x["q"], x["name"] or "%s:%d" % x["wr"][0][:2] + x["tag"]), []).append(x["i"])
        for q in "vsp":
            for t in range(RO):
                ids = [by.get((t - 1, q, w[1:]) if w[0] == "<" else (t, q, w)) for w in TURN.get(q + str(t), TURN.get(q, "")).split()]
                ids = [x for x in ids if x]
                for a, b in zip(ids, ids[1:]):
                    nodes[b[0]]["pred"].setdefault(a[-1], False)
        top, left = [], [len(x["pred"]) for x in nodes]
        qs = [x["q"] for x in nodes]
        dur = [x["dur"] for x in nodes]
        succ = [[] for _ in nodes]
        pred = [[] for _ in nodes]
        for x in nodes:
            for j, w in x["pred"].items():
                gap = nodes[j]["lat"] + (COST["own"] if qs[j] == x["q"] else WAKE) if w else 0.0
                succ[j].append((x["i"], gap))
                pred[x["i"]].append((j, gap))
        top = [i for i in range(n) if not left[i]]
        for i in top:
            for j, gap in succ[i]:
                left[j] -= 1
                if not left[j]:
                    top.append(j)
        assert len(top) == n
        top.reverse()

        def run(prio, first, then, tail):
            left = [len(x) for x in first]
            ready = list(tail)
            free = dict((q, 0.0) for q in "vspgyn")
            avail = dict((q, []) for q in "vspgyn")
            best = {}
            for i in range(n):
                if not left[i]:
                    avail[qs[i]].append(i)
            out, ends, dirty = [], [0.0] * n, set(avail)
            while len(out) < n:
                for q in dirty:
                    best.pop(q, None)
                    if avail[q]:
                        fr = free[q]
                        t0 = max(fr, min(ready[i] for i in avail[q])) + COST["look"]
                        i = max((i for i in avail[q] if ready[i] <= t0), key=lambda k: prio[k] - COST["idle"] * max(ready[k] - fr, 0.0))
                        best[q] = (max(fr, ready[i]), i)
                t1, i = min(best.values())
                q = qs[i]
                avail[q].remove(i)
                dirty = set([q])
                ends[i] = t1 + dur[i]
                if q != "n":
                    free[q] = ends[i]
                out.append(i)
                for j, gap in then[i]:
                    ready[j] = max(ready[j], ends[i] + gap)
                    left[j] -= 1
                    if not left[j]:
                        avail[qs[j]].append(j)
                        dirty.add(qs[j])
            return out, ends

        lat = [x["lat"] for x in nodes]
        prio = [0.0] * n
        for i in top:
            prio[i] = max([prio[j] + gap for j, gap in succ[i]] + [lat[i]]) + dur[i]
        best, seed, base = None, COST["seed"], prio
        PLAN["dag"] = (max(prio), prio, succ, nodes)
        prio = [prio[i] + nodes[i]["push"] for i in range(n)]
        for it in range(COST["tries"]):
            out, ends = run(prio, pred, succ, [0.0] * n)
            span = max(ends[i] + lat[i] for i in range(n))
            if best is None or span < best[0]:
                best, base, good = (span, out), ends, prio
            jit = []
            for i in range(n):
                seed = (seed * 1103515245 + 12345) % 2147483648
                jit.append(base[i] + lat[i] + COST["jit"] * (seed / 2147483648.0 - 0.5))
            prio = run([jit[i] - nodes[i]["push"] for i in range(n)], succ, pred, lat)[1]
            prio = [prio[i] + nodes[i]["push"] for i in range(n)]
        same = {}
        for x in nodes:
            same.setdefault((x["q"], tuple(x["wr"][:1])), []).append(x["i"])
        same = [x for x in same.values() if len(x) > 1]
        span, good = 1e9, list(dur)
        for it in range(COST["shifts"]):
            more = list(good)
            for step in range(1 + it % 2):
                seed = (seed * 1103515245 + 12345) % 2147483648
                for i in same[(seed >> 12) % len(same)]:
                    more[i] += COST["shift"] * ((seed >> 4) % 256 / 128.0 - 1.0)
            for i in top:
                prio[i] = max([prio[j] + gap for j, gap in succ[i]] + [lat[i]]) + more[i]
            out, ends = run(prio, pred, succ, [0.0] * n)
            new = max(ends[i] + lat[i] for i in range(n))
            seed = (seed * 1103515245 + 12345) % 2147483648
            if new <= span - COST["warm"] * (1 - it / COST["shifts"]) * math.log((seed + 1) / 2147483648.0):
                span, good = new, more
                if span < best[0]:
                    best = (span, out)
        PLAN["mid"] = best[0]
        seq = list(best[1])
        pos, before, behind, last = [0] * n, [-1] * n, [-1] * n, {}
        for k, i in enumerate(seq):
            pos[i] = k
            if qs[i] != "n":
                if qs[i] in last:
                    before[i], behind[last[qs[i]]] = last[qs[i]], i
                last[qs[i]] = i
        sinks = [i for i in range(n) if not succ[i]]

        def times(ends, k0):
            for i in seq[k0:]:
                t1 = ends[before[i]] if before[i] >= 0 else 0.0
                for j, gap in pred[i]:
                    if ends[j] + gap > t1:
                        t1 = ends[j] + gap
                ends[i] = t1 + dur[i]
            return max([ends[i] + lat[i] for i in sinks])

        def swap(u, v):
            a, b = pos[u], pos[v]
            old, late = seq[a:b + 1], set([u])
            for i in old[1:]:
                if (before[i] in late and i != v) or any(j in late for j, gap in pred[i]):
                    if i == v:
                        return None
                    late.add(i)
            seq[a:b + 1] = [i for i in old if i not in late] + [i for i in old if i in late]
            for k in range(a, b + 1):
                pos[seq[k]] = k
            p, s = before[u], behind[v]
            before[v], behind[v], before[u], behind[u] = p, u, v, s
            if p >= 0:
                behind[p] = v
            if s >= 0:
                before[s] = u
            return a

        ends = [0.0] * n
        span = times(ends, 0)
        best = (span, list(seq), ends)
        for it in range(COST["swaps"]):
            i, arcs = max(sinks, key=lambda k: ends[k] + lat[k]), []
            while i >= 0:
                start, j0 = ends[i] - dur[i] - 1e-9, -1
                for j, gap in pred[i]:
                    if ends[j] + gap > start:
                        j0 = j
                if j0 < 0 and before[i] >= 0 and ends[before[i]] > start:
                    j0 = before[i]
                    arcs.append((j0, i))
                i = j0
            if not arcs:
                break
            seed = (seed * 1103515245 + 12345) % 2147483648
            u, v = arcs[(seed >> 8) % len(arcs)]
            seed = (seed * 1103515245 + 12345) % 2147483648
            kind = (seed >> 16) % 10
            if kind < COST["drift"]:
                v = (seed >> 4) % n
            moved, a = [], n
            for step in range(1 + (seed >> 8) % COST["far"]):
                if kind % 2:
                    v = behind[u]
                else:
                    u = before[v]
                k = swap(u, v) if u >= 0 and v >= 0 else None
                if k is None:
                    break
                moved.append((u, v))
                a = min(a, k)
            if not moved:
                continue
            trial = list(ends)
            new = times(trial, a)
            seed = (seed * 1103515245 + 12345) % 2147483648
            if new <= span - COST["heat"] * (1 - it / COST["swaps"]) * math.log((seed + 1) / 2147483648.0):
                span, ends = new, trial
                if span < best[0]:
                    best = (span, list(seq), ends)
            else:
                for u, v in reversed(moved):
                    swap(v, u)
        PLAN["span"] = best[0]
        return best[1:]

    def emit():
        count = {}
        clock = dict((q, {}) for q in eng)
        event = {}
        where = {}

        def wait(q, need):
            for src in sorted(need):
                if not any(event[(o, need[o])].get(src, 0) >= need[src] for o in need if o != src):
                    eng[q].wait_ge(T.sem[qsem.get(src, src)], need[src])
            for src in need:
                for k, m in event[(src, need[src])].items():
                    clock[q][k] = max(clock[q].get(k, 0), m)

        if "seq" not in PLAN:
            PLAN["seq"], PLAN["ends"] = order()
        ends, mine = PLAN["ends"], dict((q, []) for q in eng)
        for i in PLAN["seq"]:
            x = nodes[i]
            q = x["q"]
            if q == "n":
                where[i] = (x["sem"], x["inc"])
                event[where[i]] = {x["sem"]: x["inc"]}
                continue
            need = {}
            for j, w in x["pred"].items():
                if w:
                    src, n = where[j]
                    if n > clock[q].get(src, 0):
                        need[src] = max(need.get(src, 0), n)
            if q in need:
                for j in reversed(mine[q]):
                    if ends[j] + COST["long"] <= ends[i] - x["dur"] or where[j][1] <= need[q]:
                        need[q] = max(need[q], where[j][1])
                        break
            wait(q, need)
            if x["sem"] is None:
                mine[q].append(i)
                for fn in x["fns"]:
                    fn(eng[q]).then_inc(T.sem[qsem[q]], 1)
                    count[q] = count.get(q, 0) + 1
                where[i] = (q, count[q])
            else:
                for fn in x["fns"]:
                    ins = fn(eng[q])
                    if x["sem"] != "sent":
                        ins.then_inc(T.sem[x["sem"]], 16)
                where[i] = (x["sem"], x["inc"])
            ev = dict(clock[q])
            ev[where[i][0]] = where[i][1]
            event[where[i]] = ev
        for x in nodes:
            if x["sem"] is not None and x["sem"] != "sent" and x["q"] != "n" and x["inc"] > clock["g"].get(x["sem"], 0):
                wait("g", {x["sem"]: x["inc"]})
        g.wait_ge(T.sem.sent, sum(x["inc"] for x in nodes if x["sem"] == "sent"))
        for q in ("v", "s", "p", "g"):
            if count[q] > clock["g"].get(q, 0):
                wait("g", {q: count[q]})
        return nodes
    return add, emit, hint, push, lambda: len(nodes) - 1


def rank_program(g, core, T, topo):
    rank = T.rank_of(core)
    if rank is None:
        return
    add, emit, hint, push, count = make_plan(g, T)
    C = CFG
    CYC, GATH = COST["cyc"], COST["gath"]

    def cols(x):
        if isinstance(x, str):
            x = (x, 0, T[x].shape[1])
        name, a, b = x[:3]
        if len(T[name].shape) == 3:
            return (T[name][x[4]:x[5], :, a:b] if x[3] == "all" else T[name][x[4]:x[5], x[3], a:b]), (name, a, b)
        if len(x) == 6:
            return (T[name][x[4]:x[5], a:b:x[3]] if x[3] > 1 else T[name][x[4]:x[5], a:b]), (name, a, b)
        if len(x) == 4:
            return T[name][:, a:b:x[3]], (name, a, b)
        return T[name][:, a:b], (name, a, b)

    def width(x):
        r = cols(x)[1]
        st = x[3] if len(x) >= 4 and not isinstance(x, str) else 1
        if st == "all":
            return 4 * (r[2] - r[1])
        return (r[2] - r[1] + st - 1) // st

    def buf(x):
        return x if isinstance(x, str) else x[0]

    def part(x, p0, p1):
        return (x[0], x[1], x[2], x[3] if len(x) > 3 else 1, p0, p1)

    def small(*xs):
        return all(SCRATCH[buf(x)][2] in (F16, BF, U2) for x in xs)

    def vec(ins, out, fn, cyc):
        add("v", [cols(x)[1] for x in ins], [cols(out)[1]], [fn], CYC * max(64, cyc))

    def ts(out, in0, s1, op0, s2=None, op1=None):
        o, i = cols(out)[0], cols(in0)[0]
        rd = [in0] + [x for x in (s1, s2) if isinstance(x, tuple)]
        s1 = cols(s1)[0] if isinstance(s1, tuple) else s1
        s2 = cols(s2)[0] if isinstance(s2, tuple) else s2
        if op1 is None:
            fn = lambda e: e.tensor_scalar(o, i, s1, None, op0)
        else:
            fn = lambda e: e.tensor_scalar(o, i, s1, s2, op0, op1)
        vec(rd, out, fn, width(out) * (0.5 if small(out, in0) else 1))

    def tt(out, in0, in1, op):
        o, a, b = cols(out)[0], cols(in0)[0], cols(in1)[0]
        ps = buf(in0) in PSUM or buf(in1) in PSUM
        vec([in0, in1], out, lambda e: e.tensor_tensor(o, a, b, op), width(out) * (1 if ps else 2))

    def scan(out, d0, d1):
        o, a, b = cols(out)[0], cols(d0)[0], cols(d1)[0]
        vec([d0, d1], out, lambda e: e.tensor_tensor_scan(o, a, b, -4e9, OP.max, OP.add), width(out))

    def cp(out, in0):
        o, a = cols(out)[0], cols(in0)[0]
        vec([in0], out, lambda e: e.tensor_copy(o, a), width(out) * (0.5 if small(out, in0) else 1))

    def gsub(out, win, off, in1):
        o, w, f, b = cols(out)[0], cols(win)[0], cols(off)[0], cols(in1)[0]
        vec([win, off, in1], out, lambda e: e.tensor_tensor(o, w.indirect(f), b, OP.subtract), 50 + GATH * width(out))

    def sca(win, off, in0):
        w, f, a = cols(win)[0], cols(off)[0], cols(in0)[0]
        vec([off, in0], win, lambda e: e.tensor_copy(w.indirect(f), a), 50 + COST["scat"] * width(in0))

    def fill(out, v):
        o = cols(out)[0]
        vec([], out, lambda e: e.memset(o, v), width(out) * (0.5 if small(out) else 1))

    def act(out, in0, func, off=None, **kw):
        o, a = cols(out)[0], cols(in0)[0]
        rd, wr, kk = [cols(in0)[1]], [cols(out)[1]], {}
        for k, v in kw.items():
            if isinstance(v, tuple):
                v, r = cols(v)
                (wr if k == "accum_out" else rd).append(r)
            kk[k] = v
        if off is not None:
            f, rf = cols(off)
            a = a.indirect(f)
            rd.append(rf)
        add("s", rd, wr, [lambda e: e.activation(o, a, func, **kk)], CYC * (COST["act"] + width(out) * (GATH if off is not None else 1)))

    def gat(q, out, win, off):
        if q == "s":
            act(out, win, AF.Copy, off=off)
        else:
            o, w, f = cols(out)[0], cols(win)[0], cols(off)[0]
            vec([win, off], out, lambda e: e.tensor_copy(o, w.indirect(f)), 50 + GATH * width(out))

    def lin(q, out, in0, mul=1.0, plus=0.0):
        if q == "s":
            if isinstance(plus, tuple) or plus:
                act(out, in0, AF.Identity, scale=mul, bias=plus)
            else:
                act(out, in0, AF.Copy, scale=mul)
        elif mul == 1.0 and plus == 0.0:
            cp(out, in0)
        else:
            ts(out, in0, mul, OP.mult, plus, OP.add)

    def pos(q, out, in0, plus):
        if q == "s":
            act(out, in0, AF.Relu, bias=plus)
        else:
            ts(out, in0, plus, OP.add, 0.0, OP.max)

    def one(x):
        o, a, b = cols(x[0])[0], cols(x[1])[0], cols(x[2])[0]
        return lambda e: e.matmul(o, a, b, x[3], x[4])

    def mms(all_):
        for j in range(0, len(all_), COST["chunk"]):
            xs = all_[j:j + COST["chunk"]]
            rd = sorted(set(cols(x[1])[1] for x in xs) | set(cols(x[2])[1] for x in xs))
            wr = sorted(set(cols(x[0])[1] for x in xs))
            add("p", rd, wr, [one(x) for x in xs], sum(max(64, width(x[0])) * COST["pe"] for x in xs))

    def msum(out, *pairs):
        mms([(out, a, b, j == 0, j == len(pairs) - 1) for j, (a, b) in enumerate(pairs)])

    def iota(out, pattern, base, cm, flag=True):
        o = cols(out)[0]
        if flag:
            fn = lambda e: e.iota(o, pattern, base, cm, allow_small_or_imprecise_dtypes=True)
        else:
            fn = lambda e: e.iota(o, pattern, base, cm)
        prev["g"] = add("g", [], [cols(out)[1]], [fn], 0.13 + 2 * CYC * width(out), after=prev.get("g"))

    def pick(out, pattern, op, v, base, cm):
        o, r = cols(out)
        prev["g"] = add("g", [r], [r], [lambda e: e.affine_select(o, o, pattern, op, v, base, cm)], 0.17 + 2 * CYC * width(out),
                        after=prev.get("g"))

    def dma(q, s, rd, wr, out, in_, us, turn=False):
        prev[q] = add(q, rd, wr, [lambda e: e.dma_start(out, in_)], 0.1, sem=s, inc=16, lat=us, after=prev.get(q) if turn else None)

    prev = {}

    SW, SD = ("S", 0, 2048), ("S", 0, 2176)
    DW, XW, xw = ("ZB", 0, 4096), ("ZB", 4096, 6144), ("ZB", 2048, 4096, 16)
    LOCAL = COST["local"]

    dma("s", "ds0", [], ["si"], T.si[:], T.s0[:], LOCAL)
    dma("y", "dS0", [], [SW], T.S[:, 0:2048], T.stm[:], COST["S"])
    dma("s", "dw", [], ["wi"], T.wi[:], T.wt[:], COST["S"] + 0.5, True)
    dma("y", "dX", [], [XW], T.ZB[:, 4096:6144], T.vx[:], COST["X"], True)
    dma("y", "dx0", [], ["xb"], T.xb[:], T.x0[:], COST["X"] + 0.5, True)

    iota("cp", [[1, 1]], 0, 1, False)
    iota("pf", [[0, 16]], 0, 1)
    iota("cI", [[1, 144]], 0, 0)
    iota("ex", [[1, 16]], 0, 0)
    iota("blk", [[16, 8], [0, 16]], 0, 0)
    iota("il0", [[16, 8]], 0, 0)
    iota("l256", [[1024, 2], [0, 2], [256, 4]], 0, 0)
    iota("TB", [[0, 128], [32, 16]], 256, 0)
    iota("LT", [[0, 128]], -2048, 0)
    pick("LT", [[1, 128]], OP.is_gt, 0.0, 0, -1)
    pick("LT", [[1, 128]], OP.not_equal, 4096.0, 0, -1)
    iota("TRI", [[0, 512]], 4096, 0)
    pick("TRI", [[0, 8], [-1, 64]], OP.is_ge, 0.0, -64, 1)
    P = ("pf", 0, 1)
    PX, PM, PG, PG16, KM, WC, WM, CTC, XOC = [("cf", j, j + 1) for j in range(9)]
    K0 = ("rm", 0, 1)
    ts(("cq", 0, 1), "cp", 15, OP.bitwise_and)
    ts(("cq", 1, 2), "cp", 112, OP.bitwise_and)
    ts(("cq", 3, 4), "cp", 1, OP.bitwise_and)
    cp(("cf", 1, 3), ("cq", 0, 2))
    ts(PX, ("cq", 3, 4), -2, OP.mult, 1, OP.add)
    tt(PX, PX, P, OP.add)
    ts("I16", ("cI", 0, 128), P, OP.is_equal)
    ts("P16", ("cI", 0, 128), PX, OP.is_equal)
    ts("rm", "ex", PM, OP.is_equal)
    for k in range(16):
        ts(("DA", 128 * k, 128 * k + 128), "I16", ("rm", k, k + 1), OP.mult)
        lin("s" if k < C["db"] else "v", ("DB", 128 * k, 128 * k + 128), "P16", ("rm", k ^ 1, (k ^ 1) + 1))
    for h in range(2):
        cp(("su", 4 * h, 4 * h + 4), ("si", 4 * h, 4 * h + 4))
    ts("BO", "blk", PG, OP.is_equal)
    for name, v in (("NI16", -1.0), ("NI32", -32.0), ("N512", -512.0), ("IB", 1.0), ("NIB", -1.0)):
        lin("s", name, "I16", v)
    for name, v in (("BF1", -3072.0), ("BFH", -0.5), ("BF2", -1024.0)):
        lin("s", name, "BO", v)
    fill("ONB", -32.0)
    fill(("K12", 0, 64), -1280.0)
    fill(("K12", 64, 68), 8188.0)
    ts(PG16, PG, 16.0, OP.add)
    lin("s", WC, "wi")
    lin("s", WM, "wi", -1.0)
    tt("MK", "LT", "BO", OP.mult)
    lin("s", KM, PM, 1.0, -2048.0)
    lin("s", CTC, PM, 16.0, 2048.0)
    lin("s", XOC, PM, 16.0)
    ts("L1", "cI", PG16, OP.is_equal)
    for name, v in (("WN", WM), ("WP", WC), ("LK", KM), ("L7", 2047.0)):
        lin("s", name, "L1", v)
    fill(("S", 2048, 2176), 0)
    ts("gm", "il0", PG, OP.is_equal)
    lin("s", "GI", "gm")
    for j in range(8):
        act(("SEL", 128 * j, 128 * j + 128), "I16", AF.Identity, scale=0.0, bias=("gm", j, j + 1))
    lin("s", "CT", "l256", 1.0, CTC)
    lin("s", "XO", ("l256", 4, 12), 1.0, XOC)
    lin("s", "SP", "XO", 1.0 / 16, 2048.0)
    fill("K4", 4096.0)
    fill("ZO", 0.0)
    fill("SC", 0.0)
    for j, v in ((2, -1023.5), (3, 1.5 * 2.0 ** 34), (4, -1.5 * 2.0 ** 34), (5, -4e9)):
        fill(("SC", j, 24, 6), v)
    for h in range(2):
        fill(("b%d" % (3 + h), 300, 324), -1e10)
    fill(("Z", 3072, 4096, 16), 1024.0)
    lin("s", xw, "xb")

    def slm(m):
        return 16 - m, 144 - m

    def listing(out, tab, rhs, *more):
        msum(out, *(list(more) + [((tab,) + slm(m), (rhs[0], rhs[1] + m, rhs[2], 16)) for m in range(16)]))

    def send(t, src, dst, sem):
        to = T.cores[(rank + 1 + t % (N - 1)) % N]
        rid, pid = topo.addr(to)[:2]
        mask = sum(1 << e for e in topo.engines(core, to)[:NENG])
        (a, ra), (b, rb) = cols(src), cols(dst)
        i = add("g", [ra], [], [lambda e: e.remote_dma(b, a, T.sem[sem], T.sem.sent, pid, rid, mask)], 0.3, sem="sent", inc=NENG)
        add("n", [], [rb], [], 0.0, sem=sem, inc=NENG, lat=COST["flight"], after=i)

    def sub(x, n, h):
        if isinstance(x, str):
            x = (x, 0)
        return (x[0], x[1] + n * h, x[1] + n * h + n)

    def hf(x, h):
        return sub(x, 64, h)

    def hl(x, h):
        return sub(x, 4, h)

    def ablist(st, en, o):
        a = 128 * (st // 64) + 64 * o + st % 64
        return ("ABT", a, a + en - st)

    XS, RP = ("b7", 0, 128), ("b7", 256, 384)
    FI, SE = (("FS", 0, 64), ("FS", 192, 256)), ("FS", 64, 192)
    U0, X1N, F1N = [(sub("GF", 64, j), sub("GF", 64, 5 - j)) for j in range(3)]
    LG = (("b2", 0, 12), ("b2", 16, 28))
    LU0, LX1, c1n = [(sub(LG[0], 4, j), sub(LG[1], 4, 2 - j)) for j in range(3)]

    for t in range(RO):
        last = t == RO - 1
        mN, rN, mX, rX = [sub(x, 128, t) for x in ("mN", "rN", "mX", "rX")]
        done = {}
        push[1] = t

        def named(name, fn, *args):
            if name in C["after"]:
                hint.append(done[C["after"][name]])
            fn(*args)
            done[name] = count()

        def columns(a, b):
            oo = ("b7" if b == 128 else "b3", 400 + a // 8, 400 + b // 8)
            if a == 0:
                listing(oo, "LK", ("FS", 2 * a, 2 * b), ("I16", ("CT", a // 8, b // 8)))
                lin(C["ou"], ("ou", a // 8, b // 8), oo)
            off = ("ou", 4 + a // 16, 4 + b // 16)
            if a == 64:
                gsub(("z2", a, b), "Z", off, ("xb", a, b))
                push[3] = "mX:%d" % a
                act((mX[0], mX[1] + a, mX[1] + b), ("z2", a, b), AF.Abs)
            else:
                act(("z2", a, b), DW, AF.Abs, off=off)
                xd = (oo[0], 136 + a, 136 + b) if b == 64 else (oo[0], 128 + a, 128 + b)
                msum(xd, ("BF2", (SE[0], SE[1] + a, SE[1] + b)), ("IB", ("xb", a, b)), ("NIB", ("z2", a, b)))
                push[3] = "mX:%d" % a
                act((mX[0], mX[1] + a, mX[1] + b), xd, AF.Abs, bias=1024.0)
            push[3] = None
            send(t, (mX[0], mX[1] + a, mX[1] + b), (rX[0], rX[1] + a, rX[1] + b), "aX%d%d" % (t, a // 64))

        for h in range(2):
            gat(C["cu"][h], hf("Cu", h), SW, hl("su", h))
            for j, (q, a, b) in enumerate(C["g"][h]):
                named("g%d%d" % (h, j), gat, q, ("G%d" % h, 16 * a, 16 * b), SW, ("Cu", 64 * h + a, 64 * h + b))
            if h and C["merge"][t] == 0:
                push[2] = "a"
                sca(SD, hl("sou", 0), hf("Sn", 0))
                push[2] = ""
            for a, b, qs in C["pick"][h]:
                for o, tab, bk in ((1, "DB", "b%d" % (5 + h)), (0, "DA", "b%d" % h)):
                    msum((bk, a, b), *[(sub(tab, 128, k), ("G%d" % h, 16 * a + k, 16 * b, 16)) for k in range(16)])
                    lin(qs[1 - o], ablist(64 * h + a, 64 * h + b, o), (bk, a, b))
            EN, EM = ("b%d" % (3 + h), 384, 448), ("b%d" % (3 + h), 448, 512)
            lin(C["c16"][h], hf("C16", h), hf("Cu", h))
            gat(C["sl"][h], hf("SL", h), "TB", hl("su", h))
            en = [("NI32", hf("C16", h)), ("IB", hf("SL", h))] + ([("ONB", "FCB")] if t else [])
            msum(EN, *en)
            lin(C["qe"][h], hf("qe", h), EN, 1.0 / 512, 1280.0 - 15.0 / 32)
            msum(EM, *(en + [("N512", ("K12", 0, 64)), ("N512", hf("qe", h))]))
            lin(C["n1"][h], hl("n1", h), hl("su", h), 5.0)
            push[0] = C["push"][2 * h]
            for j, (q, st, end) in enumerate(C["x"][h]):
                st, end = st + 64 * h, end + 64 * h
                xb_, d_, z_ = [(x, 16 * st, 16 * end) for x in ("XB", "ZB", "Z")]
                named("b%d%d" % (h, j), gat, q, xb_, XW, ablist(st, end, 1))
                named("d%d%d" % (h, j), gsub, d_, XW, ablist(st, end, 0), xb_)
                if C["size"][h][j] == "s":
                    named("z%d%d" % (h, j), act, z_, d_, AF.Abs)
                else:
                    named("z%d%d" % (h, j), ts, z_, d_, 0.0, OP.max, 2.0, OP.mult)
            A, V = "b%d" % h, "b%d" % (3 + h)
            push[0] = C["push"][2 * h + 1]
            U = (A, 128, 192)
            COL, SO = (A, 384, 392), (A, 400, 404)
            cl = hf("cl", h)
            off = [x for j, x in enumerate(C["x"][h]) if C["size"][h][j] == "v"]
            if off:
                a, b = off[0][1], off[-1][2]
                push[2] = "o"
                mms([(U, "ZO", ("IB", 0, 64), True, False)])
                push[2] = "d"
                mms([((A, 128 + a, 128 + b), ("WN",) + slm(k), ("ZB", 1024 * h + 16 * a + k, 1024 * h + 16 * b, 16), False, False)
                     for k in range(16)])
                push[2] = ""
            mms([(U, ("WP",) + slm(k), ("Z", 1024 * h + k, 1024 * h + 1024, 16), k == 0 and not off, k == 15) for k in range(16)])
            lin(C["q"][h], hf("ui", h), U)
            ts(hf("uk", h), hf("ui", h), 2047, OP.bitwise_and)
            act(hf("sq", h), hf("uk", h), AF.Square, bias=16.0)
            lin(C["v16"][h], hf("V16", h), hf("uk", h))
            lin(C["u0"][h], U0[h], hf("uk", h), K0)
            ts(hf("yy", h), hf("sq", h), 480, OP.bitwise_and)
            named("cl%d" % h, tt, cl, hf("yy", h), (V, 448, 512), OP.is_equal)
            R, RU, Q = (A, 192, 256), (V, 64, 128), (V, 0, 64)
            push[2] = "c"
            mms([(R, "NI16", hf("C16", h), True, False)])
            push[2] = ""
            mms([(R, "MK", cl, False, True)])
            msum(RU, ("NI16", hf("V16", h)), ("MK", cl))
            msum(Q, ("MK", cl))
            pos("v", F1N[h], R, -2048.0)
            push[3] = "mN:%d" % (64 * h)
            ts(hf(mN, h), R, 0.0, OP.max, 2048.0, OP.min)
            push[3] = None
            send(t, hf(mN, h), hf(rN, h), "aN%d%d" % (t, h))
            pos(C["x1n"][h], X1N[h], RU, -2048.0)
            pos(C["fi"][h], FI[h], Q, -4095.0)
            lanes = last and h
            if lanes:
                ts(("GF", 384, 448), Q, 2048.0, OP.is_equal, KM, OP.mult)
                ts(("GF", 448, 512), Q, 4096.0, OP.is_equal, KM, OP.mult)
            else:
                ts(hf(SE, h), Q, 2048.0, OP.is_equal)
            nj = 64 * (h + 1)
            low = (lambda x: x) if h else (lambda x: part(x, 0, 64))
            banks = ((("b6", 0, 256), 0, 4), (("b5", 256, 512), 4, 8)) if h else ((("b5", 0, 512), 0, 8),)
            msum(low(COL), (("GF", 128, 128 + nj), "GI"))
            for rows, j0, j1 in banks:
                n = 64 * (j1 - j0)
                tri = [("IB", 0, 128), ("TRI", 0, n)] if h else [("IB", 64, 128, 1, 64, 128), ("TRI", 0, n, 1, 64, 128)]
                push[2] = "t"
                mms([(low(rows), tri[0], tri[1], True, False)])
                push[2] = "r%d" % h
                mms([(low(sub(rows, 64, j - j0)), ("SEL", 128 * j, 128 * j + nj), F1N[h], False, j == j1 - 1) for j in range(j0, j1)])
                push[2] = ""
            if lanes:
                listing(("b7", 416, 436), "L1", ("GF", 192, 512))
                tt(("ou", 8, 16), ("b7", 428, 436), ("CT", 8, 16), OP.add)
                c1n, LX1, LU0 = [(None, ("b7", 416 + 4 * j, 420 + 4 * j)) for j in range(3)]
            else:
                listing(LG[h], "L1", sub("GF", 192, h))
            for rows, j0, j1 in banks:
                for j in range(j0, j1):
                    ts(("EQ%d" % h, 16 * j, 16 * j + 16, "all", 0, nj), low(sub(rows, 64, j - j0)), low(sub(COL, 1, j)), OP.is_equal)
            lin(C["c1u"][h], hl("c1u", h), c1n[h], -1.0, 2048.0)
            lin(C["c1h"][h], hl("c1h", h), c1n[h], -1.0, 2048.0)
            tt(hl("n2", h), hl("n1", h), LU0[h], OP.add)
            ts(hl("h1", h), c1n[h], 0.0, OP.is_gt, 2.0 ** 22 + 2048, OP.mult)
            tt(hl("h2", h), hl("h1", h), c1n[h], OP.subtract)
            ts(hl("n3", h), hl("n2", h), 2047, OP.bitwise_and)
            lin(C["x1"][h], hl("x1", h), LX1[h], -1.0, 2048.0)
            mms([(SO, "I16", hl("c1h", h), True, False)] +
                [(sub(SO, 1, j), ("EQ%d" % h, 0, 128, j, 0, nj), low(("K4", 0, 1)), False, j == 3) for j in range(4)])
            gsub(hf("Sd", h), SD, hl("c1u", h), X1N[h])
            ts(hf("Sn", h), hf("Sd", h), 2047, OP.bitwise_and)
            tt(hl("sou", h), SO, hl("SP", h), OP.min)
            push[0] = 0.0
        if last:
            columns(0, 64)
        if C["merge"][t] == 1:
            sca(SD, "sou", "Sn")
        else:
            if C["merge"][t] == 2:
                push[2] = "a"
                sca(SD, hl("sou", 0), hf("Sn", 0))
                push[2] = ""
            sca(SD, hl("sou", 1), hf("Sn", 1))
        if not last:
            act("sg", SE, AF.Copy, accum_out=("fc", 0, 1))
            act("FCB", ("IB", 0, 64), AF.Identity, scale=0.0, bias=("fc", 0, 1))
        for h in range(2):
            V = "b%d" % (3 + h)
            RL = (V, 301, 324, 6)
            push[3] = "sb:%d" % (4 * h)
            tt((V, 300, 324, 6), hl("h2", h), hl("n3", h), OP.max)
            push[3] = None
            push[2] = "k"
            mms([(RL, "N512", ("K12", 64, 68), True, False)])
            push[2] = ""
            a = hf(rN, h)
            mms([(RL, ("L7",) + slm(m), (a[0], a[1] + m, a[2], 16), False, m == 15) for m in range(16)])
            se = sub("se", 24, h)
            scan(se, (V, 300, 324), "SC")
            tt(hl("sf" if last else "su", h), (se[0], se[1] + 1, se[2], 6), (se[0], se[1] + 4, se[2], 6), OP.subtract)
        if last:
            dma("y", "oS", ["sf"], [], T.ys[:], T.sf[:], LOCAL)
        columns(64 if last else 0, 128)
        for h in range(2):
            act(hf("z1", h), DW, AF.Abs, off=hl("ou", 3 * h))
            msum(hf(XS, h), ("BF1", FI[h]), ("BFH", FI[h]), ("IB", hf("xb", h)), ("IB", hf("z1", h)))
        lin("s", "hv", XS, 0.5, 256.0)
        if not last:
            ts("x2", "x1", 2048 + 15, OP.bitwise_and)
            tt("xou", "x2", "XO", OP.add)
            sca(("ZB", 4096, 8192), "xou", "z1")
        else:
            for h in range(2):
                ts(hl("x2", h), hl("x1", h), 2048 + 15, OP.bitwise_and)
                tt(hl("xou", h), hl("x2", h), hl("XO", 0), OP.add)
                a = 4096 + 1024 * h
                sca(("ZB", a, 8192), hl("xou", h), hf("z1", h))
                dma("y", "oV%d" % h, [("ZB", a, a + 1024)], [], T.yv[:, 1024 * h:1024 * h + 1024], T.ZB[:, a:a + 1024], 1.4 * LOCAL)
            turn = []
            for q, a, b in C["yt"]:
                lin(q, ("SH", 256 * a, 256 * b), ("S", 256 * a, 256 * b))
                turn += range(a, b)
            for j, q in enumerate(turn):
                mms([(("b5", 256, 512), "I16", sub("SH", 256, q), j == 0, j == 7)])
            lin(C["yo"], "yto", ("b5", 256, 512))
            dma("s", "oT", ["yto"], [], T.yt[:], T.yto[:], LOCAL)
        if last:
            for h in range(2):
                tt(hf("xm", h), hf("hv", h), hf(rX, h), OP.min)
                ts(hf("xn", h), hf("xm", h), 255, OP.bitwise_and)
                lin(C["xb"][h], hf("xb", h), hf("xn", h))
        else:
            msum(RP, ("IB", rX))
            tt("xm", "hv", RP, OP.min)
            ts("xn", "xm", 255, OP.bitwise_and)
            lin("s", "xb", "xn")
            lin("s", xw, "xn")
    dma("y", "oX", ["xb"], [], T.yx[:], T.xb[:], LOCAL)
    return emit()
